import numpy as np
import ml_dtypes


def mxq(x, axis, fmt="e4m3"):
    dtype, down = {"e4m3": (ml_dtypes.float8_e4m3fn, 7), "e5m2": (ml_dtypes.float8_e5m2, 14)}[fmt]
    v = np.moveaxis(np.asarray(x, np.float32).astype(ml_dtypes.bfloat16).astype(np.float64), axis, -1)
    blocks = v.reshape(v.shape[:-1] + (-1, 32))
    amax = np.abs(blocks).max(-1, keepdims=True)
    byte = np.maximum(np.where(amax > 0, np.frexp(amax)[1] - 1 + 127, 0) - down, 1)
    scale = np.exp2(byte - 127.0)
    codes = (blocks / scale).astype(np.float32).astype(dtype).astype(np.float64)
    return np.moveaxis((codes * scale).reshape(v.shape), -1, axis)


WIDE = False


def mx_kscale(k):
    if not WIDE:
        return np.ones(k)
    levels = np.array([18, -18])
    if k % 512:
        return np.exp2(np.random.permutation(np.resize(levels, k // 32))).repeat(32)
    a = np.empty((k // 512, 16))
    for p in range(k // 512):
        a[p, :8] = np.random.permutation(np.resize(levels, 8))
        for g in range(8):
            far = levels[np.abs(levels - a[p, g]) >= 10]
            a[p, g + 8] = far[np.random.randint(len(far))]
    return np.exp2(a.ravel()).repeat(32)


def f64(x):
    return np.asarray(x).astype(np.float64)


def striped(idx):
    return np.tile(np.asarray(idx).reshape(-1, 16).T, (8, 1)).astype(np.uint16)


def unstriped(offs):
    return offs[:16].T.reshape(-1).astype(np.int64)


E2M1 = np.array([0.0, 0.5, 1.0, 1.5, 2.0, 3.0, 4.0, 6.0, -0.0, -0.5, -1.0, -1.5, -2.0, -3.0, -4.0, -6.0])


def pack_weight(w, fmt):
    k, n = w.shape
    w = f64(np.asarray(w, np.float32).astype(ml_dtypes.bfloat16)).reshape(k // 32, 32, n)
    amax = np.abs(w).max(1)
    if fmt == "e4m3":
        byte = np.frexp(amax)[1] - 1 + 127 - 7
    else:
        mant, ex = np.frexp(amax / 6.0)
        byte = np.where(mant > 0.5, ex, ex - 1) + 127
    byte = np.clip(np.where(amax > 0, byte, 1), 1, 254)
    scaled = (w * np.exp2(127.0 - byte)[:, None, :]).reshape(k, n).astype(np.float32)
    by_word = np.ascontiguousarray(scaled.reshape(k // 512, 128, 4, n).transpose(0, 1, 3, 2))
    if fmt == "e4m3":
        words = by_word.astype(ml_dtypes.float8_e4m3fn).view(np.uint8)
    else:
        c = by_word.astype(ml_dtypes.float4_e2m1fn).view(np.uint8) & 0xF
        words = (c[..., 0::2] | (c[..., 1::2] << 4)).reshape(k // 512, 128, 2 * n)
    return np.ascontiguousarray(words), np.ascontiguousarray(byte.astype(np.uint8).reshape(k // 512, 16, n))


def unpack_weight(words, scales, fmt):
    g, _, n = scales.shape
    words = np.ascontiguousarray(words).reshape(g, 128, n, -1)
    if fmt == "e4m3":
        vals = words.view(ml_dtypes.float8_e4m3fn).astype(np.float64)
    else:
        nib = np.empty((g, 128, n, 4), np.uint8)
        nib[..., 0::2] = words & 0xF
        nib[..., 1::2] = words >> 4
        vals = E2M1[nib]
    vals = vals * np.repeat(np.exp2(scales.astype(np.float64) - 127.0), 8, axis=1)[..., None]
    return vals.transpose(0, 1, 3, 2).reshape(g * 512, n)


def sig(x):
    return 1.0 / (1.0 + np.exp(-x))


def setup_inputs():
    n = np.random.standard_normal
    uni = np.random.uniform
    idx = np.random.permutation(2048)[:512]
    f_d = mx_kscale(512)
    f_e = mx_kscale(512)
    f_r = mx_kscale(1024)
    w1_ = pack_weight(n((512, 2048)) / np.sqrt(512) / f_d[:, None], "e4m3")
    w2_ = pack_weight(n((512, 2048)) / np.sqrt(512) / f_e[:, None], "e4m3")
    return {
        "xT": (n((512, 1024)) * f_d[:, None] * f_r[None, :]).astype(np.float32),
        "w1_words": w1_[0],
        "w1_scales": w1_[1],
        "dyT": (n((512, 1024)) * f_e[:, None]).astype(np.float32),
        "w2_words": w2_[0],
        "w2_scales": w2_[1],
        "us": (uni(0.75, 1.3, (1024, 1)) / f_r[:, None]).astype(np.float32),
        "ts": np.tile(uni(0.75, 1.3, 2048), (128, 1)).astype(np.float32),
        "wt": (uni(0.75, 1.3, (1024, 1)) / np.sqrt(1024)).astype(np.float32),
        "offs": striped(idx),
    }


def reference(xT, w1_words, w1_scales, dyT, w2_words, w2_scales, us, ts, wt, offs):
    idx = unstriped(offs)
    w1 = unpack_weight(w1_words, w1_scales, "e4m3")
    w1_i = w1[:, idx]
    w2 = unpack_weight(w2_words, w2_scales, "e4m3")
    w2_i = w2[:, idx]
    ts_i = f64(ts)[:1][:, idx]
    a = mxq(f64(xT), 0, "e4m3").T @ w1_i
    z = f64(us) * ts_i * a
    dh = mxq(f64(dyT), 0, "e5m2").T @ w2_i
    da = f64(wt) * f64(us) * ts_i * dh * sig(z) * (1.0 + z * (1.0 - sig(z)))
    dw1 = mxq(f64(xT), 1, "e4m3") @ mxq(da, 0, "e5m2")
    out = np.zeros((512, 2048))
    out[:, idx] = dw1
    return out

@@ -1,0 +1,215 @@
+from contextlib import ExitStack
+
+import concourse.mybir as mybir
+from concourse.masks import make_identity
+
+F32 = mybir.dt.float32
+BF16 = mybir.dt.bfloat16
+I32 = mybir.dt.int32
+U32 = mybir.dt.uint32
+U16 = mybir.dt.uint16
+U8 = mybir.dt.uint8
+E4M3 = mybir.dt.float8_e4m3fn_x4
+E5M2 = mybir.dt.float8_e5m2_x4
+ACT = mybir.ActivationFunctionType
+ALU = mybir.AluOpType
+
+P = 128
+PACK = 4
+K_PASS = P * PACK
+D, E, R, SLOTS, UNITS = 512, 512, 1024, 512, 2048
+HALVES = R // K_PASS
+FLOPS = 2 * R * SLOTS * (D + E + D)
+
+
+def tile_attend_gffn_sil_kernel(
+    tc, xT, w1_words, w1_scales, dyT, w2_words, w2_scales, us, ts, wt, offs, out
+):
+    nc = tc.nc
+    with ExitStack() as ctx:
+        lists = ctx.enter_context(tc.tile_pool(name="lists", bufs=1))
+        keep = ctx.enter_context(tc.tile_pool(name="keep", bufs=1))
+        work = ctx.enter_context(tc.tile_pool(name="work", bufs=4))
+        psum = ctx.enter_context(tc.psum_pool(name="psum", bufs=2))
+
+        offsets = lists.tile([P, SLOTS // 16], U16, name="offsets")
+        nc.sync.dma_start(offsets[:], offs)
+
+        ident = keep.tile([P, P], F32, name="ident")
+        make_identity(nc, ident[:])
+
+        x_rows = xT.rearrange("(p j) r -> p j r", j=PACK)
+        dy_rows = dyT.rearrange("(p j) r -> p j r", j=PACK)
+
+        def load_half(rows, h, tag):
+            raw = keep.tile([P, PACK, K_PASS], F32, name=tag, tag=tag)
+            nc.sync.dma_start(raw[:], rows[:, :, h * K_PASS : (h + 1) * K_PASS])
+            return raw
+
+        def load_words(words, name):
+            table = keep.tile([P, UNITS], I32, name=name)
+            nc.sync.dma_start(table[:], words[0].rearrange("p n t -> p (n t)").bitcast(I32))
+            return table
+
+        def load_scales(scales, name, queue):
+            table = keep.tile([P, UNITS], U8, name=name)
+            nc.vector.memset(table[:].bitcast(I32), 0)
+            for q in range(4):
+                queue.dma_start(
+                    table[32 * q : 32 * q + 4, :].bitcast(I32),
+                    scales[0, 4 * q : 4 * q + 4, :].bitcast(I32),
+                )
+            return table
+
+        x_raw = [load_half(x_rows, 0, "x_raw")]
+        s1_table = load_scales(w1_scales, "s1_table", nc.sync)
+        ts_table = keep.tile([P, UNITS], F32, name="ts_table")
+        nc.vector.memset(ts_table[:], 0.0)
+        nc.sync.dma_start(ts_table[0:1, :], ts[0:1, :])
+        w1_table = load_words(w1_words, "w1_table")
+        us_col = keep.tile([P, HALVES, PACK], F32, name="us_col")
+        nc.gpsimd.dma_start(us_col[:], us.rearrange("(h p t) o -> p h (t o)", h=HALVES, t=PACK))
+        wt_col = keep.tile([P, HALVES, PACK], F32, name="wt_col")
+        nc.gpsimd.dma_start(wt_col[:], wt.rearrange("(h p t) o -> p h (t o)", h=HALVES, t=PACK))
+        s2_table = load_scales(w2_scales, "s2_table", nc.gpsimd)
+        dy_raw = [load_half(dy_rows, 0, "dy_raw")]
+        w2_table = load_words(w2_words, "w2_table")
+        window0 = keep.tile([P, UNITS], F32, name="window0")
+        nc.vector.memset(window0[:], 0.0)
+
+        def gather(table, dtype, name):
+            picked = keep.tile([P, SLOTS], dtype, name=name, align_bytes=64)
+            nc.vector.tensor_copy(picked[:], table.indirect(offsets[:]))
+            return picked
+
+        ts_row = gather(ts_table[:], F32, "ts_row")
+        turned = psum.tile([P, PACK, P], F32, name="turned", tag="turn")
+        for b in range(4):
+            nc.tensor.transpose(turned[:, b, :], ts_row[:, b * P : (b + 1) * P], ident[:])
+        ts_col = keep.tile([P, 4], F32, name="ts_col")
+        nc.scalar.copy(ts_col[:], turned[:, :, 0])
+        spread = psum.tile([P, PACK, P], F32, name="spread", tag="turn")
+        for b in range(4):
+            nc.tensor.transpose(spread[:, b, :], ts_col[:, b : b + 1].to_broadcast([P, P]), ident[:])
+        ts_all = keep.tile([P, SLOTS], F32, name="ts_all")
+        nc.scalar.copy(ts_all[:], spread[:].rearrange("p b n -> p (b n)"))
+
+        s1 = gather(s1_table[:], U8, "s1")
+
+        def interleave(engine_copy, raw, name):
+            grouped = keep.tile([P, PACK * K_PASS], BF16, name=name, align_bytes=64)
+            engine_copy(
+                grouped[:].rearrange("p (t s j) -> p s j t", t=PACK, j=PACK),
+                raw[:].rearrange("p j (s t) -> p s j t", t=PACK),
+            )
+            return grouped
+
+        def quantize(grouped, fmt, name):
+            codes = keep.tile([P, K_PASS], U32, name=name + "_codes", align_bytes=64)
+            scales = keep.tile([P, K_PASS], U8, name=name + "_scales", align_bytes=64)
+            nc.vector.quantize_mx(out=codes[:].bitcast(fmt), scales=scales[:], in_=grouped[:])
+            return codes, scales
+
+        def product(bank, lhs, fmt_l, cols, rhs, fmt_r, start=True, stop=True):
+            nc.tensor.matmul_mx(
+                out=bank[:],
+                lhsT=lhs[0][:, cols].bitcast(fmt_l),
+                lhsT_scale=lhs[1][:, cols],
+                rhs=rhs[0][:].bitcast(fmt_r),
+                rhs_scale=rhs[1][:],
+                start=start,
+                stop=stop,
+            )
+
+        def turn_x(grouped, h):
+            words = grouped[:].bitcast(F32)
+            by_row = keep.tile([P, PACK * K_PASS], BF16, name=f"x_by_row{h}", align_bytes=64)
+            for u in range(2):
+                bank = psum.tile([P, PACK, P], F32, name="x_turned", tag="turn")
+                for t in range(PACK):
+                    nc.tensor.transpose(bank[:, t, :], words[:, 256 * t + u : 256 * (t + 1) : 2], ident[:])
+                nc.scalar.copy(
+                    by_row[:, 1024 * u : 1024 * (u + 1)].rearrange("s (e p t) -> s e p t", e=2, t=PACK),
+                    bank[:].rearrange("s t p -> s (t p)").bitcast(BF16).rearrange("s (t p e) -> s e p t", t=PACK, e=2),
+                )
+            return by_row
+
+        def first_product(xq, w1, h):
+            th, sl = [], []
+            for t in range(PACK):
+                a = psum.tile([P, SLOTS], F32, name="a", tag="a")
+                product(a, xq, E4M3, slice(t * P, (t + 1) * P), w1, E4M3)
+                z = work.tile([P, SLOTS], F32, name="z")
+                nc.vector.scalar_tensor_tensor(z[:], a[:], us_col[:, h, t : t + 1], ts_all[:], ALU.mult, ALU.mult)
+                sl.append(work.tile([P, SLOTS], F32, name="silu_neg"))
+                nc.scalar.activation(sl[t][:], z[:], ACT.Silu, scale=-1.0)
+                th.append(work.tile([P, SLOTS], F32, name="tanh_half"))
+                nc.scalar.activation(th[t][:], z[:], ACT.Tanh, scale=0.5)
+            return th, sl
+
+        def gradient(dyq, w2, th, sl, wu, h):
+            da = keep.tile([P, PACK, SLOTS], BF16, name=f"da{h}")
+            for t in range(PACK):
+                dh = psum.tile([P, SLOTS], F32, name="dh", tag="dh")
+                product(dh, dyq, E5M2, slice(t * P, (t + 1) * P), w2, E4M3)
+                y = work.tile([P, SLOTS], F32, name="y")
+                nc.vector.scalar_tensor_tensor(y[:], dh[:], wu[:, h, t : t + 1], ts_all[:], ALU.mult, ALU.mult)
+                q = work.tile([P, SLOTS], F32, name="q")
+                nc.vector.scalar_tensor_tensor(q[:], th[t][:], 1.0, y[:], ALU.add, ALU.mult)
+                nc.vector.scalar_tensor_tensor(da[:, t, :], sl[t][:], 1.0, q[:], ALU.subtract, ALU.mult)
+            return da
+
+        def interleave_da(shares, da):
+            grouped = keep.tile([P, PACK * SLOTS], BF16, name="da_grouped", tag="da_grouped", align_bytes=64)
+            for engine_copy, lo, hi in shares:
+                engine_copy(
+                    grouped[:, PACK * lo : PACK * hi].rearrange("p (c i t) -> p c t i", i=4, t=PACK),
+                    da[:, :, lo:hi].rearrange("p t (c i) -> p c t i", i=4),
+                )
+            return grouped
+
+        xg0 = interleave(nc.scalar.copy, x_raw[0], "x_grouped0")
+        x_raw.append(load_half(x_rows, 1, "x_raw"))
+        xq0 = quantize(xg0, E4M3, "x0")
+        w1 = (gather(w1_table[:].bitcast(U32), U32, "w1"), s1)
+        wu = keep.tile([P, HALVES, PACK], F32, name="wu")
+        nc.vector.scalar_tensor_tensor(wu[:], us_col[:], -0.5, wt_col[:], ALU.mult, ALU.mult)
+        xr0 = turn_x(xg0, 0)
+        dyg0 = interleave(nc.scalar.copy, dy_raw[0], "dy_grouped0")
+        dy_raw.append(load_half(dy_rows, 1, "dy_raw"))
+        th0, sl0 = first_product(xq0, w1, 0)
+        s2 = gather(s2_table[:], U8, "s2")
+        xrq = [quantize(xr0, E4M3, "xr0")]
+        dyq0 = quantize(dyg0, E5M2, "dy0")
+        w2 = (gather(w2_table[:].bitcast(U32), U32, "w2"), s2)
+        xg1 = interleave(nc.scalar.copy, x_raw[1], "x_grouped1")
+        dyg1 = interleave(nc.scalar.copy, dy_raw[1], "dy_grouped1")
+        da0 = gradient(dyq0, w2, th0, sl0, wu, 0)
+        xq1 = quantize(xg1, E4M3, "x1")
+        th1, sl1 = first_product(xq1, w1, 1)
+        dyq1 = quantize(dyg1, E5M2, "dy1")
+        xr1 = turn_x(xg1, 1)
+        dag0 = interleave_da([(nc.scalar.copy, 0, SLOTS)], da0)
+        da1 = gradient(dyq1, w2, th1, sl1, wu, 1)
+        xrq.append(quantize(xr1, E4M3, "xr1"))
+        daq = [quantize(dag0, E5M2, "da0")]
+        dag1 = interleave_da([(nc.vector.tensor_copy, 0, 320), (nc.scalar.copy, 320, SLOTS)], da1)
+        daq.append(quantize(dag1, E5M2, "da1"))
+
+        window1 = keep.tile([P, UNITS], F32, name="window1", tag="da_grouped", align_bytes=64)
+        nc.gpsimd.memset(window1[:], 0.0)
+        windows = [window0, window1]
+        out_rows = out.rearrange("(p j) n -> p j n", j=PACK)
+        for j in range(PACK):
+            dw = psum.tile([P, SLOTS], F32, name="dw", tag="dw")
+            for h in range(HALVES):
+                product(dw, xrq[h], E4M3, slice(j * P, (j + 1) * P), daq[h], E5M2, h == 0, h == HALVES - 1)
+            dw_sb = keep.tile([P, SLOTS], F32, name=f"dw_sb{j}", tag=f"dw_sb{j}")
+            nc.scalar.copy(dw_sb[:], dw[:])
+            window = windows[j % 3]
+            nc.vector.tensor_copy(window[:].indirect(offsets[:]), dw_sb[:])
+            nc.sync.dma_start(out_rows[:, j, :], window[:])
+            if j == 0:
+                window2 = keep.tile([P, UNITS], F32, name="window2", tag="dw_sb0")
+                nc.gpsimd.memset(window2[:], 0.0)
+                windows.append(window2)

@@ -19,6 +19,7 @@ PACK = 4
 K_PASS = P * PACK
 D, E, R, SLOTS, UNITS = 512, 512, 1024, 512, 2048
 HALVES = R // K_PASS
+XS = 88
 FLOPS = 2 * R * SLOTS * (D + E + D)
 
 
@@ -30,83 +31,96 @@ def tile_attend_gffn_sil_kernel(
         lists = ctx.enter_context(tc.tile_pool(name="lists", bufs=1))
         keep = ctx.enter_context(tc.tile_pool(name="keep", bufs=1))
         work = ctx.enter_context(tc.tile_pool(name="work", bufs=4))
-        psum = ctx.enter_context(tc.psum_pool(name="psum", bufs=2))
+        psum = ctx.enter_context(tc.psum_pool(name="psum", bufs=1))
 
         offsets = lists.tile([P, SLOTS // 16], U16, name="offsets")
         nc.sync.dma_start(offsets[:], offs)
 
-        ident = keep.tile([P, P], F32, name="ident")
-        make_identity(nc, ident[:])
-
         x_rows = xT.rearrange("(p j) r -> p j r", j=PACK)
         dy_rows = dyT.rearrange("(p j) r -> p j r", j=PACK)
 
-        def load_half(rows, h, tag):
-            raw = keep.tile([P, PACK, K_PASS], F32, name=tag, tag=tag)
+        def load_half(rows, h, name):
+            raw = keep.tile([P, PACK, K_PASS], F32, name=name, align_bytes=64)
             nc.sync.dma_start(raw[:], rows[:, :, h * K_PASS : (h + 1) * K_PASS])
             return raw
 
         def load_words(words, name):
-            table = keep.tile([P, UNITS], I32, name=name)
+            table = keep.tile([P, UNITS], I32, name=name, align_bytes=64)
             nc.sync.dma_start(table[:], words[0].rearrange("p n t -> p (n t)").bitcast(I32))
             return table
 
-        def load_scales(scales, name, queue):
-            table = keep.tile([P, UNITS], U8, name=name)
-            nc.vector.memset(table[:].bitcast(I32), 0)
-            for q in range(4):
-                queue.dma_start(
-                    table[32 * q : 32 * q + 4, :].bitcast(I32),
-                    scales[0, 4 * q : 4 * q + 4, :].bitcast(I32),
-                )
+        def cleared_plane(name, tag, engine):
+            table = keep.tile([P, UNITS // 4], I32, name=name, tag=tag, align_bytes=64)
+            engine.memset(table[:], 0)
             return table
 
-        x_raw = [load_half(x_rows, 0, "x_raw")]
-        s1_table = load_scales(w1_scales, "s1_table", nc.sync)
+        def load_scales(table, scales, queue):
+            for q in range(4):
+                queue.dma_start(
+                    table[32 * q : 32 * q + 4, :],
+                    scales[0, 4 * q : 4 * q + 4, :].bitcast(I32),
+                )
+
+        def bank(n, name):
+            return psum.tile([P, SLOTS], F32, name=name, tag=f"bank{n}")
+
+        x_raw = [load_half(x_rows, 0, "x_raw0")]
         ts_table = keep.tile([P, UNITS], F32, name="ts_table")
-        nc.vector.memset(ts_table[:], 0.0)
-        nc.sync.dma_start(ts_table[0:1, :], ts[0:1, :])
-        w1_table = load_words(w1_words, "w1_table")
+        nc.scalar.dma_start(ts_table[96:P, :], ts[96:P, :])
+        nc.vector.memset(ts_table[0:96, :], 0.0)
+        s1_table = cleared_plane("s1_table", "x_grouped0b", nc.gpsimd)
+        load_scales(s1_table, w1_scales, nc.scalar)
+        warm = keep.tile([P, 2], F32, name="warm")
+        nc.vector.memset(warm[:, 0:1], 0.0)
+        nc.scalar.activation(warm[:, 1:2], warm[:, 0:1], ACT.Silu)
         us_col = keep.tile([P, HALVES, PACK], F32, name="us_col")
-        nc.gpsimd.dma_start(us_col[:], us.rearrange("(h p t) o -> p h (t o)", h=HALVES, t=PACK))
+        nc.scalar.dma_start(us_col[:], us.rearrange("(h p t) o -> p h (t o)", h=HALVES, t=PACK))
         wt_col = keep.tile([P, HALVES, PACK], F32, name="wt_col")
-        nc.gpsimd.dma_start(wt_col[:], wt.rearrange("(h p t) o -> p h (t o)", h=HALVES, t=PACK))
-        s2_table = load_scales(w2_scales, "s2_table", nc.gpsimd)
-        dy_raw = [load_half(dy_rows, 0, "dy_raw")]
+        nc.scalar.dma_start(wt_col[:], wt.rearrange("(h p t) o -> p h (t o)", h=HALVES, t=PACK))
+        w1_table = load_words(w1_words, "w1_table")
+        dy_raw = [load_half(dy_rows, 0, "dy_raw0")]
         w2_table = load_words(w2_words, "w2_table")
+        x_raw.append(load_half(x_rows, 1, "x_raw1"))
+        dy_raw.append(load_half(dy_rows, 1, "dy_raw1"))
+        ident = keep.tile([P, P], F32, name="ident")
+        make_identity(nc, ident[:])
         window0 = keep.tile([P, UNITS], F32, name="window0")
         nc.vector.memset(window0[:], 0.0)
+        s2_table = cleared_plane("s2_table", "s2_table", nc.gpsimd)
+        load_scales(s2_table, w2_scales, nc.gpsimd)
 
-        def gather(table, dtype, name):
-            picked = keep.tile([P, SLOTS], dtype, name=name, align_bytes=64)
+        def gather(table, dtype, name, tag=None):
+            picked = keep.tile([P, SLOTS], dtype, name=name, tag=tag or name, align_bytes=64)
             nc.vector.tensor_copy(picked[:], table.indirect(offsets[:]))
             return picked
 
-        ts_row = gather(ts_table[:], F32, "ts_row")
-        turned = psum.tile([P, PACK, P], F32, name="turned", tag="turn")
-        for b in range(4):
-            nc.tensor.transpose(turned[:, b, :], ts_row[:, b * P : (b + 1) * P], ident[:])
-        ts_col = keep.tile([P, 4], F32, name="ts_col")
-        nc.scalar.copy(ts_col[:], turned[:, :, 0])
-        spread = psum.tile([P, PACK, P], F32, name="spread", tag="turn")
-        for b in range(4):
-            nc.tensor.transpose(spread[:, b, :], ts_col[:, b : b + 1].to_broadcast([P, P]), ident[:])
-        ts_all = keep.tile([P, SLOTS], F32, name="ts_all")
-        nc.scalar.copy(ts_all[:], spread[:].rearrange("p b n -> p (b n)"))
-
-        s1 = gather(s1_table[:], U8, "s1")
-
-        def interleave(engine_copy, raw, name):
-            grouped = keep.tile([P, PACK * K_PASS], BF16, name=name, align_bytes=64)
+        def interleave(engine_copy, raw, pair, name):
+            grouped = keep.tile([P, 2 * K_PASS], BF16, name=name, align_bytes=64)
             engine_copy(
-                grouped[:].rearrange("p (t s j) -> p s j t", t=PACK, j=PACK),
-                raw[:].rearrange("p j (s t) -> p s j t", t=PACK),
+                grouped[:].rearrange("p (t s j) -> p s j t", t=2, j=PACK),
+                raw[:].rearrange("p j (s t) -> p s j t", t=PACK)[:, :, :, 2 * pair : 2 * pair + 2],
             )
             return grouped
 
+        s1 = gather(s1_table[:].bitcast(U8), U8, "s1")
+        xg0 = [interleave(nc.scalar.copy, x_raw[0], 0, "x_grouped0a")]
+        ts_row = gather(ts_table[:], F32, "ts_row")
+        xg0.append(interleave(nc.vector.tensor_copy, x_raw[0], 1, "x_grouped0b"))
+        turned = bank(4, "turned")
+        for b in range(4):
+            nc.tensor.transpose(turned[:, b * P : (b + 1) * P], ts_row[:, b * P : (b + 1) * P], ident[:])
+        ts_col = keep.tile([P, 4], F32, name="ts_col")
+        nc.scalar.copy(ts_col[:], turned[:, 96::P])
+        spread = bank(5, "spread")
+        for b in range(4):
+            nc.tensor.transpose(spread[:, b * P : (b + 1) * P], ts_col[:, b : b + 1].to_broadcast([P, P]), ident[:])
+        ts_all = keep.tile([P, SLOTS], F32, name="ts_all")
+        nc.scalar.copy(ts_all[:], spread[:])
+
         def quantize(grouped, fmt, name):
-            codes = keep.tile([P, K_PASS], U32, name=name + "_codes", align_bytes=64)
-            scales = keep.tile([P, K_PASS], U8, name=name + "_scales", align_bytes=64)
+            width = grouped.shape[1] // PACK
+            codes = keep.tile([P, width], U32, name=name + "_codes", align_bytes=64)
+            scales = keep.tile([P, width], U8, name=name + "_scales", align_bytes=64)
             nc.vector.quantize_mx(out=codes[:].bitcast(fmt), scales=scales[:], in_=grouped[:])
             return codes, scales
 
@@ -121,24 +135,21 @@ def tile_attend_gffn_sil_kernel(
                 stop=stop,
             )
 
-        def turn_x(grouped, h):
-            words = grouped[:].bitcast(F32)
-            by_row = keep.tile([P, PACK * K_PASS], BF16, name=f"x_by_row{h}", align_bytes=64)
-            for u in range(2):
-                bank = psum.tile([P, PACK, P], F32, name="x_turned", tag="turn")
-                for t in range(PACK):
-                    nc.tensor.transpose(bank[:, t, :], words[:, 256 * t + u : 256 * (t + 1) : 2], ident[:])
-                nc.scalar.copy(
-                    by_row[:, 1024 * u : 1024 * (u + 1)].rearrange("s (e p t) -> s e p t", e=2, t=PACK),
-                    bank[:].rearrange("s t p -> s (t p)").bitcast(BF16).rearrange("s (t p e) -> s e p t", t=PACK, e=2),
-                )
-            return by_row
+        def turn_x(grouped, by_row, u, n):
+            turned_words = bank(n, "x_turned")
+            for t in range(PACK):
+                words = grouped[t // 2][:].bitcast(F32)[:, 256 * (t % 2) + u : 256 * (t % 2 + 1) : 2]
+                nc.tensor.transpose(turned_words[:, t * P : (t + 1) * P], words, ident[:])
+            nc.scalar.copy(
+                by_row[:, 1024 * u : 1024 * (u + 1)].rearrange("s (e p t) -> s e p t", e=2, t=PACK),
+                turned_words[:].bitcast(BF16).rearrange("s (t p e) -> s e p t", t=PACK, e=2),
+            )
 
-        def first_product(xq, w1, h):
+        def first_product(xq, w1, h, banks):
             th, sl = [], []
             for t in range(PACK):
-                a = psum.tile([P, SLOTS], F32, name="a", tag="a")
-                product(a, xq, E4M3, slice(t * P, (t + 1) * P), w1, E4M3)
+                a = bank(banks[t], "a")
+                product(a, xq[t // 2], E4M3, slice(t % 2 * P, (t % 2 + 1) * P), w1, E4M3)
                 z = work.tile([P, SLOTS], F32, name="z")
                 nc.vector.scalar_tensor_tensor(z[:], a[:], us_col[:, h, t : t + 1], ts_all[:], ALU.mult, ALU.mult)
                 sl.append(work.tile([P, SLOTS], F32, name="silu_neg"))
@@ -147,20 +158,28 @@ def tile_attend_gffn_sil_kernel(
                 nc.scalar.activation(th[t][:], z[:], ACT.Tanh, scale=0.5)
             return th, sl
 
-        def gradient(dyq, w2, th, sl, wu, h):
-            da = keep.tile([P, PACK, SLOTS], BF16, name=f"da{h}")
-            for t in range(PACK):
-                dh = psum.tile([P, SLOTS], F32, name="dh", tag="dh")
-                product(dh, dyq, E5M2, slice(t * P, (t + 1) * P), w2, E4M3)
-                y = work.tile([P, SLOTS], F32, name="y")
-                nc.vector.scalar_tensor_tensor(y[:], dh[:], wu[:, h, t : t + 1], ts_all[:], ALU.mult, ALU.mult)
-                q = work.tile([P, SLOTS], F32, name="q")
-                nc.vector.scalar_tensor_tensor(q[:], th[t][:], 1.0, y[:], ALU.add, ALU.mult)
-                nc.vector.scalar_tensor_tensor(da[:, t, :], sl[t][:], 1.0, q[:], ALU.subtract, ALU.mult)
-            return da
+        def gradient(da, dyq, w2, th, sl, wu, h, pair):
+            y, q = {}, {}
 
-        def interleave_da(shares, da):
-            grouped = keep.tile([P, PACK * SLOTS], BF16, name="da_grouped", tag="da_grouped", align_bytes=64)
+            def scale_dh(t):
+                dh = bank(t % 2, "dh")
+                product(dh, dyq[t // 2], E5M2, slice(t % 2 * P, (t % 2 + 1) * P), w2, E4M3)
+                y[t] = work.tile([P, SLOTS], F32, name="y")
+                nc.vector.scalar_tensor_tensor(y[t][:], dh[:], wu[:, h, t : t + 1], ts_all[:], ALU.mult, ALU.mult)
+
+            def times_sigmoid(t):
+                q[t] = work.tile([P, SLOTS], F32, name="q")
+                nc.vector.scalar_tensor_tensor(q[t][:], th[t][:], 1.0, y[t][:], ALU.add, ALU.mult)
+
+            def finish(t):
+                nc.vector.scalar_tensor_tensor(da[:, t, :], sl[t][:], 1.0, q[t][:], ALU.subtract, ALU.mult)
+
+            for step in (scale_dh, times_sigmoid, finish):
+                for t in (2 * pair, 2 * pair + 1):
+                    step(t)
+
+        def interleave_da(shares, da, name):
+            grouped = keep.tile([P, PACK * SLOTS], BF16, name=name, align_bytes=64)
             for engine_copy, lo, hi in shares:
                 engine_copy(
                     grouped[:, PACK * lo : PACK * hi].rearrange("p (c i t) -> p c t i", i=4, t=PACK),
@@ -168,40 +187,45 @@ def tile_attend_gffn_sil_kernel(
                 )
             return grouped
 
-        xg0 = interleave(nc.scalar.copy, x_raw[0], "x_grouped0")
-        x_raw.append(load_half(x_rows, 1, "x_raw"))
-        xq0 = quantize(xg0, E4M3, "x0")
-        w1 = (gather(w1_table[:].bitcast(U32), U32, "w1"), s1)
+        xr0 = keep.tile([P, PACK * K_PASS], BF16, name="x_by_row0", align_bytes=64)
+        turn_x(xg0, xr0, 0, 7)
+        xq0 = [quantize(xg0[k], E4M3, f"x0{k}") for k in range(2)]
+        w1 = (gather(w1_table[:].bitcast(U32), U32, "w1", "x_raw0"), s1)
+        s2 = gather(s2_table[:].bitcast(U8), U8, "s2", "w1_table")
         wu = keep.tile([P, HALVES, PACK], F32, name="wu")
         nc.vector.scalar_tensor_tensor(wu[:], us_col[:], -0.5, wt_col[:], ALU.mult, ALU.mult)
-        xr0 = turn_x(xg0, 0)
-        dyg0 = interleave(nc.scalar.copy, dy_raw[0], "dy_grouped0")
-        dy_raw.append(load_half(dy_rows, 1, "dy_raw"))
-        th0, sl0 = first_product(xq0, w1, 0)
-        s2 = gather(s2_table[:], U8, "s2")
-        xrq = [quantize(xr0, E4M3, "xr0")]
-        dyq0 = quantize(dyg0, E5M2, "dy0")
+        dyg0 = [interleave(nc.scalar.copy, dy_raw[0], k, f"dy_grouped0{k}") for k in range(2)]
+        th0, sl0 = first_product(xq0, w1, 0, (0, 1, 2, 3))
         w2 = (gather(w2_table[:].bitcast(U32), U32, "w2"), s2)
-        xg1 = interleave(nc.scalar.copy, x_raw[1], "x_grouped1")
-        dyg1 = interleave(nc.scalar.copy, dy_raw[1], "dy_grouped1")
-        da0 = gradient(dyq0, w2, th0, sl0, wu, 0)
-        xq1 = quantize(xg1, E4M3, "x1")
-        th1, sl1 = first_product(xq1, w1, 1)
-        dyq1 = quantize(dyg1, E5M2, "dy1")
-        xr1 = turn_x(xg1, 1)
-        dag0 = interleave_da([(nc.scalar.copy, 0, SLOTS)], da0)
-        da1 = gradient(dyq1, w2, th1, sl1, wu, 1)
-        xrq.append(quantize(xr1, E4M3, "xr1"))
+        dyq0 = [quantize(dyg0[k], E5M2, f"dy0{k}") for k in range(2)]
+        xg1 = [interleave(nc.scalar.copy, x_raw[1], k, f"x_grouped1{k}") for k in range(2)]
+        dyg1 = [interleave(nc.scalar.copy, dy_raw[1], k, f"dy_grouped1{k}") for k in range(2)]
+        da0 = keep.tile([P, PACK, SLOTS], BF16, name="da0")
+        gradient(da0, dyq0, w2, th0, sl0, wu, 0, 0)
+        xq1 = [quantize(xg1[k], E4M3, f"x1{k}") for k in range(2)]
+        gradient(da0, dyq0, w2, th0, sl0, wu, 0, 1)
+        dyq1 = [quantize(dyg1[k], E5M2, f"dy1{k}") for k in range(2)]
+        th1, sl1 = first_product(xq1, w1, 1, (2, 4, 5, 6))
+        turn_x(xg0, xr0, 1, 3)
+        dag0 = interleave_da([(nc.scalar.copy, 0, SLOTS)], da0, "da_grouped0")
+        xr1 = keep.tile([P, PACK * K_PASS], BF16, name="x_by_row1", align_bytes=64)
+        turn_x(xg1, xr1, 0, 7)
+        turn_x(xg1, xr1, 1, 2)
+        xrq = [quantize(xr0, E4M3, "xr0")]
+        da1 = keep.tile([P, PACK, SLOTS], BF16, name="da1")
+        gradient(da1, dyq1, w2, th1, sl1, wu, 1, 0)
         daq = [quantize(dag0, E5M2, "da0")]
-        dag1 = interleave_da([(nc.vector.tensor_copy, 0, 320), (nc.scalar.copy, 320, SLOTS)], da1)
+        xrq.append(quantize(xr1, E4M3, "xr1"))
+        gradient(da1, dyq1, w2, th1, sl1, wu, 1, 1)
+        dag1 = interleave_da([(nc.vector.tensor_copy, 0, 320), (nc.scalar.copy, 320, SLOTS)], da1, "da_grouped1")
         daq.append(quantize(dag1, E5M2, "da1"))
 
-        window1 = keep.tile([P, UNITS], F32, name="window1", tag="da_grouped", align_bytes=64)
-        nc.gpsimd.memset(window1[:], 0.0)
+        window1 = keep.tile([P, UNITS], F32, name="window1", tag="da_grouped1", align_bytes=64)
+        nc.vector.memset(window1[:], 0.0)
         windows = [window0, window1]
         out_rows = out.rearrange("(p j) n -> p j n", j=PACK)
         for j in range(PACK):
-            dw = psum.tile([P, SLOTS], F32, name="dw", tag="dw")
+            dw = bank((4, 5, 6, 0)[j], "dw")
             for h in range(HALVES):
                 product(dw, xrq[h], E4M3, slice(j * P, (j + 1) * P), daq[h], E5M2, h == 0, h == HALVES - 1)
             dw_sb = keep.tile([P, SLOTS], F32, name=f"dw_sb{j}", tag=f"dw_sb{j}")

@@ -30,7 +30,7 @@ def tile_attend_gffn_sil_kernel(
     with ExitStack() as ctx:
         lists = ctx.enter_context(tc.tile_pool(name="lists", bufs=1))
         keep = ctx.enter_context(tc.tile_pool(name="keep", bufs=1))
-        work = ctx.enter_context(tc.tile_pool(name="work", bufs=4))
+        work = ctx.enter_context(tc.tile_pool(name="work", bufs=2))
         psum = ctx.enter_context(tc.psum_pool(name="psum", bufs=1))
 
         offsets = lists.tile([P, SLOTS // 16], U16, name="offsets")
@@ -86,6 +86,8 @@ def tile_attend_gffn_sil_kernel(
         make_identity(nc, ident[:])
         window0 = keep.tile([P, UNITS], F32, name="window0")
         nc.vector.memset(window0[:], 0.0)
+        window2 = keep.tile([P, UNITS], F32, name="window2")
+        nc.vector.memset(window2[:], 0.0)
         s2_table = cleared_plane("s2_table", "s2_table", nc.gpsimd)
         load_scales(s2_table, w2_scales, nc.gpsimd)
 
@@ -147,36 +149,48 @@ def tile_attend_gffn_sil_kernel(
 
         def first_product(xq, w1, h, banks):
             th, sl = [], []
-            for t in range(PACK):
-                a = bank(banks[t], "a")
-                product(a, xq[t // 2], E4M3, slice(t % 2 * P, (t % 2 + 1) * P), w1, E4M3)
-                z = work.tile([P, SLOTS], F32, name="z")
-                nc.vector.scalar_tensor_tensor(z[:], a[:], us_col[:, h, t : t + 1], ts_all[:], ALU.mult, ALU.mult)
-                sl.append(work.tile([P, SLOTS], F32, name="silu_neg"))
-                nc.scalar.activation(sl[t][:], z[:], ACT.Silu, scale=-1.0)
-                th.append(work.tile([P, SLOTS], F32, name="tanh_half"))
-                nc.scalar.activation(th[t][:], z[:], ACT.Tanh, scale=0.5)
+            for pair in range(2):
+                z = work.tile([P, 2, SLOTS], F32, name="z")
+                for k in range(2):
+                    t = 2 * pair + k
+                    a = bank(banks[t], "a")
+                    product(a, xq[pair], E4M3, slice(k * P, (k + 1) * P), w1, E4M3)
+                    nc.vector.scalar_tensor_tensor(
+                        z[:, k, :], a[:], us_col[:, h, t : t + 1], ts_all[:], ALU.mult, ALU.mult
+                    )
+                th.append(work.tile([P, 2, SLOTS], F32, name="tanh_half"))
+                sl.append(work.tile([P, 2, SLOTS], F32, name="silu_neg"))
+                nc.scalar.activation(th[pair][:], z[:], ACT.Tanh, scale=0.5)
+                nc.scalar.activation(sl[pair][:], z[:], ACT.Silu, scale=-1.0)
             return th, sl
 
-        def gradient(da, dyq, w2, th, sl, wu, h, pair):
-            y, q = {}, {}
+        def scale_dh(dyq, w2, wu, h, banks):
+            y = []
+            for pair in range(2):
+                y.append(work.tile([P, 2, SLOTS], F32, name="y"))
+                for k in range(2):
+                    t = 2 * pair + k
+                    dh = bank(banks[t], "dh")
+                    product(dh, dyq[pair], E5M2, slice(k * P, (k + 1) * P), w2, E4M3)
+                    nc.vector.scalar_tensor_tensor(
+                        y[pair][:, k, :], dh[:], wu[:, h, t : t + 1], ts_all[:], ALU.mult, ALU.mult
+                    )
+            return y
 
-            def scale_dh(t):
-                dh = bank(t % 2, "dh")
-                product(dh, dyq[t // 2], E5M2, slice(t % 2 * P, (t % 2 + 1) * P), w2, E4M3)
-                y[t] = work.tile([P, SLOTS], F32, name="y")
-                nc.vector.scalar_tensor_tensor(y[t][:], dh[:], wu[:, h, t : t + 1], ts_all[:], ALU.mult, ALU.mult)
+        def times_sigmoid(th, y):
+            q = []
+            for pair in range(2):
+                q.append(work.tile([P, 2, SLOTS], F32, name="q"))
+                nc.vector.scalar_tensor_tensor(q[pair][:], th[pair][:], 1.0, y[pair][:], ALU.add, ALU.mult)
+            return q
 
-            def times_sigmoid(t):
-                q[t] = work.tile([P, SLOTS], F32, name="q")
-                nc.vector.scalar_tensor_tensor(q[t][:], th[t][:], 1.0, y[t][:], ALU.add, ALU.mult)
-
-            def finish(t):
-                nc.vector.scalar_tensor_tensor(da[:, t, :], sl[t][:], 1.0, q[t][:], ALU.subtract, ALU.mult)
-
-            for step in (scale_dh, times_sigmoid, finish):
-                for t in (2 * pair, 2 * pair + 1):
-                    step(t)
+        def finish(sl, q, h):
+            da = keep.tile([P, PACK, SLOTS], BF16, name=f"da{h}")
+            for pair in range(2):
+                nc.vector.scalar_tensor_tensor(
+                    da[:, 2 * pair : 2 * pair + 2, :], sl[pair][:], 1.0, q[pair][:], ALU.subtract, ALU.mult
+                )
+            return da
 
         def interleave_da(shares, da, name):
             grouped = keep.tile([P, PACK * SLOTS], BF16, name=name, align_bytes=64)
@@ -200,32 +214,32 @@ def tile_attend_gffn_sil_kernel(
         dyq0 = [quantize(dyg0[k], E5M2, f"dy0{k}") for k in range(2)]
         xg1 = [interleave(nc.scalar.copy, x_raw[1], k, f"x_grouped1{k}") for k in range(2)]
         dyg1 = [interleave(nc.scalar.copy, dy_raw[1], k, f"dy_grouped1{k}") for k in range(2)]
-        da0 = keep.tile([P, PACK, SLOTS], BF16, name="da0")
-        gradient(da0, dyq0, w2, th0, sl0, wu, 0, 0)
+        y0 = scale_dh(dyq0, w2, wu, 0, (0, 1, 2, 3))
+        q0 = times_sigmoid(th0, y0)
         xq1 = [quantize(xg1[k], E4M3, f"x1{k}") for k in range(2)]
-        gradient(da0, dyq0, w2, th0, sl0, wu, 0, 1)
+        da0 = finish(sl0, q0, 0)
         dyq1 = [quantize(dyg1[k], E5M2, f"dy1{k}") for k in range(2)]
-        th1, sl1 = first_product(xq1, w1, 1, (2, 4, 5, 6))
+        th1, sl1 = first_product(xq1, w1, 1, (4, 5, 6, 7))
+        y1 = scale_dh(dyq1, w2, wu, 1, (0, 1, 2, 4))
         turn_x(xg0, xr0, 1, 3)
         dag0 = interleave_da([(nc.scalar.copy, 0, SLOTS)], da0, "da_grouped0")
         xr1 = keep.tile([P, PACK * K_PASS], BF16, name="x_by_row1", align_bytes=64)
-        turn_x(xg1, xr1, 0, 7)
-        turn_x(xg1, xr1, 1, 2)
+        turn_x(xg1, xr1, 0, 5)
+        turn_x(xg1, xr1, 1, 6)
         xrq = [quantize(xr0, E4M3, "xr0")]
-        da1 = keep.tile([P, PACK, SLOTS], BF16, name="da1")
-        gradient(da1, dyq1, w2, th1, sl1, wu, 1, 0)
+        q1 = times_sigmoid(th1, y1)
         daq = [quantize(dag0, E5M2, "da0")]
+        da1 = finish(sl1, q1, 1)
         xrq.append(quantize(xr1, E4M3, "xr1"))
-        gradient(da1, dyq1, w2, th1, sl1, wu, 1, 1)
         dag1 = interleave_da([(nc.vector.tensor_copy, 0, 320), (nc.scalar.copy, 320, SLOTS)], da1, "da_grouped1")
         daq.append(quantize(dag1, E5M2, "da1"))
 
         window1 = keep.tile([P, UNITS], F32, name="window1", tag="da_grouped1", align_bytes=64)
         nc.vector.memset(window1[:], 0.0)
-        windows = [window0, window1]
+        windows = [window0, window1, window2]
         out_rows = out.rearrange("(p j) n -> p j n", j=PACK)
         for j in range(PACK):
-            dw = bank((4, 5, 6, 0)[j], "dw")
+            dw = bank((7, 0, 1, 2)[j], "dw")
             for h in range(HALVES):
                 product(dw, xrq[h], E4M3, slice(j * P, (j + 1) * P), daq[h], E5M2, h == 0, h == HALVES - 1)
             dw_sb = keep.tile([P, SLOTS], F32, name=f"dw_sb{j}", tag=f"dw_sb{j}")
@@ -233,7 +247,3 @@ def tile_attend_gffn_sil_kernel(
             window = windows[j % 3]
             nc.vector.tensor_copy(window[:].indirect(offsets[:]), dw_sb[:])
             nc.sync.dma_start(out_rows[:, j, :], window[:])
-            if j == 0:
-                window2 = keep.tile([P, UNITS], F32, name="window2", tag="dw_sb0")
-                nc.gpsimd.memset(window2[:], 0.0)
-                windows.append(window2)

@@ -49,27 +49,30 @@ def tile_attend_gffn_sil_kernel(
             nc.sync.dma_start(table[:], words[0].rearrange("p n t -> p (n t)").bitcast(I32))
             return table
 
-        def cleared_plane(name, tag, engine):
-            table = keep.tile([P, UNITS // 4], I32, name=name, tag=tag, align_bytes=64)
-            engine.memset(table[:], 0)
-            return table
-
-        def load_scales(table, scales, queue):
+        def load_scales(scales, name):
+            table = keep.tile([P, UNITS // 4], I32, name=name, align_bytes=64)
+            nc.vector.memset(table[:], 0)
             for q in range(4):
-                queue.dma_start(
+                nc.sync.dma_start(
                     table[32 * q : 32 * q + 4, :],
                     scales[0, 4 * q : 4 * q + 4, :].bitcast(I32),
                 )
+            return table
 
         def bank(n, name):
             return psum.tile([P, SLOTS], F32, name=name, tag=f"bank{n}")
 
-        x_raw = [load_half(x_rows, 0, "x_raw0")]
         ts_table = keep.tile([P, UNITS], F32, name="ts_table")
         nc.scalar.dma_start(ts_table[96:P, :], ts[96:P, :])
+        x_raw = [load_half(x_rows, 0, "x_raw0")]
+        s1_table = load_scales(w1_scales, "s1_table")
         nc.vector.memset(ts_table[0:96, :], 0.0)
-        s1_table = cleared_plane("s1_table", "x_grouped0b", nc.gpsimd)
-        load_scales(s1_table, w1_scales, nc.scalar)
+        w1_table = load_words(w1_words, "w1_table")
+        s2_table = load_scales(w2_scales, "s2_table")
+        dy_raw = [load_half(dy_rows, 0, "dy_raw0")]
+        w2_table = load_words(w2_words, "w2_table")
+        x_raw.append(load_half(x_rows, 1, "x_raw1"))
+        dy_raw.append(load_half(dy_rows, 1, "dy_raw1"))
         warm = keep.tile([P, 2], F32, name="warm")
         nc.vector.memset(warm[:, 0:1], 0.0)
         nc.scalar.activation(warm[:, 1:2], warm[:, 0:1], ACT.Silu)
@@ -77,37 +80,30 @@ def tile_attend_gffn_sil_kernel(
         nc.scalar.dma_start(us_col[:], us.rearrange("(h p t) o -> p h (t o)", h=HALVES, t=PACK))
         wt_col = keep.tile([P, HALVES, PACK], F32, name="wt_col")
         nc.scalar.dma_start(wt_col[:], wt.rearrange("(h p t) o -> p h (t o)", h=HALVES, t=PACK))
-        w1_table = load_words(w1_words, "w1_table")
-        dy_raw = [load_half(dy_rows, 0, "dy_raw0")]
-        w2_table = load_words(w2_words, "w2_table")
-        x_raw.append(load_half(x_rows, 1, "x_raw1"))
-        dy_raw.append(load_half(dy_rows, 1, "dy_raw1"))
         ident = keep.tile([P, P], F32, name="ident")
         make_identity(nc, ident[:])
-        window0 = keep.tile([P, UNITS], F32, name="window0")
-        nc.vector.memset(window0[:], 0.0)
-        window2 = keep.tile([P, UNITS], F32, name="window2")
-        nc.vector.memset(window2[:], 0.0)
-        s2_table = cleared_plane("s2_table", "s2_table", nc.gpsimd)
-        load_scales(s2_table, w2_scales, nc.gpsimd)
 
         def gather(table, dtype, name, tag=None):
             picked = keep.tile([P, SLOTS], dtype, name=name, tag=tag or name, align_bytes=64)
             nc.vector.tensor_copy(picked[:], table.indirect(offsets[:]))
             return picked
 
-        def interleave(engine_copy, raw, pair, name):
-            grouped = keep.tile([P, 2 * K_PASS], BF16, name=name, align_bytes=64)
+        def interleave(engine_copy, raw, pair, grouped):
             engine_copy(
-                grouped[:].rearrange("p (t s j) -> p s j t", t=2, j=PACK),
+                grouped.rearrange("p (t s j) -> p s j t", t=2, j=PACK),
                 raw[:].rearrange("p j (s t) -> p s j t", t=PACK)[:, :, :, 2 * pair : 2 * pair + 2],
             )
             return grouped
 
-        s1 = gather(s1_table[:].bitcast(U8), U8, "s1")
-        xg0 = [interleave(nc.scalar.copy, x_raw[0], 0, "x_grouped0a")]
+        def interleave_on_scalar(raw, name):
+            grouped = keep.tile([P, 2, 2 * K_PASS], BF16, name=name, align_bytes=64)
+            return [interleave(nc.scalar.copy, raw, pair, grouped[:, pair, :]) for pair in range(2)]
+
+        x_first = keep.tile([P, 2 * K_PASS], BF16, name="x_grouped0a", align_bytes=64)
+        xg0 = [interleave(nc.scalar.copy, x_raw[0], 0, x_first[:])]
         ts_row = gather(ts_table[:], F32, "ts_row")
-        xg0.append(interleave(nc.vector.tensor_copy, x_raw[0], 1, "x_grouped0b"))
+        x_second = keep.tile([P, 2 * K_PASS], BF16, name="x_grouped0b", align_bytes=64)
+        xg0.append(interleave(nc.vector.tensor_copy, x_raw[0], 1, x_second[:]))
         turned = bank(4, "turned")
         for b in range(4):
             nc.tensor.transpose(turned[:, b * P : (b + 1) * P], ts_row[:, b * P : (b + 1) * P], ident[:])
@@ -119,11 +115,11 @@ def tile_attend_gffn_sil_kernel(
         ts_all = keep.tile([P, SLOTS], F32, name="ts_all")
         nc.scalar.copy(ts_all[:], spread[:])
 
-        def quantize(grouped, fmt, name):
+        def quantize(grouped, fmt, name, tag=None):
             width = grouped.shape[1] // PACK
-            codes = keep.tile([P, width], U32, name=name + "_codes", align_bytes=64)
+            codes = keep.tile([P, width], U32, name=name + "_codes", tag=tag or name + "_codes", align_bytes=64)
             scales = keep.tile([P, width], U8, name=name + "_scales", align_bytes=64)
-            nc.vector.quantize_mx(out=codes[:].bitcast(fmt), scales=scales[:], in_=grouped[:])
+            nc.vector.quantize_mx(out=codes[:].bitcast(fmt), scales=scales[:], in_=grouped)
             return codes, scales
 
         def product(bank, lhs, fmt_l, cols, rhs, fmt_r, start=True, stop=True):
@@ -140,17 +136,19 @@ def tile_attend_gffn_sil_kernel(
         def turn_x(grouped, by_row, u, n):
             turned_words = bank(n, "x_turned")
             for t in range(PACK):
-                words = grouped[t // 2][:].bitcast(F32)[:, 256 * (t % 2) + u : 256 * (t % 2 + 1) : 2]
+                words = grouped[t // 2].bitcast(F32)[:, 256 * (t % 2) + u : 256 * (t % 2 + 1) : 2]
                 nc.tensor.transpose(turned_words[:, t * P : (t + 1) * P], words, ident[:])
             nc.scalar.copy(
                 by_row[:, 1024 * u : 1024 * (u + 1)].rearrange("s (e p t) -> s e p t", e=2, t=PACK),
                 turned_words[:].bitcast(BF16).rearrange("s (t p e) -> s e p t", t=PACK, e=2),
             )
 
-        def first_product(xq, w1, h, banks):
-            th, sl = [], []
+        def first_product(xq, w1, h, banks, tag, act_tag):
+            acts = keep.tile([P, 2, 2, 2, SLOTS], F32, name=f"acts{h}", tag=act_tag, align_bytes=64)
+            th, sl = acts[:, 0], acts[:, 1]
+            z_all = keep.tile([P, 2, 2, SLOTS], F32, name=f"z{h}", tag=tag, align_bytes=64)
             for pair in range(2):
-                z = work.tile([P, 2, SLOTS], F32, name="z")
+                z = z_all[:, pair]
                 for k in range(2):
                     t = 2 * pair + k
                     a = bank(banks[t], "a")
@@ -158,10 +156,8 @@ def tile_attend_gffn_sil_kernel(
                     nc.vector.scalar_tensor_tensor(
                         z[:, k, :], a[:], us_col[:, h, t : t + 1], ts_all[:], ALU.mult, ALU.mult
                     )
-                th.append(work.tile([P, 2, SLOTS], F32, name="tanh_half"))
-                sl.append(work.tile([P, 2, SLOTS], F32, name="silu_neg"))
-                nc.scalar.activation(th[pair][:], z[:], ACT.Tanh, scale=0.5)
-                nc.scalar.activation(sl[pair][:], z[:], ACT.Silu, scale=-1.0)
+                nc.scalar.activation(th[:, pair], z, ACT.Tanh, scale=0.5)
+                nc.scalar.activation(sl[:, pair], z, ACT.Silu, scale=-1.0)
             return th, sl
 
         def scale_dh(dyq, w2, wu, h, banks):
@@ -181,14 +177,14 @@ def tile_attend_gffn_sil_kernel(
             q = []
             for pair in range(2):
                 q.append(work.tile([P, 2, SLOTS], F32, name="q"))
-                nc.vector.scalar_tensor_tensor(q[pair][:], th[pair][:], 1.0, y[pair][:], ALU.add, ALU.mult)
+                nc.vector.scalar_tensor_tensor(q[pair][:], th[:, pair], 1.0, y[pair][:], ALU.add, ALU.mult)
             return q
 
         def finish(sl, q, h):
             da = keep.tile([P, PACK, SLOTS], BF16, name=f"da{h}")
             for pair in range(2):
                 nc.vector.scalar_tensor_tensor(
-                    da[:, 2 * pair : 2 * pair + 2, :], sl[pair][:], 1.0, q[pair][:], ALU.subtract, ALU.mult
+                    da[:, 2 * pair : 2 * pair + 2, :], sl[:, pair], 1.0, q[pair][:], ALU.subtract, ALU.mult
                 )
             return da
 
@@ -202,44 +198,49 @@ def tile_attend_gffn_sil_kernel(
             return grouped
 
         xr0 = keep.tile([P, PACK * K_PASS], BF16, name="x_by_row0", align_bytes=64)
-        turn_x(xg0, xr0, 0, 7)
+        turn_x(xg0, xr0, 0, 4)
+        turn_x(xg0, xr0, 1, 5)
         xq0 = [quantize(xg0[k], E4M3, f"x0{k}") for k in range(2)]
-        w1 = (gather(w1_table[:].bitcast(U32), U32, "w1", "x_raw0"), s1)
-        s2 = gather(s2_table[:].bitcast(U8), U8, "s2", "w1_table")
+        s1 = gather(s1_table[:].bitcast(U8), U8, "s1")
+        w1 = (gather(w1_table[:].bitcast(U32), U32, "w1"), s1)
+        s2 = gather(s2_table[:].bitcast(U8), U8, "s2")
         wu = keep.tile([P, HALVES, PACK], F32, name="wu")
         nc.vector.scalar_tensor_tensor(wu[:], us_col[:], -0.5, wt_col[:], ALU.mult, ALU.mult)
-        dyg0 = [interleave(nc.scalar.copy, dy_raw[0], k, f"dy_grouped0{k}") for k in range(2)]
-        th0, sl0 = first_product(xq0, w1, 0, (0, 1, 2, 3))
+        dyg0 = interleave_on_scalar(dy_raw[0], "dy_grouped0")
+        th0, sl0 = first_product(xq0, w1, 0, (0, 1, 2, 3), "s2_table", "dy_raw0")
         w2 = (gather(w2_table[:].bitcast(U32), U32, "w2"), s2)
-        dyq0 = [quantize(dyg0[k], E5M2, f"dy0{k}") for k in range(2)]
-        xg1 = [interleave(nc.scalar.copy, x_raw[1], k, f"x_grouped1{k}") for k in range(2)]
-        dyg1 = [interleave(nc.scalar.copy, dy_raw[1], k, f"dy_grouped1{k}") for k in range(2)]
+        dyq0 = [quantize(dyg0[0], E5M2, "dy00"), quantize(dyg0[1], E5M2, "dy01", "w2_table")]
+        xrq = [quantize(xr0[:], E4M3, "xr0", "dy_grouped0")]
+        window0 = keep.tile([P, UNITS], F32, name="window0", tag="x_by_row0", align_bytes=64)
+        nc.gpsimd.memset(window0[:], 0.0)
+        xg1 = interleave_on_scalar(x_raw[1], "x_grouped1")
+        dyg1 = interleave_on_scalar(dy_raw[1], "dy_grouped1")
         y0 = scale_dh(dyq0, w2, wu, 0, (0, 1, 2, 3))
         q0 = times_sigmoid(th0, y0)
         xq1 = [quantize(xg1[k], E4M3, f"x1{k}") for k in range(2)]
         da0 = finish(sl0, q0, 0)
         dyq1 = [quantize(dyg1[k], E5M2, f"dy1{k}") for k in range(2)]
-        th1, sl1 = first_product(xq1, w1, 1, (4, 5, 6, 7))
-        y1 = scale_dh(dyq1, w2, wu, 1, (0, 1, 2, 4))
-        turn_x(xg0, xr0, 1, 3)
-        dag0 = interleave_da([(nc.scalar.copy, 0, SLOTS)], da0, "da_grouped0")
+        window2 = keep.tile([P, UNITS], F32, name="window2", tag="dy_grouped1", align_bytes=64)
+        nc.gpsimd.memset(window2[:], 0.0)
+        th1, sl1 = first_product(xq1, w1, 1, (0, 1, 2, 3), "s2_table", "acts1")
+        y1 = scale_dh(dyq1, w2, wu, 1, (4, 5, 0, 1))
+        dag0 = interleave_da([(nc.scalar.copy, 0, 256), (nc.scalar.copy, 256, SLOTS)], da0, "da_grouped0")
         xr1 = keep.tile([P, PACK * K_PASS], BF16, name="x_by_row1", align_bytes=64)
-        turn_x(xg1, xr1, 0, 5)
-        turn_x(xg1, xr1, 1, 6)
-        xrq = [quantize(xr0, E4M3, "xr0")]
+        turn_x(xg1, xr1, 0, 6)
+        turn_x(xg1, xr1, 1, 7)
         q1 = times_sigmoid(th1, y1)
-        daq = [quantize(dag0, E5M2, "da0")]
+        daq = [quantize(dag0[:], E5M2, "da0")]
         da1 = finish(sl1, q1, 1)
-        xrq.append(quantize(xr1, E4M3, "xr1"))
+        xrq.append(quantize(xr1[:], E4M3, "xr1"))
         dag1 = interleave_da([(nc.vector.tensor_copy, 0, 320), (nc.scalar.copy, 320, SLOTS)], da1, "da_grouped1")
-        daq.append(quantize(dag1, E5M2, "da1"))
+        daq.append(quantize(dag1[:], E5M2, "da1"))
 
         window1 = keep.tile([P, UNITS], F32, name="window1", tag="da_grouped1", align_bytes=64)
         nc.vector.memset(window1[:], 0.0)
         windows = [window0, window1, window2]
         out_rows = out.rearrange("(p j) n -> p j n", j=PACK)
         for j in range(PACK):
-            dw = bank((7, 0, 1, 2)[j], "dw")
+            dw = bank((2, 3, 4, 5)[j], "dw")
             for h in range(HALVES):
                 product(dw, xrq[h], E4M3, slice(j * P, (j + 1) * P), daq[h], E5M2, h == 0, h == HALVES - 1)
             dw_sb = keep.tile([P, SLOTS], F32, name=f"dw_sb{j}", tag=f"dw_sb{j}")

@@ -19,7 +19,6 @@ PACK = 4
 K_PASS = P * PACK
 D, E, R, SLOTS, UNITS = 512, 512, 1024, 512, 2048
 HALVES = R // K_PASS
-XS = 88
 FLOPS = 2 * R * SLOTS * (D + E + D)
 
 
@@ -30,8 +29,13 @@ def tile_attend_gffn_sil_kernel(
     with ExitStack() as ctx:
         lists = ctx.enter_context(tc.tile_pool(name="lists", bufs=1))
         keep = ctx.enter_context(tc.tile_pool(name="keep", bufs=1))
-        work = ctx.enter_context(tc.tile_pool(name="work", bufs=2))
         psum = ctx.enter_context(tc.psum_pool(name="psum", bufs=1))
+
+        def sbuf(shape, dtype, name, tag=None):
+            return keep.tile([P, *shape], dtype, name=name, tag=tag or name, align_bytes=64)
+
+        def bank(n, name):
+            return psum.tile([P, SLOTS], F32, name=name, tag=f"bank{n}")
 
         offsets = lists.tile([P, SLOTS // 16], U16, name="offsets")
         nc.sync.dma_start(offsets[:], offs)
@@ -40,17 +44,17 @@ def tile_attend_gffn_sil_kernel(
         dy_rows = dyT.rearrange("(p j) r -> p j r", j=PACK)
 
         def load_half(rows, h, name):
-            raw = keep.tile([P, PACK, K_PASS], F32, name=name, align_bytes=64)
+            raw = sbuf([PACK, K_PASS], F32, name)
             nc.sync.dma_start(raw[:], rows[:, :, h * K_PASS : (h + 1) * K_PASS])
             return raw
 
         def load_words(words, name):
-            table = keep.tile([P, UNITS], I32, name=name, align_bytes=64)
+            table = sbuf([UNITS], I32, name)
             nc.sync.dma_start(table[:], words[0].rearrange("p n t -> p (n t)").bitcast(I32))
             return table
 
         def load_scales(scales, name):
-            table = keep.tile([P, UNITS // 4], I32, name=name, align_bytes=64)
+            table = sbuf([UNITS // 4], I32, name)
             nc.vector.memset(table[:], 0)
             for q in range(4):
                 nc.sync.dma_start(
@@ -59,10 +63,12 @@ def tile_attend_gffn_sil_kernel(
                 )
             return table
 
-        def bank(n, name):
-            return psum.tile([P, SLOTS], F32, name=name, tag=f"bank{n}")
+        def load_column(vector, name):
+            column = sbuf([HALVES, PACK], F32, name)
+            nc.scalar.dma_start(column[:], vector.rearrange("(h p t) o -> p h (t o)", h=HALVES, t=PACK))
+            return column
 
-        ts_table = keep.tile([P, UNITS], F32, name="ts_table")
+        ts_table = sbuf([UNITS], F32, "ts_table")
         nc.scalar.dma_start(ts_table[96:P, :], ts[96:P, :])
         x_raw = [load_half(x_rows, 0, "x_raw0")]
         s1_table = load_scales(w1_scales, "s1_table")
@@ -73,58 +79,38 @@ def tile_attend_gffn_sil_kernel(
         w2_table = load_words(w2_words, "w2_table")
         x_raw.append(load_half(x_rows, 1, "x_raw1"))
         dy_raw.append(load_half(dy_rows, 1, "dy_raw1"))
-        warm = keep.tile([P, 2], F32, name="warm")
+        us_col = load_column(us, "us_col")
+        wt_col = load_column(wt, "wt_col")
+        warm = sbuf([2], F32, "warm")
         nc.vector.memset(warm[:, 0:1], 0.0)
         nc.scalar.activation(warm[:, 1:2], warm[:, 0:1], ACT.Silu)
-        us_col = keep.tile([P, HALVES, PACK], F32, name="us_col")
-        nc.scalar.dma_start(us_col[:], us.rearrange("(h p t) o -> p h (t o)", h=HALVES, t=PACK))
-        wt_col = keep.tile([P, HALVES, PACK], F32, name="wt_col")
-        nc.scalar.dma_start(wt_col[:], wt.rearrange("(h p t) o -> p h (t o)", h=HALVES, t=PACK))
-        ident = keep.tile([P, P], F32, name="ident")
+        ident = sbuf([P], F32, "ident")
         make_identity(nc, ident[:])
 
-        def gather(table, dtype, name, tag=None):
-            picked = keep.tile([P, SLOTS], dtype, name=name, tag=tag or name, align_bytes=64)
+        def gather(table, dtype, name):
+            picked = sbuf([SLOTS], dtype, name)
             nc.vector.tensor_copy(picked[:], table.indirect(offsets[:]))
             return picked
 
-        def interleave(engine_copy, raw, pair, grouped):
-            engine_copy(
-                grouped.rearrange("p (t s j) -> p s j t", t=2, j=PACK),
+        def group(raw, pair, name):
+            grouped = sbuf([2 * K_PASS], BF16, name)
+            nc.scalar.copy(
+                grouped[:].rearrange("p (t s j) -> p s j t", t=2, j=PACK),
                 raw[:].rearrange("p j (s t) -> p s j t", t=PACK)[:, :, :, 2 * pair : 2 * pair + 2],
             )
             return grouped
 
-        def interleave_on_scalar(raw, name):
-            grouped = keep.tile([P, 2, 2 * K_PASS], BF16, name=name, align_bytes=64)
-            return [interleave(nc.scalar.copy, raw, pair, grouped[:, pair, :]) for pair in range(2)]
-
-        x_first = keep.tile([P, 2 * K_PASS], BF16, name="x_grouped0a", align_bytes=64)
-        xg0 = [interleave(nc.scalar.copy, x_raw[0], 0, x_first[:])]
-        ts_row = gather(ts_table[:], F32, "ts_row")
-        x_second = keep.tile([P, 2 * K_PASS], BF16, name="x_grouped0b", align_bytes=64)
-        xg0.append(interleave(nc.vector.tensor_copy, x_raw[0], 1, x_second[:]))
-        turned = bank(4, "turned")
-        for b in range(4):
-            nc.tensor.transpose(turned[:, b * P : (b + 1) * P], ts_row[:, b * P : (b + 1) * P], ident[:])
-        ts_col = keep.tile([P, 4], F32, name="ts_col")
-        nc.scalar.copy(ts_col[:], turned[:, 96::P])
-        spread = bank(5, "spread")
-        for b in range(4):
-            nc.tensor.transpose(spread[:, b * P : (b + 1) * P], ts_col[:, b : b + 1].to_broadcast([P, P]), ident[:])
-        ts_all = keep.tile([P, SLOTS], F32, name="ts_all")
-        nc.scalar.copy(ts_all[:], spread[:])
-
-        def quantize(grouped, fmt, name, tag=None):
+        def quantize(grouped, fmt, name):
             width = grouped.shape[1] // PACK
-            codes = keep.tile([P, width], U32, name=name + "_codes", tag=tag or name + "_codes", align_bytes=64)
-            scales = keep.tile([P, width], U8, name=name + "_scales", align_bytes=64)
-            nc.vector.quantize_mx(out=codes[:].bitcast(fmt), scales=scales[:], in_=grouped)
+            codes = sbuf([width], U32, name + "_codes")
+            scales = sbuf([width], U8, name + "_scales")
+            nc.vector.quantize_mx(out=codes[:].bitcast(fmt), scales=scales[:], in_=grouped[:])
             return codes, scales
 
-        def product(bank, lhs, fmt_l, cols, rhs, fmt_r, start=True, stop=True):
+        def product(acc, lhs, fmt_l, k, rhs, fmt_r, start=True, stop=True):
+            cols = slice(k * P, (k + 1) * P)
             nc.tensor.matmul_mx(
-                out=bank[:],
+                out=acc[:],
                 lhsT=lhs[0][:, cols].bitcast(fmt_l),
                 lhsT_scale=lhs[1][:, cols],
                 rhs=rhs[0][:].bitcast(fmt_r),
@@ -133,117 +119,141 @@ def tile_attend_gffn_sil_kernel(
                 stop=stop,
             )
 
-        def turn_x(grouped, by_row, u, n):
-            turned_words = bank(n, "x_turned")
+        def turn_x(grouped, u, n, name):
+            turned_words = bank(n, name + "_words")
             for t in range(PACK):
-                words = grouped[t // 2].bitcast(F32)[:, 256 * (t % 2) + u : 256 * (t % 2 + 1) : 2]
+                words = grouped[t // 2][:].bitcast(F32)[:, 256 * (t % 2) + u : 256 * (t % 2 + 1) : 2]
                 nc.tensor.transpose(turned_words[:, t * P : (t + 1) * P], words, ident[:])
+            by_row = sbuf([2 * K_PASS], BF16, name)
             nc.scalar.copy(
-                by_row[:, 1024 * u : 1024 * (u + 1)].rearrange("s (e p t) -> s e p t", e=2, t=PACK),
+                by_row[:].rearrange("s (e p t) -> s e p t", e=2, t=PACK),
                 turned_words[:].bitcast(BF16).rearrange("s (t p e) -> s e p t", t=PACK, e=2),
             )
+            return by_row
 
-        def first_product(xq, w1, h, banks, tag, act_tag):
-            acts = keep.tile([P, 2, 2, 2, SLOTS], F32, name=f"acts{h}", tag=act_tag, align_bytes=64)
-            th, sl = acts[:, 0], acts[:, 1]
-            z_all = keep.tile([P, 2, 2, SLOTS], F32, name=f"z{h}", tag=tag, align_bytes=64)
+        def scaled_first_product(xq, w1, h, z, t):
+            a = bank(t, "a")
+            product(a, xq[t // 2], E4M3, t % 2, w1, E4M3)
+            nc.vector.scalar_tensor_tensor(z[:, t, :], a[:], us_col[:, h, t : t + 1], ts_all[:], ALU.mult, ALU.mult)
+
+        def activations(z, h):
+            acts = sbuf([2, PACK, SLOTS], F32, f"acts{h}", ("dy_raw0", "acts1")[h])
+            sl, th = acts[:, 0], acts[:, 1]
             for pair in range(2):
-                z = z_all[:, pair]
-                for k in range(2):
-                    t = 2 * pair + k
-                    a = bank(banks[t], "a")
-                    product(a, xq[pair], E4M3, slice(k * P, (k + 1) * P), w1, E4M3)
-                    nc.vector.scalar_tensor_tensor(
-                        z[:, k, :], a[:], us_col[:, h, t : t + 1], ts_all[:], ALU.mult, ALU.mult
-                    )
-                nc.scalar.activation(th[:, pair], z, ACT.Tanh, scale=0.5)
-                nc.scalar.activation(sl[:, pair], z, ACT.Silu, scale=-1.0)
-            return th, sl
-
-        def scale_dh(dyq, w2, wu, h, banks):
-            y = []
+                rows = slice(2 * pair, 2 * pair + 2)
+                nc.scalar.activation(sl[:, rows, :], z[:, rows, :], ACT.Silu, scale=-1.0)
             for pair in range(2):
-                y.append(work.tile([P, 2, SLOTS], F32, name="y"))
-                for k in range(2):
-                    t = 2 * pair + k
-                    dh = bank(banks[t], "dh")
-                    product(dh, dyq[pair], E5M2, slice(k * P, (k + 1) * P), w2, E4M3)
-                    nc.vector.scalar_tensor_tensor(
-                        y[pair][:, k, :], dh[:], wu[:, h, t : t + 1], ts_all[:], ALU.mult, ALU.mult
-                    )
-            return y
+                rows = slice(2 * pair, 2 * pair + 2)
+                nc.scalar.activation(th[:, rows, :], z[:, rows, :], ACT.Tanh, scale=0.5)
+            return sl, th
 
-        def times_sigmoid(th, y):
-            q = []
+        def times_dh(sl, dyq, w2, h):
+            m = sbuf([PACK, SLOTS], F32, f"m{h}", "m")
+            for t in range(PACK):
+                dh = bank(4 + t, "dh")
+                product(dh, dyq[t // 2], E5M2, t % 2, w2, E4M3)
+                nc.vector.scalar_tensor_tensor(m[:, t, :], sl[:, t, :], 1.0, dh[:], ALU.subtract, ALU.mult)
+            return m
+
+        def times_sigmoid(th, m, h):
+            n = sbuf([PACK, SLOTS], F32, f"n{h}")
             for pair in range(2):
-                q.append(work.tile([P, 2, SLOTS], F32, name="q"))
-                nc.vector.scalar_tensor_tensor(q[pair][:], th[:, pair], 1.0, y[pair][:], ALU.add, ALU.mult)
-            return q
+                rows = slice(2 * pair, 2 * pair + 2)
+                nc.vector.scalar_tensor_tensor(n[:, rows, :], th[:, rows, :], 1.0, m[:, rows, :], ALU.add, ALU.mult)
+            return n
 
-        def finish(sl, q, h):
-            da = keep.tile([P, PACK, SLOTS], BF16, name=f"da{h}")
-            for pair in range(2):
-                nc.vector.scalar_tensor_tensor(
-                    da[:, 2 * pair : 2 * pair + 2, :], sl[:, pair], 1.0, q[pair][:], ALU.subtract, ALU.mult
-                )
-            return da
+        def finish(n, h, da, part):
+            cols = slice(part * 256, (part + 1) * 256)
+            nc.vector.tensor_tensor(
+                da[:, PACK * cols.start : PACK * cols.stop].rearrange("p (c i t) -> p c t i", i=4, t=PACK),
+                n[:, :, cols].rearrange("p t (c i) -> p c t i", i=4),
+                factors[h][:, :, cols].rearrange("p t (c i) -> p c t i", i=4),
+                ALU.mult,
+            )
 
-        def interleave_da(shares, da, name):
-            grouped = keep.tile([P, PACK * SLOTS], BF16, name=name, align_bytes=64)
-            for engine_copy, lo, hi in shares:
-                engine_copy(
-                    grouped[:, PACK * lo : PACK * hi].rearrange("p (c i t) -> p c t i", i=4, t=PACK),
-                    da[:, :, lo:hi].rearrange("p t (c i) -> p c t i", i=4),
-                )
-            return grouped
+        ts_row = gather(ts_table[:], F32, "ts_row")
+        xg0 = [group(x_raw[0], 0, "x_grouped00")]
+        turned = bank(6, "turned")
+        for b in range(4):
+            nc.tensor.transpose(turned[:, b * P : (b + 1) * P], ts_row[:, b * P : (b + 1) * P], ident[:])
+        ts_col = sbuf([4], F32, "ts_col")
+        nc.scalar.copy(ts_col[:], turned[:, 96::P])
+        xg0.append(group(x_raw[0], 1, "x_grouped01"))
+        spread = bank(7, "spread")
+        for b in range(4):
+            nc.tensor.transpose(spread[:, b * P : (b + 1) * P], ts_col[:, b : b + 1].to_broadcast([P, P]), ident[:])
+        ts_all = sbuf([SLOTS], F32, "ts_all")
+        nc.scalar.copy(ts_all[:], spread[:])
 
-        xr0 = keep.tile([P, PACK * K_PASS], BF16, name="x_by_row0", align_bytes=64)
-        turn_x(xg0, xr0, 0, 4)
-        turn_x(xg0, xr0, 1, 5)
-        xq0 = [quantize(xg0[k], E4M3, f"x0{k}") for k in range(2)]
+        wu = sbuf([HALVES, PACK], F32, "wu")
+        nc.vector.scalar_tensor_tensor(wu[:], us_col[:], -0.5, wt_col[:], ALU.mult, ALU.mult)
+        factors = [sbuf([PACK, SLOTS], F32, f"factors{h}") for h in range(HALVES)]
+        for h in range(HALVES):
+            for t in range(PACK):
+                nc.gpsimd.tensor_scalar(factors[h][:, t, :], ts_all[:], wu[:, h, t : t + 1], 0.0, ALU.mult, ALU.add)
+
         s1 = gather(s1_table[:].bitcast(U8), U8, "s1")
+        xq0 = [quantize(xg0[0], E4M3, "x00")]
+        xq0.append(quantize(xg0[1], E4M3, "x01"))
         w1 = (gather(w1_table[:].bitcast(U32), U32, "w1"), s1)
         s2 = gather(s2_table[:].bitcast(U8), U8, "s2")
-        wu = keep.tile([P, HALVES, PACK], F32, name="wu")
-        nc.vector.scalar_tensor_tensor(wu[:], us_col[:], -0.5, wt_col[:], ALU.mult, ALU.mult)
-        dyg0 = interleave_on_scalar(dy_raw[0], "dy_grouped0")
-        th0, sl0 = first_product(xq0, w1, 0, (0, 1, 2, 3), "s2_table", "dy_raw0")
+        xr = {(0, 0): turn_x(xg0, 0, 4, "x_by_row00")}
+        dyg0 = [group(dy_raw[0], pair, f"dy_grouped0{pair}") for pair in range(2)]
+        z0 = sbuf([PACK, SLOTS], F32, "z0", "z")
+        for t in range(PACK):
+            scaled_first_product(xq0, w1, 0, z0, t)
+        xrq = {(0, 0): quantize(xr[0, 0], E4M3, "xr00")}
+        sl0, th0 = activations(z0, 0)
         w2 = (gather(w2_table[:].bitcast(U32), U32, "w2"), s2)
-        dyq0 = [quantize(dyg0[0], E5M2, "dy00"), quantize(dyg0[1], E5M2, "dy01", "w2_table")]
-        xrq = [quantize(xr0[:], E4M3, "xr0", "dy_grouped0")]
-        window0 = keep.tile([P, UNITS], F32, name="window0", tag="x_by_row0", align_bytes=64)
-        nc.gpsimd.memset(window0[:], 0.0)
-        xg1 = interleave_on_scalar(x_raw[1], "x_grouped1")
-        dyg1 = interleave_on_scalar(dy_raw[1], "dy_grouped1")
-        y0 = scale_dh(dyq0, w2, wu, 0, (0, 1, 2, 3))
-        q0 = times_sigmoid(th0, y0)
-        xq1 = [quantize(xg1[k], E4M3, f"x1{k}") for k in range(2)]
-        da0 = finish(sl0, q0, 0)
-        dyq1 = [quantize(dyg1[k], E5M2, f"dy1{k}") for k in range(2)]
-        window2 = keep.tile([P, UNITS], F32, name="window2", tag="dy_grouped1", align_bytes=64)
+        dyq0 = [quantize(dyg0[pair], E5M2, f"dy0{pair}") for pair in range(2)]
+        window1 = sbuf([UNITS], F32, "window1", "dy_grouped01")
+        nc.gpsimd.memset(window1[:], 0.0)
+        m0 = times_dh(sl0, dyq0, w2, 0)
+        window2 = sbuf([UNITS], F32, "window2", "dy01_codes")
         nc.gpsimd.memset(window2[:], 0.0)
-        th1, sl1 = first_product(xq1, w1, 1, (0, 1, 2, 3), "s2_table", "acts1")
-        y1 = scale_dh(dyq1, w2, wu, 1, (4, 5, 0, 1))
-        dag0 = interleave_da([(nc.scalar.copy, 0, 256), (nc.scalar.copy, 256, SLOTS)], da0, "da_grouped0")
-        xr1 = keep.tile([P, PACK * K_PASS], BF16, name="x_by_row1", align_bytes=64)
-        turn_x(xg1, xr1, 0, 6)
-        turn_x(xg1, xr1, 1, 7)
-        q1 = times_sigmoid(th1, y1)
-        daq = [quantize(dag0[:], E5M2, "da0")]
-        da1 = finish(sl1, q1, 1)
-        xrq.append(quantize(xr1[:], E4M3, "xr1"))
-        dag1 = interleave_da([(nc.vector.tensor_copy, 0, 320), (nc.scalar.copy, 320, SLOTS)], da1, "da_grouped1")
-        daq.append(quantize(dag1[:], E5M2, "da1"))
+        xg1 = [group(x_raw[1], pair, f"x_grouped1{pair}") for pair in range(2)]
+        dyg1 = [group(dy_raw[1], pair, f"dy_grouped1{pair}") for pair in range(2)]
+        n0 = times_sigmoid(th0, m0, 0)
+        xq1 = [quantize(xg1[0], E4M3, "x10")]
+        da0 = sbuf([PACK * SLOTS], BF16, "da0")
+        finish(n0, 0, da0, 0)
+        xq1.append(quantize(xg1[1], E4M3, "x11"))
+        z1 = sbuf([PACK, SLOTS], F32, "z1", "z")
+        for t in range(PACK):
+            scaled_first_product(xq1, w1, 1, z1, t)
+        sl1, th1 = activations(z1, 1)
+        dyq1 = [quantize(dyg1[0], E5M2, "dy10")]
+        finish(n0, 0, da0, 1)
+        dyq1.append(quantize(dyg1[1], E5M2, "dy11"))
+        daq = [quantize(da0, E5M2, "da0")]
+        window0 = sbuf([UNITS], F32, "window0", "da0")
+        nc.gpsimd.memset(window0[:], 0.0)
+        xr[1, 0] = turn_x(xg1, 0, 0, "x_by_row10")
+        m1 = times_dh(sl1, dyq1, w2, 1)
+        n1 = times_sigmoid(th1, m1, 1)
+        xrq[1, 0] = quantize(xr[1, 0], E4M3, "xr10")
+        da1 = sbuf([PACK * SLOTS], BF16, "da1")
+        codes1 = sbuf([SLOTS], U32, "da1_codes")
+        scales1 = sbuf([SLOTS], U8, "da1_scales")
+        for part in range(2):
+            finish(n1, 1, da1, part)
+        for part in range(2):
+            cols = slice(part * 256, (part + 1) * 256)
+            nc.vector.quantize_mx(
+                out=codes1[:, cols].bitcast(E5M2), scales=scales1[:, cols], in_=da1[:, part * 1024 : (part + 1) * 1024]
+            )
+        daq.append((codes1, scales1))
+        for h, grouped in enumerate((xg0, xg1)):
+            xr[h, 1] = turn_x(grouped, 1, 4 + h, f"x_by_row{h}1")
+            xrq[h, 1] = quantize(xr[h, 1], E4M3, f"xr{h}1")
 
-        window1 = keep.tile([P, UNITS], F32, name="window1", tag="da_grouped1", align_bytes=64)
-        nc.vector.memset(window1[:], 0.0)
         windows = [window0, window1, window2]
         out_rows = out.rearrange("(p j) n -> p j n", j=PACK)
         for j in range(PACK):
-            dw = bank((2, 3, 4, 5)[j], "dw")
+            dw = bank((1, 2, 3, 6)[j], "dw")
             for h in range(HALVES):
-                product(dw, xrq[h], E4M3, slice(j * P, (j + 1) * P), daq[h], E5M2, h == 0, h == HALVES - 1)
-            dw_sb = keep.tile([P, SLOTS], F32, name=f"dw_sb{j}", tag=f"dw_sb{j}")
+                product(dw, xrq[h, j // 2], E4M3, j % 2, daq[h], E5M2, h == 0, h == HALVES - 1)
+            dw_sb = sbuf([SLOTS], F32, f"dw_sb{j}")
             nc.scalar.copy(dw_sb[:], dw[:])
             window = windows[j % 3]
             nc.vector.tensor_copy(window[:].indirect(offsets[:]), dw_sb[:])

@@ -56,31 +56,29 @@ def tile_attend_gffn_sil_kernel(
         def load_scales(scales, name):
             table = sbuf([UNITS // 4], I32, name)
             nc.vector.memset(table[:], 0)
-            for q in range(4):
-                nc.sync.dma_start(
-                    table[32 * q : 32 * q + 4, :],
-                    scales[0, 4 * q : 4 * q + 4, :].bitcast(I32),
-                )
+            for r in range(4):
+                nc.sync.dma_start(table[r:P:32, :], scales[0, r:16:4, :].bitcast(I32))
             return table
 
         def load_column(vector, name):
-            column = sbuf([HALVES, PACK], F32, name)
-            nc.scalar.dma_start(column[:], vector.rearrange("(h p t) o -> p h (t o)", h=HALVES, t=PACK))
+            padded = sbuf([HALVES, 2 * PACK], F32, name)
+            column = padded[:, :, 0:PACK]
+            nc.sync.dma_start(column, vector.rearrange("(h p t) o -> p h (t o)", h=HALVES, t=PACK))
             return column
 
         ts_table = sbuf([UNITS], F32, "ts_table")
-        nc.scalar.dma_start(ts_table[96:P, :], ts[96:P, :])
+        nc.vector.memset(ts_table[:], 0.0)
+        nc.scalar.dma_start(ts_table[0:1, :], ts[0:1, :])
         x_raw = [load_half(x_rows, 0, "x_raw0")]
         s1_table = load_scales(w1_scales, "s1_table")
-        nc.vector.memset(ts_table[0:96, :], 0.0)
         w1_table = load_words(w1_words, "w1_table")
+        us_col = load_column(us, "us_col")
+        wt_col = load_column(wt, "wt_col")
         s2_table = load_scales(w2_scales, "s2_table")
         dy_raw = [load_half(dy_rows, 0, "dy_raw0")]
         w2_table = load_words(w2_words, "w2_table")
         x_raw.append(load_half(x_rows, 1, "x_raw1"))
         dy_raw.append(load_half(dy_rows, 1, "dy_raw1"))
-        us_col = load_column(us, "us_col")
-        wt_col = load_column(wt, "wt_col")
         warm = sbuf([2], F32, "warm")
         nc.vector.memset(warm[:, 0:1], 0.0)
         nc.scalar.activation(warm[:, 1:2], warm[:, 0:1], ACT.Silu)
@@ -177,7 +175,7 @@ def tile_attend_gffn_sil_kernel(
         for b in range(4):
             nc.tensor.transpose(turned[:, b * P : (b + 1) * P], ts_row[:, b * P : (b + 1) * P], ident[:])
         ts_col = sbuf([4], F32, "ts_col")
-        nc.scalar.copy(ts_col[:], turned[:, 96::P])
+        nc.scalar.copy(ts_col[:], turned[:, 0::P])
         xg0.append(group(x_raw[0], 1, "x_grouped01"))
         spread = bank(7, "spread")
         for b in range(4):
@@ -186,9 +184,11 @@ def tile_attend_gffn_sil_kernel(
         nc.scalar.copy(ts_all[:], spread[:])
 
         wu = sbuf([HALVES, PACK], F32, "wu")
-        nc.vector.scalar_tensor_tensor(wu[:], us_col[:], -0.5, wt_col[:], ALU.mult, ALU.mult)
-        factors = [sbuf([PACK, SLOTS], F32, f"factors{h}") for h in range(HALVES)]
-        for h in range(HALVES):
+        nc.vector.scalar_tensor_tensor(wu[:], us_col, -0.5, wt_col, ALU.mult, ALU.mult)
+        factors = []
+
+        def outer_product(h, tag):
+            factors.append(sbuf([PACK, SLOTS], F32, f"factors{h}", tag))
             for t in range(PACK):
                 nc.gpsimd.tensor_scalar(factors[h][:, t, :], ts_all[:], wu[:, h, t : t + 1], 0.0, ALU.mult, ALU.add)
 
@@ -196,6 +196,7 @@ def tile_attend_gffn_sil_kernel(
         xq0 = [quantize(xg0[0], E4M3, "x00")]
         xq0.append(quantize(xg0[1], E4M3, "x01"))
         w1 = (gather(w1_table[:].bitcast(U32), U32, "w1"), s1)
+        outer_product(0, "w1_table")
         s2 = gather(s2_table[:].bitcast(U8), U8, "s2")
         xr = {(0, 0): turn_x(xg0, 0, 4, "x_by_row00")}
         dyg0 = [group(dy_raw[0], pair, f"dy_grouped0{pair}") for pair in range(2)]
@@ -221,6 +222,7 @@ def tile_attend_gffn_sil_kernel(
         z1 = sbuf([PACK, SLOTS], F32, "z1", "z")
         for t in range(PACK):
             scaled_first_product(xq1, w1, 1, z1, t)
+        outer_product(1, "x10_codes")
         sl1, th1 = activations(z1, 1)
         dyq1 = [quantize(dyg1[0], E5M2, "dy10")]
         finish(n0, 0, da0, 1)

@@ -72,9 +72,9 @@ def tile_attend_gffn_sil_kernel(
         x_raw = [load_half(x_rows, 0, "x_raw0")]
         s1_table = load_scales(w1_scales, "s1_table")
         w1_table = load_words(w1_words, "w1_table")
+        s2_table = load_scales(w2_scales, "s2_table")
         us_col = load_column(us, "us_col")
         wt_col = load_column(wt, "wt_col")
-        s2_table = load_scales(w2_scales, "s2_table")
         dy_raw = [load_half(dy_rows, 0, "dy_raw0")]
         w2_table = load_words(w2_words, "w2_table")
         x_raw.append(load_half(x_rows, 1, "x_raw1"))
@@ -85,22 +85,22 @@ def tile_attend_gffn_sil_kernel(
         ident = sbuf([P], F32, "ident")
         make_identity(nc, ident[:])
 
-        def gather(table, dtype, name):
-            picked = sbuf([SLOTS], dtype, name)
+        def gather(table, dtype, name, tag=None):
+            picked = sbuf([SLOTS], dtype, name, tag)
             nc.vector.tensor_copy(picked[:], table.indirect(offsets[:]))
             return picked
 
-        def group(raw, pair, name):
+        def group(raw, pair, name, copy=nc.scalar.copy):
             grouped = sbuf([2 * K_PASS], BF16, name)
-            nc.scalar.copy(
+            copy(
                 grouped[:].rearrange("p (t s j) -> p s j t", t=2, j=PACK),
                 raw[:].rearrange("p j (s t) -> p s j t", t=PACK)[:, :, :, 2 * pair : 2 * pair + 2],
             )
             return grouped
 
-        def quantize(grouped, fmt, name):
+        def quantize(grouped, fmt, name, tag=None):
             width = grouped.shape[1] // PACK
-            codes = sbuf([width], U32, name + "_codes")
+            codes = sbuf([width], U32, name + "_codes", tag)
             scales = sbuf([width], U8, name + "_scales")
             nc.vector.quantize_mx(out=codes[:].bitcast(fmt), scales=scales[:], in_=grouped[:])
             return codes, scales
@@ -153,12 +153,9 @@ def tile_attend_gffn_sil_kernel(
                 nc.vector.scalar_tensor_tensor(m[:, t, :], sl[:, t, :], 1.0, dh[:], ALU.subtract, ALU.mult)
             return m
 
-        def times_sigmoid(th, m, h):
-            n = sbuf([PACK, SLOTS], F32, f"n{h}")
-            for pair in range(2):
-                rows = slice(2 * pair, 2 * pair + 2)
-                nc.vector.scalar_tensor_tensor(n[:, rows, :], th[:, rows, :], 1.0, m[:, rows, :], ALU.add, ALU.mult)
-            return n
+        def times_sigmoid(th, m, n, pair):
+            rows = slice(2 * pair, 2 * pair + 2)
+            nc.vector.scalar_tensor_tensor(n[:, rows, :], th[:, rows, :], 1.0, m[:, rows, :], ALU.add, ALU.mult)
 
         def finish(n, h, da, part):
             cols = slice(part * 256, (part + 1) * 256)
@@ -184,7 +181,6 @@ def tile_attend_gffn_sil_kernel(
         nc.scalar.copy(ts_all[:], spread[:])
 
         wu = sbuf([HALVES, PACK], F32, "wu")
-        nc.vector.scalar_tensor_tensor(wu[:], us_col, -0.5, wt_col, ALU.mult, ALU.mult)
         factors = []
 
         def outer_product(h, tag):
@@ -192,47 +188,55 @@ def tile_attend_gffn_sil_kernel(
             for t in range(PACK):
                 nc.gpsimd.tensor_scalar(factors[h][:, t, :], ts_all[:], wu[:, h, t : t + 1], 0.0, ALU.mult, ALU.add)
 
-        s1 = gather(s1_table[:].bitcast(U8), U8, "s1")
-        xq0 = [quantize(xg0[0], E4M3, "x00")]
-        xq0.append(quantize(xg0[1], E4M3, "x01"))
+        def cleared_window(name, tag):
+            window = sbuf([UNITS], F32, name, tag)
+            nc.gpsimd.memset(window[:], 0.0)
+            return window
+
+        s1 = gather(s1_table[:].bitcast(U8), U8, "s1", "ts_table")
+        xq0 = [quantize(xg0[0], E4M3, "x00", "s1_table")]
+        xq0.append(quantize(xg0[1], E4M3, "x01", "ts_row"))
         w1 = (gather(w1_table[:].bitcast(U32), U32, "w1"), s1)
-        outer_product(0, "w1_table")
         s2 = gather(s2_table[:].bitcast(U8), U8, "s2")
-        xr = {(0, 0): turn_x(xg0, 0, 4, "x_by_row00")}
-        dyg0 = [group(dy_raw[0], pair, f"dy_grouped0{pair}") for pair in range(2)]
-        z0 = sbuf([PACK, SLOTS], F32, "z0", "z")
+        half_us = sbuf([HALVES, PACK], F32, "half_us")
+        nc.gpsimd.tensor_scalar(half_us[:], us_col, -0.5, 0.0, ALU.mult, ALU.add)
+        nc.gpsimd.tensor_tensor(wu[:], half_us[:], wt_col, ALU.mult)
+        xr = {(0, 0): turn_x(xg0, 0, 6, "x_by_row00")}
+        outer_product(0, "w1_table")
+        dyg0 = [group(dy_raw[0], 0, "dy_grouped00")]
+        z0 = sbuf([PACK, SLOTS], F32, "z0", "s2_table")
         for t in range(PACK):
             scaled_first_product(xq0, w1, 0, z0, t)
-        xrq = {(0, 0): quantize(xr[0, 0], E4M3, "xr00")}
+        dyg0.append(group(dy_raw[0], 1, "dy_grouped01", nc.vector.tensor_copy))
         sl0, th0 = activations(z0, 0)
-        w2 = (gather(w2_table[:].bitcast(U32), U32, "w2"), s2)
         dyq0 = [quantize(dyg0[pair], E5M2, f"dy0{pair}") for pair in range(2)]
-        window1 = sbuf([UNITS], F32, "window1", "dy_grouped01")
-        nc.gpsimd.memset(window1[:], 0.0)
+        w2 = (gather(w2_table[:].bitcast(U32), U32, "w2"), s2)
+        xrq = {(0, 0): quantize(xr[0, 0], E4M3, "xr00", "w2_table")}
+        outer_product(1, "x_by_row00")
+        windows = [cleared_window("window0", "dy01_codes")]
         m0 = times_dh(sl0, dyq0, w2, 0)
-        window2 = sbuf([UNITS], F32, "window2", "dy01_codes")
-        nc.gpsimd.memset(window2[:], 0.0)
         xg1 = [group(x_raw[1], pair, f"x_grouped1{pair}") for pair in range(2)]
         dyg1 = [group(dy_raw[1], pair, f"dy_grouped1{pair}") for pair in range(2)]
-        n0 = times_sigmoid(th0, m0, 0)
-        xq1 = [quantize(xg1[0], E4M3, "x10")]
+        n0 = sbuf([PACK, SLOTS], F32, "n0")
+        for pair in range(2):
+            times_sigmoid(th0, m0, n0, pair)
+        xq1 = [quantize(xg1[pair], E4M3, f"x1{pair}") for pair in range(2)]
         da0 = sbuf([PACK * SLOTS], BF16, "da0")
         finish(n0, 0, da0, 0)
-        xq1.append(quantize(xg1[1], E4M3, "x11"))
-        z1 = sbuf([PACK, SLOTS], F32, "z1", "z")
+        z1 = sbuf([PACK, SLOTS], F32, "z1", "s2_table")
         for t in range(PACK):
             scaled_first_product(xq1, w1, 1, z1, t)
-        outer_product(1, "x10_codes")
+        windows.append(cleared_window("window1", "x10_codes"))
         sl1, th1 = activations(z1, 1)
-        dyq1 = [quantize(dyg1[0], E5M2, "dy10")]
+        dyq1 = [quantize(dyg1[pair], E5M2, f"dy1{pair}") for pair in range(2)]
         finish(n0, 0, da0, 1)
-        dyq1.append(quantize(dyg1[1], E5M2, "dy11"))
         daq = [quantize(da0, E5M2, "da0")]
-        window0 = sbuf([UNITS], F32, "window0", "da0")
-        nc.gpsimd.memset(window0[:], 0.0)
-        xr[1, 0] = turn_x(xg1, 0, 0, "x_by_row10")
+        windows.append(cleared_window("window2", "da0"))
+        xr[1, 0] = turn_x(xg1, 0, 3, "x_by_row10")
         m1 = times_dh(sl1, dyq1, w2, 1)
-        n1 = times_sigmoid(th1, m1, 1)
+        n1 = sbuf([PACK, SLOTS], F32, "n1")
+        for pair in range(2):
+            times_sigmoid(th1, m1, n1, pair)
         xrq[1, 0] = quantize(xr[1, 0], E4M3, "xr10")
         da1 = sbuf([PACK * SLOTS], BF16, "da1")
         codes1 = sbuf([SLOTS], U32, "da1_codes")
@@ -249,10 +253,9 @@ def tile_attend_gffn_sil_kernel(
             xr[h, 1] = turn_x(grouped, 1, 4 + h, f"x_by_row{h}1")
             xrq[h, 1] = quantize(xr[h, 1], E4M3, f"xr{h}1")
 
-        windows = [window0, window1, window2]
         out_rows = out.rearrange("(p j) n -> p j n", j=PACK)
         for j in range(PACK):
-            dw = bank((1, 2, 3, 6)[j], "dw")
+            dw = bank((0, 1, 2, 6)[j], "dw")
             for h in range(HALVES):
                 product(dw, xrq[h, j // 2], E4M3, j % 2, daq[h], E5M2, h == 0, h == HALVES - 1)
             dw_sb = sbuf([SLOTS], F32, f"dw_sb{j}")

@@ -72,9 +72,9 @@ def tile_attend_gffn_sil_kernel(
         x_raw = [load_half(x_rows, 0, "x_raw0")]
         s1_table = load_scales(w1_scales, "s1_table")
         w1_table = load_words(w1_words, "w1_table")
-        s2_table = load_scales(w2_scales, "s2_table")
         us_col = load_column(us, "us_col")
         wt_col = load_column(wt, "wt_col")
+        s2_table = load_scales(w2_scales, "s2_table")
         dy_raw = [load_half(dy_rows, 0, "dy_raw0")]
         w2_table = load_words(w2_words, "w2_table")
         x_raw.append(load_half(x_rows, 1, "x_raw1"))
@@ -132,35 +132,55 @@ def tile_attend_gffn_sil_kernel(
         def scaled_first_product(xq, w1, h, z, t):
             a = bank(t, "a")
             product(a, xq[t // 2], E4M3, t % 2, w1, E4M3)
-            nc.vector.scalar_tensor_tensor(z[:, t, :], a[:], us_col[:, h, t : t + 1], ts_all[:], ALU.mult, ALU.mult)
+            nc.vector.scalar_tensor_tensor(z[t // 2][:, t % 2, :], a[:], us_col[:, h, t : t + 1], ts_all[:], ALU.mult, ALU.mult)
+
+        def turned_first_product(xq, w1):
+            sums = [bank(4 + g, "a_by_slot") for g in range(4)]
+            for g in range(4):
+                product(sums[g], w1, E4M3, g, xq, E4M3)
+            by_row = [bank(t, "a_by_row") for t in range(PACK)]
+            for g in range(4):
+                scaled = sbuf([K_PASS], F32, f"a_scaled{g}")
+                nc.scalar.activation(scaled[:], sums[g][:], ACT.Copy, scale=ts_col[:, g : g + 1])
+                for t in range(PACK):
+                    nc.tensor.transpose(by_row[t][:, g * P : (g + 1) * P], scaled[:, t * P : (t + 1) * P], ident[:])
+            acts = sbuf([2, PACK, SLOTS], F32, "acts0")
+            sl, th = acts[:, 0], acts[:, 1]
+            for t in range(PACK):
+                nc.scalar.activation(sl[:, t, :], by_row[t][:], ACT.Silu, scale=minus_us[:, t : t + 1])
+            for t in range(PACK):
+                nc.scalar.activation(th[:, t, :], by_row[t][:], ACT.Tanh, scale=half_us[:, t : t + 1])
+            return sl, th
 
         def activations(z, h):
-            acts = sbuf([2, PACK, SLOTS], F32, f"acts{h}", ("dy_raw0", "acts1")[h])
+            acts = sbuf([2, PACK, SLOTS], F32, f"acts{h}", f"dy_raw{h}")
             sl, th = acts[:, 0], acts[:, 1]
             for pair in range(2):
                 rows = slice(2 * pair, 2 * pair + 2)
-                nc.scalar.activation(sl[:, rows, :], z[:, rows, :], ACT.Silu, scale=-1.0)
+                nc.scalar.activation(sl[:, rows, :], z[pair][:], ACT.Silu, scale=-1.0)
             for pair in range(2):
                 rows = slice(2 * pair, 2 * pair + 2)
-                nc.scalar.activation(th[:, rows, :], z[:, rows, :], ACT.Tanh, scale=0.5)
+                nc.scalar.activation(th[:, rows, :], z[pair][:], ACT.Tanh, scale=0.5)
             return sl, th
 
         def times_dh(sl, dyq, w2, h):
-            m = sbuf([PACK, SLOTS], F32, f"m{h}", "m")
+            m = sbuf([PACK, SLOTS], F32, f"m{h}")
             for t in range(PACK):
                 dh = bank(4 + t, "dh")
                 product(dh, dyq[t // 2], E5M2, t % 2, w2, E4M3)
                 nc.vector.scalar_tensor_tensor(m[:, t, :], sl[:, t, :], 1.0, dh[:], ALU.subtract, ALU.mult)
             return m
 
-        def times_sigmoid(th, m, n, pair):
-            rows = slice(2 * pair, 2 * pair + 2)
-            nc.vector.scalar_tensor_tensor(n[:, rows, :], th[:, rows, :], 1.0, m[:, rows, :], ALU.add, ALU.mult)
+        def times_sigmoid(th, m, h):
+            n = sbuf([PACK, SLOTS], F32, f"n{h}")
+            for pair in range(2):
+                rows = slice(2 * pair, 2 * pair + 2)
+                nc.vector.scalar_tensor_tensor(n[:, rows, :], th[:, rows, :], 1.0, m[:, rows, :], ALU.add, ALU.mult)
+            return n
 
-        def finish(n, h, da, part):
-            cols = slice(part * 256, (part + 1) * 256)
-            nc.vector.tensor_tensor(
-                da[:, PACK * cols.start : PACK * cols.stop].rearrange("p (c i t) -> p c t i", i=4, t=PACK),
+        def finish(engine, n, h, grouped, cols):
+            engine.tensor_tensor(
+                grouped.rearrange("p (c i t) -> p c t i", i=4, t=PACK),
                 n[:, :, cols].rearrange("p t (c i) -> p c t i", i=4),
                 factors[h][:, :, cols].rearrange("p t (c i) -> p c t i", i=4),
                 ALU.mult,
@@ -168,19 +188,20 @@ def tile_attend_gffn_sil_kernel(
 
         ts_row = gather(ts_table[:], F32, "ts_row")
         xg0 = [group(x_raw[0], 0, "x_grouped00")]
-        turned = bank(6, "turned")
+        turned = bank(0, "turned")
         for b in range(4):
             nc.tensor.transpose(turned[:, b * P : (b + 1) * P], ts_row[:, b * P : (b + 1) * P], ident[:])
         ts_col = sbuf([4], F32, "ts_col")
         nc.scalar.copy(ts_col[:], turned[:, 0::P])
         xg0.append(group(x_raw[0], 1, "x_grouped01"))
-        spread = bank(7, "spread")
+        spread = bank(1, "spread")
         for b in range(4):
             nc.tensor.transpose(spread[:, b * P : (b + 1) * P], ts_col[:, b : b + 1].to_broadcast([P, P]), ident[:])
         ts_all = sbuf([SLOTS], F32, "ts_all")
         nc.scalar.copy(ts_all[:], spread[:])
 
         wu = sbuf([HALVES, PACK], F32, "wu")
+        nc.vector.scalar_tensor_tensor(wu[:], us_col, -0.5, wt_col, ALU.mult, ALU.mult)
         factors = []
 
         def outer_product(h, tag):
@@ -188,74 +209,75 @@ def tile_attend_gffn_sil_kernel(
             for t in range(PACK):
                 nc.gpsimd.tensor_scalar(factors[h][:, t, :], ts_all[:], wu[:, h, t : t + 1], 0.0, ALU.mult, ALU.add)
 
-        def cleared_window(name, tag):
-            window = sbuf([UNITS], F32, name, tag)
-            nc.gpsimd.memset(window[:], 0.0)
-            return window
-
         s1 = gather(s1_table[:].bitcast(U8), U8, "s1", "ts_table")
-        xq0 = [quantize(xg0[0], E4M3, "x00", "s1_table")]
-        xq0.append(quantize(xg0[1], E4M3, "x01", "ts_row"))
+        xq0 = (sbuf([K_PASS], U32, "x0_codes", "s1_table"), sbuf([K_PASS], U8, "x0_scales"))
+        for pair in range(2):
+            cols = slice(pair * 256, (pair + 1) * 256)
+            nc.vector.quantize_mx(out=xq0[0][:, cols].bitcast(E4M3), scales=xq0[1][:, cols], in_=xg0[pair][:])
         w1 = (gather(w1_table[:].bitcast(U32), U32, "w1"), s1)
         s2 = gather(s2_table[:].bitcast(U8), U8, "s2")
-        half_us = sbuf([HALVES, PACK], F32, "half_us")
-        nc.gpsimd.tensor_scalar(half_us[:], us_col, -0.5, 0.0, ALU.mult, ALU.add)
-        nc.gpsimd.tensor_tensor(wu[:], half_us[:], wt_col, ALU.mult)
-        xr = {(0, 0): turn_x(xg0, 0, 6, "x_by_row00")}
-        outer_product(0, "w1_table")
-        dyg0 = [group(dy_raw[0], 0, "dy_grouped00")]
-        z0 = sbuf([PACK, SLOTS], F32, "z0", "s2_table")
-        for t in range(PACK):
-            scaled_first_product(xq0, w1, 0, z0, t)
-        dyg0.append(group(dy_raw[0], 1, "dy_grouped01", nc.vector.tensor_copy))
-        sl0, th0 = activations(z0, 0)
+        minus_us = sbuf([PACK], F32, "minus_us")
+        half_us = sbuf([PACK], F32, "half_us")
+        nc.vector.tensor_scalar(minus_us[:], us_col[:, 0, :], -1.0, 0.0, ALU.mult, ALU.add)
+        nc.vector.tensor_scalar(half_us[:], us_col[:, 0, :], 0.5, 0.0, ALU.mult, ALU.add)
+        outer_product(0, None)
+        xr = {(0, 0): turn_x(xg0, 0, 0, "x_by_row00")}
+        sl0, th0 = turned_first_product(xq0, w1)
+        dyg0 = [group(dy_raw[0], pair, f"dy_grouped0{pair}", nc.vector.tensor_copy) for pair in range(2)]
         dyq0 = [quantize(dyg0[pair], E5M2, f"dy0{pair}") for pair in range(2)]
+        outer_product(1, "dy_grouped01")
         w2 = (gather(w2_table[:].bitcast(U32), U32, "w2"), s2)
-        xrq = {(0, 0): quantize(xr[0, 0], E4M3, "xr00", "w2_table")}
-        outer_product(1, "x_by_row00")
-        windows = [cleared_window("window0", "dy01_codes")]
         m0 = times_dh(sl0, dyq0, w2, 0)
+        window1 = sbuf([UNITS], F32, "window1", "dy01_codes")
+        nc.gpsimd.memset(window1[:], 0.0)
         xg1 = [group(x_raw[1], pair, f"x_grouped1{pair}") for pair in range(2)]
         dyg1 = [group(dy_raw[1], pair, f"dy_grouped1{pair}") for pair in range(2)]
-        n0 = sbuf([PACK, SLOTS], F32, "n0")
-        for pair in range(2):
-            times_sigmoid(th0, m0, n0, pair)
-        xq1 = [quantize(xg1[pair], E4M3, f"x1{pair}") for pair in range(2)]
-        da0 = sbuf([PACK * SLOTS], BF16, "da0")
-        finish(n0, 0, da0, 0)
-        z1 = sbuf([PACK, SLOTS], F32, "z1", "s2_table")
-        for t in range(PACK):
-            scaled_first_product(xq1, w1, 1, z1, t)
-        windows.append(cleared_window("window1", "x10_codes"))
+        n0 = times_sigmoid(th0, m0, 0)
+        xq1 = [quantize(xg1[0], E4M3, "x10")]
+        xq1.append(quantize(xg1[1], E4M3, "x11"))
+        xrq = {(0, 0): quantize(xr[0, 0], E4M3, "xr00", "m0")}
+        z1 = [sbuf([2, SLOTS], F32, f"z1{pair}") for pair in range(2)]
+        parts = [slice(0, SLOTS // 2), slice(SLOTS // 2, SLOTS)]
+
+        def quantize_da(da, h, tag=None):
+            codes = sbuf([SLOTS], U32, f"da{h}_codes", tag)
+            scales = sbuf([SLOTS], U8, f"da{h}_scales")
+            for grouped, cols in da:
+                nc.vector.quantize_mx(out=codes[:, cols].bitcast(E5M2), scales=scales[:, cols], in_=grouped[:])
+            return codes, scales
+
+        def finish_part(engine, n, h, cols, tag=None):
+            grouped = sbuf([PACK * (cols.stop - cols.start)], BF16, f"da{h}_{cols.start}", tag)
+            finish(engine, n, h, grouped[:], cols)
+            return grouped, cols
+
+        da0 = [finish_part(nc.gpsimd, n0, 0, slice(0, 128), "x10_codes")]
+        dyq1 = []
+        for pair, cols in enumerate((slice(128, 256), parts[1])):
+            for t in (2 * pair, 2 * pair + 1):
+                scaled_first_product(xq1, w1, 1, z1, t)
+            dyq1.append(quantize(dyg1[pair], E5M2, f"dy1{pair}"))
+            da0.append(finish_part(nc.gpsimd, n0, 0, cols, f"dy_grouped1{pair}"))
         sl1, th1 = activations(z1, 1)
-        dyq1 = [quantize(dyg1[pair], E5M2, f"dy1{pair}") for pair in range(2)]
-        finish(n0, 0, da0, 1)
-        daq = [quantize(da0, E5M2, "da0")]
-        windows.append(cleared_window("window2", "da0"))
-        xr[1, 0] = turn_x(xg1, 0, 3, "x_by_row10")
         m1 = times_dh(sl1, dyq1, w2, 1)
-        n1 = sbuf([PACK, SLOTS], F32, "n1")
-        for pair in range(2):
-            times_sigmoid(th1, m1, n1, pair)
+        xr[1, 0] = turn_x(xg1, 0, 4, "x_by_row10")
+        window2 = sbuf([UNITS], F32, "window2", "dy11_codes")
+        nc.gpsimd.memset(window2[:], 0.0)
+        n1 = times_sigmoid(th1, m1, 1)
+        daq = [quantize_da(da0, 0, "z10")]
         xrq[1, 0] = quantize(xr[1, 0], E4M3, "xr10")
-        da1 = sbuf([PACK * SLOTS], BF16, "da1")
-        codes1 = sbuf([SLOTS], U32, "da1_codes")
-        scales1 = sbuf([SLOTS], U8, "da1_scales")
-        for part in range(2):
-            finish(n1, 1, da1, part)
-        for part in range(2):
-            cols = slice(part * 256, (part + 1) * 256)
-            nc.vector.quantize_mx(
-                out=codes1[:, cols].bitcast(E5M2), scales=scales1[:, cols], in_=da1[:, part * 1024 : (part + 1) * 1024]
-            )
-        daq.append((codes1, scales1))
+        window0 = sbuf([UNITS], F32, "window0", "x_by_row10")
+        nc.gpsimd.memset(window0[:], 0.0)
+        da1 = [finish_part(nc.vector, n1, 1, cols) for cols in parts]
+        daq.append(quantize_da(da1, 1))
         for h, grouped in enumerate((xg0, xg1)):
-            xr[h, 1] = turn_x(grouped, 1, 4 + h, f"x_by_row{h}1")
+            xr[h, 1] = turn_x(grouped, 1, 5 + h, f"x_by_row{h}1")
             xrq[h, 1] = quantize(xr[h, 1], E4M3, f"xr{h}1")
 
+        windows = [window1, window2, window0]
         out_rows = out.rearrange("(p j) n -> p j n", j=PACK)
         for j in range(PACK):
-            dw = bank((0, 1, 2, 6)[j], "dw")
+            dw = bank(j, "dw")
             for h in range(HALVES):
                 product(dw, xrq[h, j // 2], E4M3, j % 2, daq[h], E5M2, h == 0, h == HALVES - 1)
             dw_sb = sbuf([SLOTS], F32, f"dw_sb{j}")

@@ -220,12 +220,11 @@ def tile_attend_gffn_sil_kernel(
         half_us = sbuf([PACK], F32, "half_us")
         nc.vector.tensor_scalar(minus_us[:], us_col[:, 0, :], -1.0, 0.0, ALU.mult, ALU.add)
         nc.vector.tensor_scalar(half_us[:], us_col[:, 0, :], 0.5, 0.0, ALU.mult, ALU.add)
-        outer_product(0, None)
         xr = {(0, 0): turn_x(xg0, 0, 0, "x_by_row00")}
         sl0, th0 = turned_first_product(xq0, w1)
         dyg0 = [group(dy_raw[0], pair, f"dy_grouped0{pair}", nc.vector.tensor_copy) for pair in range(2)]
         dyq0 = [quantize(dyg0[pair], E5M2, f"dy0{pair}") for pair in range(2)]
-        outer_product(1, "dy_grouped01")
+        outer_product(0, "dy_grouped01")
         w2 = (gather(w2_table[:].bitcast(U32), U32, "w2"), s2)
         m0 = times_dh(sl0, dyq0, w2, 0)
         window1 = sbuf([UNITS], F32, "window1", "dy01_codes")
@@ -251,27 +250,28 @@ def tile_attend_gffn_sil_kernel(
             finish(engine, n, h, grouped[:], cols)
             return grouped, cols
 
-        da0 = [finish_part(nc.gpsimd, n0, 0, slice(0, 128), "x10_codes")]
-        dyq1 = []
-        for pair, cols in enumerate((slice(128, 256), parts[1])):
-            for t in (2 * pair, 2 * pair + 1):
-                scaled_first_product(xq1, w1, 1, z1, t)
-            dyq1.append(quantize(dyg1[pair], E5M2, f"dy1{pair}"))
-            da0.append(finish_part(nc.gpsimd, n0, 0, cols, f"dy_grouped1{pair}"))
+        for t in range(PACK):
+            scaled_first_product(xq1, w1, 1, z1, t)
+        da0 = [finish_part(nc.gpsimd, n0, 0, parts[0], "x10_codes")]
         sl1, th1 = activations(z1, 1)
+        dyq1 = [quantize(dyg1[pair], E5M2, f"dy1{pair}") for pair in range(2)]
+        da0.append(finish_part(nc.gpsimd, n0, 0, parts[1], "dy_grouped11"))
         m1 = times_dh(sl1, dyq1, w2, 1)
-        xr[1, 0] = turn_x(xg1, 0, 4, "x_by_row10")
+        factors.append(sbuf([PACK, SLOTS], F32, "factors1", "z10"))
+        for t in range(PACK):
+            nc.scalar.activation(factors[1][:, t, :], ts_all[:], ACT.Copy, scale=wu[:, 1, t : t + 1])
+        xr[1, 0] = turn_x(xg1, 0, 7, "x_by_row10")
         window2 = sbuf([UNITS], F32, "window2", "dy11_codes")
         nc.gpsimd.memset(window2[:], 0.0)
         n1 = times_sigmoid(th1, m1, 1)
-        daq = [quantize_da(da0, 0, "z10")]
-        xrq[1, 0] = quantize(xr[1, 0], E4M3, "xr10")
-        window0 = sbuf([UNITS], F32, "window0", "x_by_row10")
+        daq = [quantize_da(da0, 0, "z11")]
+        window0 = sbuf([UNITS], F32, "window0", "dy_grouped11")
         nc.gpsimd.memset(window0[:], 0.0)
         da1 = [finish_part(nc.vector, n1, 1, cols) for cols in parts]
+        xrq[1, 0] = quantize(xr[1, 0], E4M3, "xr10")
         daq.append(quantize_da(da1, 1))
         for h, grouped in enumerate((xg0, xg1)):
-            xr[h, 1] = turn_x(grouped, 1, 5 + h, f"x_by_row{h}1")
+            xr[h, 1] = turn_x(grouped, 1, 7 - h, f"x_by_row{h}1")
             xrq[h, 1] = quantize(xr[h, 1], E4M3, f"xr{h}1")
 
         windows = [window1, window2, window0]

@@ -84,6 +84,8 @@ def tile_attend_gffn_sil_kernel(
         nc.scalar.activation(warm[:, 1:2], warm[:, 0:1], ACT.Silu)
         ident = sbuf([P], F32, "ident")
         make_identity(nc, ident[:])
+        window2 = sbuf([UNITS], F32, "window2")
+        nc.vector.memset(window2[:], 0.0)
 
         def gather(table, dtype, name, tag=None):
             picked = sbuf([SLOTS], dtype, name, tag)
@@ -153,8 +155,8 @@ def tile_attend_gffn_sil_kernel(
             return sl, th
 
         def activations(z, h):
-            acts = sbuf([2, PACK, SLOTS], F32, f"acts{h}", f"dy_raw{h}")
-            sl, th = acts[:, 0], acts[:, 1]
+            sl = sbuf([PACK, SLOTS], F32, f"silu{h}", f"dy_raw{h}")
+            th = sbuf([PACK, SLOTS], F32, f"tanh{h}", "us_col")
             for pair in range(2):
                 rows = slice(2 * pair, 2 * pair + 2)
                 nc.scalar.activation(sl[:, rows, :], z[pair][:], ACT.Silu, scale=-1.0)
@@ -204,10 +206,6 @@ def tile_attend_gffn_sil_kernel(
         nc.vector.scalar_tensor_tensor(wu[:], us_col, -0.5, wt_col, ALU.mult, ALU.mult)
         factors = []
 
-        def outer_product(h, tag):
-            factors.append(sbuf([PACK, SLOTS], F32, f"factors{h}", tag))
-            for t in range(PACK):
-                nc.gpsimd.tensor_scalar(factors[h][:, t, :], ts_all[:], wu[:, h, t : t + 1], 0.0, ALU.mult, ALU.add)
 
         s1 = gather(s1_table[:].bitcast(U8), U8, "s1", "ts_table")
         xq0 = (sbuf([K_PASS], U32, "x0_codes", "s1_table"), sbuf([K_PASS], U8, "x0_scales"))
@@ -224,18 +222,16 @@ def tile_attend_gffn_sil_kernel(
         sl0, th0 = turned_first_product(xq0, w1)
         dyg0 = [group(dy_raw[0], pair, f"dy_grouped0{pair}", nc.vector.tensor_copy) for pair in range(2)]
         dyq0 = [quantize(dyg0[pair], E5M2, f"dy0{pair}") for pair in range(2)]
-        outer_product(0, "dy_grouped01")
         w2 = (gather(w2_table[:].bitcast(U32), U32, "w2"), s2)
+        factors.append(sbuf([PACK, SLOTS], F32, "factors0", "w2_table"))
+        for t in range(PACK):
+            nc.vector.tensor_scalar(factors[0][:, t, :], ts_all[:], wu[:, 0, t : t + 1], None, ALU.mult)
         m0 = times_dh(sl0, dyq0, w2, 0)
         window1 = sbuf([UNITS], F32, "window1", "dy01_codes")
         nc.gpsimd.memset(window1[:], 0.0)
         xg1 = [group(x_raw[1], pair, f"x_grouped1{pair}") for pair in range(2)]
         dyg1 = [group(dy_raw[1], pair, f"dy_grouped1{pair}") for pair in range(2)]
         n0 = times_sigmoid(th0, m0, 0)
-        xq1 = [quantize(xg1[0], E4M3, "x10")]
-        xq1.append(quantize(xg1[1], E4M3, "x11"))
-        xrq = {(0, 0): quantize(xr[0, 0], E4M3, "xr00", "m0")}
-        z1 = [sbuf([2, SLOTS], F32, f"z1{pair}") for pair in range(2)]
         parts = [slice(0, SLOTS // 2), slice(SLOTS // 2, SLOTS)]
 
         def quantize_da(da, h, tag=None):
@@ -250,19 +246,23 @@ def tile_attend_gffn_sil_kernel(
             finish(engine, n, h, grouped[:], cols)
             return grouped, cols
 
+        xq1 = [quantize(xg1[0], E4M3, "x10")]
+        da0 = [finish_part(nc.vector, n0, 0, slice(0, 128))]
+        xq1.append(quantize(xg1[1], E4M3, "x11"))
+        xrq = {(0, 0): quantize(xr[0, 0], E4M3, "xr00", "m0")}
+        z1 = [sbuf([2, SLOTS], F32, f"z1{pair}") for pair in range(2)]
         for t in range(PACK):
             scaled_first_product(xq1, w1, 1, z1, t)
-        da0 = [finish_part(nc.gpsimd, n0, 0, parts[0], "x10_codes")]
+        da0.append(finish_part(nc.gpsimd, n0, 0, slice(128, 256), "x10_codes"))
         sl1, th1 = activations(z1, 1)
         dyq1 = [quantize(dyg1[pair], E5M2, f"dy1{pair}") for pair in range(2)]
-        da0.append(finish_part(nc.gpsimd, n0, 0, parts[1], "dy_grouped11"))
+        da0.append(finish_part(nc.vector, n0, 0, slice(256, 384), "dy_grouped10"))
+        da0.append(finish_part(nc.gpsimd, n0, 0, slice(384, SLOTS), "dy_grouped11"))
         m1 = times_dh(sl1, dyq1, w2, 1)
         factors.append(sbuf([PACK, SLOTS], F32, "factors1", "z10"))
         for t in range(PACK):
             nc.scalar.activation(factors[1][:, t, :], ts_all[:], ACT.Copy, scale=wu[:, 1, t : t + 1])
         xr[1, 0] = turn_x(xg1, 0, 7, "x_by_row10")
-        window2 = sbuf([UNITS], F32, "window2", "dy11_codes")
-        nc.gpsimd.memset(window2[:], 0.0)
         n1 = times_sigmoid(th1, m1, 1)
         daq = [quantize_da(da0, 0, "z11")]
         window0 = sbuf([UNITS], F32, "window0", "dy_grouped11")

@@ -107,14 +107,17 @@ def tile_attend_gffn_sil_kernel(
             nc.vector.quantize_mx(out=codes[:].bitcast(fmt), scales=scales[:], in_=grouped[:])
             return codes, scales
 
+        def whole(operand):
+            return operand[0][:], operand[1][:]
+
         def product(acc, lhs, fmt_l, k, rhs, fmt_r, start=True, stop=True):
             cols = slice(k * P, (k + 1) * P)
             nc.tensor.matmul_mx(
                 out=acc[:],
                 lhsT=lhs[0][:, cols].bitcast(fmt_l),
                 lhsT_scale=lhs[1][:, cols],
-                rhs=rhs[0][:].bitcast(fmt_r),
-                rhs_scale=rhs[1][:],
+                rhs=rhs[0].bitcast(fmt_r),
+                rhs_scale=rhs[1],
                 start=start,
                 stop=stop,
             )
@@ -133,25 +136,30 @@ def tile_attend_gffn_sil_kernel(
 
         def scaled_first_product(xq, w1, h, z, t):
             a = bank(t, "a")
-            product(a, xq[t // 2], E4M3, t % 2, w1, E4M3)
+            product(a, xq[t // 2], E4M3, t % 2, whole(w1), E4M3)
             nc.vector.scalar_tensor_tensor(z[t // 2][:, t % 2, :], a[:], us_col[:, h, t : t + 1], ts_all[:], ALU.mult, ALU.mult)
 
         def turned_first_product(xq, w1):
             sums = [bank(4 + g, "a_by_slot") for g in range(4)]
             for g in range(4):
-                product(sums[g], w1, E4M3, g, xq, E4M3)
-            by_row = [bank(t, "a_by_row") for t in range(PACK)]
+                product(sums[g], w1, E4M3, g, whole(xq), E4M3)
+            by_row = [bank(b, "a_by_row") for b in range(4)]
+
+            def turned_sums(t, half):
+                return by_row[2 * half + t // 2][:, 256 * (t % 2) : 256 * (t % 2 + 1)]
+
             for g in range(4):
                 scaled = sbuf([K_PASS], F32, f"a_scaled{g}")
                 nc.scalar.activation(scaled[:], sums[g][:], ACT.Copy, scale=ts_col[:, g : g + 1])
                 for t in range(PACK):
-                    nc.tensor.transpose(by_row[t][:, g * P : (g + 1) * P], scaled[:, t * P : (t + 1) * P], ident[:])
+                    nc.tensor.transpose(turned_sums(t, g // 2)[:, g % 2 * P : (g % 2 + 1) * P], scaled[:, t * P : (t + 1) * P], ident[:])
             acts = sbuf([2, PACK, SLOTS], F32, "acts0")
             sl, th = acts[:, 0], acts[:, 1]
-            for t in range(PACK):
-                nc.scalar.activation(sl[:, t, :], by_row[t][:], ACT.Silu, scale=minus_us[:, t : t + 1])
-            for t in range(PACK):
-                nc.scalar.activation(th[:, t, :], by_row[t][:], ACT.Tanh, scale=half_us[:, t : t + 1])
+            for values, func, scale in ((sl, ACT.Silu, minus_us), (th, ACT.Tanh, half_us)):
+                for half in range(2):
+                    for t in range(PACK):
+                        cols = slice(256 * half, 256 * (half + 1))
+                        nc.scalar.activation(values[:, t, cols], turned_sums(t, half), func, scale=scale[:, t : t + 1])
             return sl, th
 
         def activations(z, h):
@@ -169,7 +177,7 @@ def tile_attend_gffn_sil_kernel(
             m = sbuf([PACK, SLOTS], F32, f"m{h}")
             for t in range(PACK):
                 dh = bank(4 + t, "dh")
-                product(dh, dyq[t // 2], E5M2, t % 2, w2, E4M3)
+                product(dh, dyq[t // 2], E5M2, t % 2, whole(w2), E4M3)
                 nc.vector.scalar_tensor_tensor(m[:, t, :], sl[:, t, :], 1.0, dh[:], ALU.subtract, ALU.mult)
             return m
 
@@ -212,7 +220,10 @@ def tile_attend_gffn_sil_kernel(
         for pair in range(2):
             cols = slice(pair * 256, (pair + 1) * 256)
             nc.vector.quantize_mx(out=xq0[0][:, cols].bitcast(E4M3), scales=xq0[1][:, cols], in_=xg0[pair][:])
-        w1 = (gather(w1_table[:].bitcast(U32), U32, "w1"), s1)
+        w1 = (sbuf([SLOTS], U32, "w1"), s1)
+        for half in range(2):
+            listed = offsets[:, 16 * half : 16 * (half + 1)]
+            nc.vector.tensor_copy(w1[0][:, 256 * half : 256 * (half + 1)], w1_table[:].bitcast(U32).indirect(listed))
         s2 = gather(s2_table[:].bitcast(U8), U8, "s2")
         minus_us = sbuf([PACK], F32, "minus_us")
         half_us = sbuf([PACK], F32, "half_us")
@@ -230,16 +241,23 @@ def tile_attend_gffn_sil_kernel(
         window1 = sbuf([UNITS], F32, "window1", "dy01_codes")
         nc.gpsimd.memset(window1[:], 0.0)
         xg1 = [group(x_raw[1], pair, f"x_grouped1{pair}") for pair in range(2)]
+        xr[1, 0] = turn_x(xg1, 0, 7, "x_by_row10")
         dyg1 = [group(dy_raw[1], pair, f"dy_grouped1{pair}") for pair in range(2)]
         n0 = times_sigmoid(th0, m0, 0)
         parts = [slice(0, SLOTS // 2), slice(SLOTS // 2, SLOTS)]
 
-        def quantize_da(da, h, tag=None):
-            codes = sbuf([SLOTS], U32, f"da{h}_codes", tag)
-            scales = sbuf([SLOTS], U8, f"da{h}_scales")
-            for grouped, cols in da:
-                nc.vector.quantize_mx(out=codes[:, cols].bitcast(E5M2), scales=scales[:, cols], in_=grouped[:])
-            return codes, scales
+        da_codes = sbuf([5 * 256], U32, "da_codes")
+        da_scales = sbuf([5 * 256], U8, "da_scales")
+        first = (0, 768)
+        again = 512
+
+        def quantize_da(part, start):
+            grouped, cols = part
+            place = slice(start + cols.start, start + cols.stop)
+            nc.vector.quantize_mx(out=da_codes[:, place].bitcast(E5M2), scales=da_scales[:, place], in_=grouped[:])
+
+        def da_operand(start):
+            return da_codes[:, start : start + SLOTS], da_scales[:, start : start + SLOTS]
 
         def finish_part(engine, n, h, cols, tag=None):
             grouped = sbuf([PACK * (cols.stop - cols.start)], BF16, f"da{h}_{cols.start}", tag)
@@ -257,31 +275,51 @@ def tile_attend_gffn_sil_kernel(
         sl1, th1 = activations(z1, 1)
         dyq1 = [quantize(dyg1[pair], E5M2, f"dy1{pair}") for pair in range(2)]
         da0.append(finish_part(nc.vector, n0, 0, slice(256, 384), "dy_grouped10"))
+        for part in da0[:2]:
+            quantize_da(part, first[0])
+            quantize_da(part, again)
         da0.append(finish_part(nc.gpsimd, n0, 0, slice(384, SLOTS), "dy_grouped11"))
         m1 = times_dh(sl1, dyq1, w2, 1)
         factors.append(sbuf([PACK, SLOTS], F32, "factors1", "z10"))
-        for t in range(PACK):
-            nc.scalar.activation(factors[1][:, t, :], ts_all[:], ACT.Copy, scale=wu[:, 1, t : t + 1])
-        xr[1, 0] = turn_x(xg1, 0, 7, "x_by_row10")
-        n1 = times_sigmoid(th1, m1, 1)
-        daq = [quantize_da(da0, 0, "z11")]
-        window0 = sbuf([UNITS], F32, "window0", "dy_grouped11")
+        for cols in parts:
+            for t in range(PACK):
+                nc.scalar.activation(factors[1][:, t, cols], ts_all[:, cols], ACT.Copy, scale=wu[:, 1, t : t + 1])
+        window0 = sbuf([UNITS], F32, "window0", "dy11_codes")
         nc.gpsimd.memset(window0[:], 0.0)
-        da1 = [finish_part(nc.vector, n1, 1, cols) for cols in parts]
-        xrq[1, 0] = quantize(xr[1, 0], E4M3, "xr10")
-        daq.append(quantize_da(da1, 1))
+        n1 = times_sigmoid(th1, m1, 1)
+        for part in da0[2:]:
+            quantize_da(part, first[0])
         for h, grouped in enumerate((xg0, xg1)):
-            xr[h, 1] = turn_x(grouped, 1, 7 - h, f"x_by_row{h}1")
-            xrq[h, 1] = quantize(xr[h, 1], E4M3, f"xr{h}1")
+            xr[h, 1] = turn_x(grouped, 1, 4 + h, f"x_by_row{h}1")
+        da1 = [finish_part(nc.vector, n1, 1, parts[0])]
+        xrq[1, 0] = quantize(xr[1, 0], E4M3, "xr10", "dy_grouped11")
+        quantize_da(da1[0], first[1])
 
-        windows = [window1, window2, window0]
-        out_rows = out.rearrange("(p j) n -> p j n", j=PACK)
-        for j in range(PACK):
-            dw = bank(j, "dw")
+        def output_sums(j, n, starts, cols, name):
+            dw = bank(n, name)
             for h in range(HALVES):
-                product(dw, xrq[h, j // 2], E4M3, j % 2, daq[h], E5M2, h == 0, h == HALVES - 1)
-            dw_sb = sbuf([SLOTS], F32, f"dw_sb{j}")
-            nc.scalar.copy(dw_sb[:], dw[:])
-            window = windows[j % 3]
-            nc.vector.tensor_copy(window[:].indirect(offsets[:]), dw_sb[:])
+                product(dw, xrq[h, j // 2], E4M3, j % 2, da_operand(starts[h]), E5M2, h == 0, h == HALVES - 1)
+            sums = sbuf([cols.stop - cols.start], F32, name + "_sb")
+            nc.scalar.copy(sums[:], dw[:, cols])
+            return sums
+
+        def scatter(window, sums, cols):
+            nc.vector.tensor_copy(window[:].indirect(offsets[:, cols.start // 16 : cols.stop // 16]), sums[:])
+
+        early = output_sums(0, 0, (256, again), parts[1], "dw0_early")
+        da1.append(finish_part(nc.vector, n1, 1, parts[1]))
+        xrq[1, 1] = quantize(xr[1, 1], E4M3, "xr11")
+        quantize_da(da1[1], first[1])
+        xrq[0, 1] = quantize(xr[0, 1], E4M3, "xr01", "n1")
+        every = slice(0, SLOTS)
+        sums1 = output_sums(1, 1, first, every, "dw1")
+        late = output_sums(0, 2, first, parts[1], "dw0_late")
+        out_rows = out.rearrange("(p j) n -> p j n", j=PACK)
+        scatter(window1, early, parts[0])
+        scatter(window2, sums1, every)
+        nc.sync.dma_start(out_rows[:, 1, :], window2[:])
+        scatter(window1, late, parts[1])
+        nc.sync.dma_start(out_rows[:, 0, :], window1[:])
+        for j, n, window in ((2, 3, window0), (3, 6, window2)):
+            scatter(window, output_sums(j, n, first, every, f"dw{j}"), every)
             nc.sync.dma_start(out_rows[:, j, :], window[:])

@@ -248,8 +248,7 @@ def tile_attend_gffn_sil_kernel(
 
         da_codes = sbuf([5 * 256], U32, "da_codes")
         da_scales = sbuf([5 * 256], U8, "da_scales")
-        first = (0, 768)
-        again = 512
+        first = (256, 768)
 
         def quantize_da(part, start):
             grouped, cols = part
@@ -273,18 +272,18 @@ def tile_attend_gffn_sil_kernel(
             scaled_first_product(xq1, w1, 1, z1, t)
         da0.append(finish_part(nc.gpsimd, n0, 0, slice(128, 256), "x10_codes"))
         sl1, th1 = activations(z1, 1)
-        dyq1 = [quantize(dyg1[pair], E5M2, f"dy1{pair}") for pair in range(2)]
+        dyq1 = [quantize(dyg1[0], E5M2, "dy10"), (da_codes[:, 0:256], da_scales[:, 0:256])]
+        nc.vector.quantize_mx(out=dyq1[1][0].bitcast(E5M2), scales=dyq1[1][1], in_=dyg1[1][:])
         da0.append(finish_part(nc.vector, n0, 0, slice(256, 384), "dy_grouped10"))
         for part in da0[:2]:
             quantize_da(part, first[0])
-            quantize_da(part, again)
         da0.append(finish_part(nc.gpsimd, n0, 0, slice(384, SLOTS), "dy_grouped11"))
         m1 = times_dh(sl1, dyq1, w2, 1)
         factors.append(sbuf([PACK, SLOTS], F32, "factors1", "z10"))
         for cols in parts:
             for t in range(PACK):
                 nc.scalar.activation(factors[1][:, t, cols], ts_all[:, cols], ACT.Copy, scale=wu[:, 1, t : t + 1])
-        window0 = sbuf([UNITS], F32, "window0", "dy11_codes")
+        window0 = sbuf([UNITS], F32, "window0", "dy10_codes")
         nc.gpsimd.memset(window0[:], 0.0)
         n1 = times_sigmoid(th1, m1, 1)
         for part in da0[2:]:
@@ -306,7 +305,7 @@ def tile_attend_gffn_sil_kernel(
         def scatter(window, sums, cols):
             nc.vector.tensor_copy(window[:].indirect(offsets[:, cols.start // 16 : cols.stop // 16]), sums[:])
 
-        early = output_sums(0, 0, (256, again), parts[1], "dw0_early")
+        early = output_sums(0, 0, (first[0] - 256, first[1] - 256), parts[1], "dw0_early")
         da1.append(finish_part(nc.vector, n1, 1, parts[1]))
         xrq[1, 1] = quantize(xr[1, 1], E4M3, "xr11")
         quantize_da(da1[1], first[1])

@@ -75,24 +75,31 @@ def tile_attend_gffn_sil_kernel(
         us_col = load_column(us, "us_col")
         wt_col = load_column(wt, "wt_col")
         s2_table = load_scales(w2_scales, "s2_table")
+        x_raw.append(load_half(x_rows, 1, "x_raw1"))
         dy_raw = [load_half(dy_rows, 0, "dy_raw0")]
         w2_table = load_words(w2_words, "w2_table")
-        x_raw.append(load_half(x_rows, 1, "x_raw1"))
         dy_raw.append(load_half(dy_rows, 1, "dy_raw1"))
         warm = sbuf([2], F32, "warm")
         nc.vector.memset(warm[:, 0:1], 0.0)
         nc.scalar.activation(warm[:, 1:2], warm[:, 0:1], ACT.Silu)
         ident = sbuf([P], F32, "ident")
         make_identity(nc, ident[:])
-        window2 = sbuf([UNITS], F32, "window2")
-        nc.vector.memset(window2[:], 0.0)
+        windows = [sbuf([UNITS], F32, "window0")]
+        nc.vector.memset(windows[0][:], 0.0)
 
-        def gather(table, dtype, name, tag=None):
-            picked = sbuf([SLOTS], dtype, name, tag)
-            nc.vector.tensor_copy(picked[:], table.indirect(offsets[:]))
+        def listed(table, cols):
+            return table.indirect(offsets[:, cols.start // 16 : cols.stop // 16])
+
+        every = slice(0, SLOTS)
+        parts = [slice(0, SLOTS // 2), slice(SLOTS // 2, SLOTS)]
+
+        def gather(table, dtype, name, pieces):
+            picked = sbuf([SLOTS], dtype, name)
+            for cols in pieces:
+                nc.vector.tensor_copy(picked[:, cols], listed(table[:].bitcast(dtype), cols))
             return picked
 
-        def group(raw, pair, name, copy=nc.scalar.copy):
+        def group(raw, pair, name, copy):
             grouped = sbuf([2 * K_PASS], BF16, name)
             copy(
                 grouped[:].rearrange("p (t s j) -> p s j t", t=2, j=PACK),
@@ -100,33 +107,40 @@ def tile_attend_gffn_sil_kernel(
             )
             return grouped
 
-        def quantize(grouped, fmt, name, tag=None):
-            width = grouped.shape[1] // PACK
-            codes = sbuf([width], U32, name + "_codes", tag)
-            scales = sbuf([width], U8, name + "_scales")
-            nc.vector.quantize_mx(out=codes[:].bitcast(fmt), scales=scales[:], in_=grouped[:])
-            return codes, scales
+        def operand(width, name, tag=None):
+            return sbuf([width], U32, name + "_codes", tag), sbuf([width], U8, name + "_scales")
 
-        def whole(operand):
-            return operand[0][:], operand[1][:]
+        def columns(pair, cols):
+            return pair[0][:, cols], pair[1][:, cols]
 
-        def product(acc, lhs, fmt_l, k, rhs, fmt_r, start=True, stop=True):
-            cols = slice(k * P, (k + 1) * P)
+        def quantize(target, fmt, grouped):
+            nc.vector.quantize_mx(out=target[0].bitcast(fmt), scales=target[1], in_=grouped)
+
+        def product(acc, lhs, fmt_l, rhs, fmt_r, start=True, stop=True):
             nc.tensor.matmul_mx(
-                out=acc[:],
-                lhsT=lhs[0][:, cols].bitcast(fmt_l),
-                lhsT_scale=lhs[1][:, cols],
+                out=acc,
+                lhsT=lhs[0].bitcast(fmt_l),
+                lhsT_scale=lhs[1],
                 rhs=rhs[0].bitcast(fmt_r),
                 rhs_scale=rhs[1],
                 start=start,
                 stop=stop,
             )
 
+        def block(k):
+            return slice(k * P, (k + 1) * P)
+
+        def quantize_pairs(grouped, fmt, name, tag=None):
+            target = operand(K_PASS, name, tag)
+            for pair in range(2):
+                quantize(columns(target, parts[pair]), fmt, grouped[pair][:])
+            return target
+
         def turn_x(grouped, u, n, name):
             turned_words = bank(n, name + "_words")
             for t in range(PACK):
                 words = grouped[t // 2][:].bitcast(F32)[:, 256 * (t % 2) + u : 256 * (t % 2 + 1) : 2]
-                nc.tensor.transpose(turned_words[:, t * P : (t + 1) * P], words, ident[:])
+                nc.tensor.transpose(turned_words[:, block(t)], words, ident[:])
             by_row = sbuf([2 * K_PASS], BF16, name)
             nc.scalar.copy(
                 by_row[:].rearrange("s (e p t) -> s e p t", e=2, t=PACK),
@@ -134,191 +148,151 @@ def tile_attend_gffn_sil_kernel(
             )
             return by_row
 
-        def scaled_first_product(xq, w1, h, z, t):
-            a = bank(t, "a")
-            product(a, xq[t // 2], E4M3, t % 2, whole(w1), E4M3)
-            nc.vector.scalar_tensor_tensor(z[t // 2][:, t % 2, :], a[:], us_col[:, h, t : t + 1], ts_all[:], ALU.mult, ALU.mult)
-
-        def turned_first_product(xq, w1):
+        def first_product(xq, h):
             sums = [bank(4 + g, "a_by_slot") for g in range(4)]
             for g in range(4):
-                product(sums[g], w1, E4M3, g, whole(xq), E4M3)
-            by_row = [bank(b, "a_by_row") for b in range(4)]
-
-            def turned_sums(t, half):
-                return by_row[2 * half + t // 2][:, 256 * (t % 2) : 256 * (t % 2 + 1)]
-
+                product(sums[g][:], columns(w1, block(g)), E4M3, columns(xq, every), E4M3)
+            by_row = [bank(t, "a_by_row") for t in range(PACK)]
             for g in range(4):
-                scaled = sbuf([K_PASS], F32, f"a_scaled{g}")
+                scaled = sbuf([K_PASS], F32, f"a_scaled{h}{g}", f"a_scaled{g}")
                 nc.scalar.activation(scaled[:], sums[g][:], ACT.Copy, scale=ts_col[:, g : g + 1])
                 for t in range(PACK):
-                    nc.tensor.transpose(turned_sums(t, g // 2)[:, g % 2 * P : (g % 2 + 1) * P], scaled[:, t * P : (t + 1) * P], ident[:])
-            acts = sbuf([2, PACK, SLOTS], F32, "acts0")
-            sl, th = acts[:, 0], acts[:, 1]
-            for values, func, scale in ((sl, ACT.Silu, minus_us), (th, ACT.Tanh, half_us)):
-                for half in range(2):
-                    for t in range(PACK):
-                        cols = slice(256 * half, 256 * (half + 1))
-                        nc.scalar.activation(values[:, t, cols], turned_sums(t, half), func, scale=scale[:, t : t + 1])
-            return sl, th
+                    nc.tensor.transpose(by_row[t][:, block(g)], scaled[:, block(t)], ident[:])
+            return by_row
 
-        def activations(z, h):
-            sl = sbuf([PACK, SLOTS], F32, f"silu{h}", f"dy_raw{h}")
-            th = sbuf([PACK, SLOTS], F32, f"tanh{h}", "us_col")
-            for pair in range(2):
-                rows = slice(2 * pair, 2 * pair + 2)
-                nc.scalar.activation(sl[:, rows, :], z[pair][:], ACT.Silu, scale=-1.0)
-            for pair in range(2):
-                rows = slice(2 * pair, 2 * pair + 2)
-                nc.scalar.activation(th[:, rows, :], z[pair][:], ACT.Tanh, scale=0.5)
-            return sl, th
-
-        def times_dh(sl, dyq, w2, h):
-            m = sbuf([PACK, SLOTS], F32, f"m{h}")
+        def activation(by_row, func, scale, name, tag):
+            values = sbuf([PACK, SLOTS], F32, name, tag)
             for t in range(PACK):
-                dh = bank(4 + t, "dh")
-                product(dh, dyq[t // 2], E5M2, t % 2, whole(w2), E4M3)
-                nc.vector.scalar_tensor_tensor(m[:, t, :], sl[:, t, :], 1.0, dh[:], ALU.subtract, ALU.mult)
-            return m
+                nc.scalar.activation(values[:, t, :], by_row[t][:], func, scale=scale[:, t : t + 1])
+            return values
 
-        def times_sigmoid(th, m, h):
-            n = sbuf([PACK, SLOTS], F32, f"n{h}")
+        def outer(engine, h, tag=None):
+            factor = sbuf([PACK, SLOTS], F32, f"factor{h}", tag)
+            for t in range(PACK):
+                engine.tensor_scalar(factor[:, t, :], ts_all[:], wu[:, h, t : t + 1], 0.0, ALU.mult, ALU.add)
+            return factor
+
+        def times(result, values, op, factor):
             for pair in range(2):
                 rows = slice(2 * pair, 2 * pair + 2)
-                nc.vector.scalar_tensor_tensor(n[:, rows, :], th[:, rows, :], 1.0, m[:, rows, :], ALU.add, ALU.mult)
-            return n
+                nc.vector.scalar_tensor_tensor(result[:, rows, :], values[:, rows, :], 1.0, factor[:, rows, :], op, ALU.mult)
 
-        def finish(engine, n, h, grouped, cols):
-            engine.tensor_tensor(
+        def second_product(dyq, q, n):
+            dh = bank(n, "dh")
+            for t in range(PACK):
+                product(dh[:, block(t)], columns(dyq, block(t)), E5M2, columns(w2, block(q)), E4M3)
+            return dh
+
+        def finish(grouped, dh, factor, q):
+            nc.vector.tensor_tensor(
                 grouped.rearrange("p (c i t) -> p c t i", i=4, t=PACK),
-                n[:, :, cols].rearrange("p t (c i) -> p c t i", i=4),
-                factors[h][:, :, cols].rearrange("p t (c i) -> p c t i", i=4),
+                dh[:].rearrange("p (t c i) -> p c t i", i=4, t=PACK),
+                factor[:, :, block(q)].rearrange("p t (c i) -> p c t i", i=4),
                 ALU.mult,
             )
 
-        ts_row = gather(ts_table[:], F32, "ts_row")
-        xg0 = [group(x_raw[0], 0, "x_grouped00")]
+        def cleared(name, tag):
+            window = sbuf([UNITS], F32, name, tag)
+            nc.gpsimd.memset(window[:], 0.0)
+            return window
+
+        ts_row = sbuf([SLOTS], F32, "ts_row")
+        nc.scalar.activation(ts_row[:], listed(ts_table[:], every), ACT.Copy)
         turned = bank(0, "turned")
         for b in range(4):
-            nc.tensor.transpose(turned[:, b * P : (b + 1) * P], ts_row[:, b * P : (b + 1) * P], ident[:])
+            nc.tensor.transpose(turned[:, block(b)], ts_row[:, block(b)], ident[:])
         ts_col = sbuf([4], F32, "ts_col")
         nc.scalar.copy(ts_col[:], turned[:, 0::P])
-        xg0.append(group(x_raw[0], 1, "x_grouped01"))
         spread = bank(1, "spread")
         for b in range(4):
-            nc.tensor.transpose(spread[:, b * P : (b + 1) * P], ts_col[:, b : b + 1].to_broadcast([P, P]), ident[:])
+            nc.tensor.transpose(spread[:, block(b)], ts_col[:, b : b + 1].to_broadcast([P, P]), ident[:])
         ts_all = sbuf([SLOTS], F32, "ts_all")
         nc.scalar.copy(ts_all[:], spread[:])
 
+        s1 = gather(s1_table, U8, "s1", [every])
+        xg0 = [group(x_raw[0], 0, "x_grouped00", nc.vector.tensor_copy), group(x_raw[0], 1, "x_grouped01", nc.scalar.copy)]
+        xq0 = quantize_pairs(xg0, E4M3, "x0")
+        xr0 = [turn_x(xg0, 0, 2, "x_by_row00")]
+        w1 = (gather(w1_table, U32, "w1", parts), s1)
         wu = sbuf([HALVES, PACK], F32, "wu")
+        minus_us = sbuf([HALVES, PACK], F32, "minus_us")
+        half_us = [sbuf([PACK], F32, f"half_us{h}") for h in range(HALVES)]
         nc.vector.scalar_tensor_tensor(wu[:], us_col, -0.5, wt_col, ALU.mult, ALU.mult)
-        factors = []
-
-
-        s1 = gather(s1_table[:].bitcast(U8), U8, "s1", "ts_table")
-        xq0 = (sbuf([K_PASS], U32, "x0_codes", "s1_table"), sbuf([K_PASS], U8, "x0_scales"))
-        for pair in range(2):
-            cols = slice(pair * 256, (pair + 1) * 256)
-            nc.vector.quantize_mx(out=xq0[0][:, cols].bitcast(E4M3), scales=xq0[1][:, cols], in_=xg0[pair][:])
-        w1 = (sbuf([SLOTS], U32, "w1"), s1)
-        for half in range(2):
-            listed = offsets[:, 16 * half : 16 * (half + 1)]
-            nc.vector.tensor_copy(w1[0][:, 256 * half : 256 * (half + 1)], w1_table[:].bitcast(U32).indirect(listed))
-        s2 = gather(s2_table[:].bitcast(U8), U8, "s2")
-        minus_us = sbuf([PACK], F32, "minus_us")
-        half_us = sbuf([PACK], F32, "half_us")
-        nc.vector.tensor_scalar(minus_us[:], us_col[:, 0, :], -1.0, 0.0, ALU.mult, ALU.add)
-        nc.vector.tensor_scalar(half_us[:], us_col[:, 0, :], 0.5, 0.0, ALU.mult, ALU.add)
-        xr = {(0, 0): turn_x(xg0, 0, 0, "x_by_row00")}
-        sl0, th0 = turned_first_product(xq0, w1)
+        nc.vector.tensor_scalar(minus_us[:], us_col, -1.0, 0.0, ALU.mult, ALU.add)
+        for h in range(HALVES):
+            nc.vector.tensor_scalar(half_us[h][:], us_col[:, h, :], 0.5, 0.0, ALU.mult, ALU.add)
+        a0 = first_product(xq0, 0)
+        factor0 = outer(nc.vector, 0)
+        xrq = [operand(K_PASS, "xr0", "w1_table")]
+        quantize(columns(xrq[0], parts[0]), E4M3, xr0[0][:])
+        s2 = gather(s2_table, U8, "s2", [every])
+        xg1 = [group(x_raw[1], 0, "x_grouped10", nc.scalar.copy), group(x_raw[1], 1, "x_grouped11", nc.vector.tensor_copy)]
+        th0 = activation(a0, ACT.Tanh, half_us[0], "tanh0", "x_raw1")
+        sl0 = activation(a0, ACT.Silu, minus_us[:, 0, :], "silu0", "half_us0")
         dyg0 = [group(dy_raw[0], pair, f"dy_grouped0{pair}", nc.vector.tensor_copy) for pair in range(2)]
-        dyq0 = [quantize(dyg0[pair], E5M2, f"dy0{pair}") for pair in range(2)]
-        w2 = (gather(w2_table[:].bitcast(U32), U32, "w2"), s2)
-        factors.append(sbuf([PACK, SLOTS], F32, "factors0", "w2_table"))
-        for t in range(PACK):
-            nc.vector.tensor_scalar(factors[0][:, t, :], ts_all[:], wu[:, 0, t : t + 1], None, ALU.mult)
-        m0 = times_dh(sl0, dyq0, w2, 0)
-        window1 = sbuf([UNITS], F32, "window1", "dy01_codes")
-        nc.gpsimd.memset(window1[:], 0.0)
-        xg1 = [group(x_raw[1], pair, f"x_grouped1{pair}") for pair in range(2)]
-        xr[1, 0] = turn_x(xg1, 0, 7, "x_by_row10")
-        dyg1 = [group(dy_raw[1], pair, f"dy_grouped1{pair}") for pair in range(2)]
-        n0 = times_sigmoid(th0, m0, 0)
-        parts = [slice(0, SLOTS // 2), slice(SLOTS // 2, SLOTS)]
+        xq1 = quantize_pairs(xg1, E4M3, "x1", "dy_raw0")
+        a1 = first_product(xq1, 1)
+        dyq0 = quantize_pairs(dyg0, E5M2, "dy0")
+        w2 = (gather(w2_table, U32, "w2", [every]), s2)
+        slope0 = sbuf([PACK, SLOTS], F32, "slope0", "w2_table")
+        times(slope0, th0, ALU.add, factor0)
+        windows.append(cleared("window1", "factor0"))
+        times(slope0, sl0, ALU.subtract, slope0)
+        factor1 = outer(nc.gpsimd, 1, "half_us0")
+        da0 = sbuf([PACK * SLOTS], BF16, "da0")
+        for q in range(4):
+            finish(da0[:, q * K_PASS : (q + 1) * K_PASS], second_product(dyq0, q, 4 + q), slope0, q)
+        daq = [operand(SLOTS, f"daq{h}") for h in range(HALVES)]
+        quantize(columns(daq[0], every), E5M2, da0[:])
 
-        da_codes = sbuf([5 * 256], U32, "da_codes")
-        da_scales = sbuf([5 * 256], U8, "da_scales")
-        first = (256, 768)
+        dyg1 = [group(dy_raw[1], pair, f"dy_grouped1{pair}", nc.scalar.copy) for pair in range(2)]
+        th1 = activation(a1, ACT.Tanh, half_us[1], "tanh1", "dy_raw1")
+        sl1 = activation(a1, ACT.Silu, minus_us[:, 1, :], "silu1", "half_us1")
+        dyq1 = quantize_pairs(dyg1, E5M2, "dy1")
+        windows.append(cleared("window2", "dy_grouped11"))
+        times(factor1, th1, ALU.add, factor1)
+        windows.append(cleared("window3", "dy_raw1"))
+        times(factor1, sl1, ALU.subtract, factor1)
+        xr1 = [turn_x(xg1, u, u, f"x_by_row1{u}") for u in range(2)]
+        xr0.append(turn_x(xg0, 1, 2, "x_by_row01"))
+        da1 = [sbuf([PACK * SLOTS // 2], BF16, f"da1{part}") for part in range(2)]
+        dh1 = [second_product(dyq1, q, 4 + q) for q in range(4)]
+        xrq.append(operand(K_PASS, "xr1"))
+        for q in range(3):
+            finish(da1[q // 2][:, q % 2 * K_PASS : (q % 2 + 1) * K_PASS], dh1[q], factor1, q)
+            if q == 0:
+                quantize(columns(xrq[1], parts[0]), E4M3, xr1[0][:])
+        quantize(columns(daq[1], parts[0]), E5M2, da1[0][:])
 
-        def quantize_da(part, start):
-            grouped, cols = part
-            place = slice(start + cols.start, start + cols.stop)
-            nc.vector.quantize_mx(out=da_codes[:, place].bitcast(E5M2), scales=da_scales[:, place], in_=grouped[:])
-
-        def da_operand(start):
-            return da_codes[:, start : start + SLOTS], da_scales[:, start : start + SLOTS]
-
-        def finish_part(engine, n, h, cols, tag=None):
-            grouped = sbuf([PACK * (cols.stop - cols.start)], BF16, f"da{h}_{cols.start}", tag)
-            finish(engine, n, h, grouped[:], cols)
-            return grouped, cols
-
-        xq1 = [quantize(xg1[0], E4M3, "x10")]
-        da0 = [finish_part(nc.vector, n0, 0, slice(0, 128))]
-        xq1.append(quantize(xg1[1], E4M3, "x11"))
-        xrq = {(0, 0): quantize(xr[0, 0], E4M3, "xr00", "m0")}
-        z1 = [sbuf([2, SLOTS], F32, f"z1{pair}") for pair in range(2)]
-        for t in range(PACK):
-            scaled_first_product(xq1, w1, 1, z1, t)
-        da0.append(finish_part(nc.gpsimd, n0, 0, slice(128, 256), "x10_codes"))
-        sl1, th1 = activations(z1, 1)
-        dyq1 = [quantize(dyg1[0], E5M2, "dy10"), (da_codes[:, 0:256], da_scales[:, 0:256])]
-        nc.vector.quantize_mx(out=dyq1[1][0].bitcast(E5M2), scales=dyq1[1][1], in_=dyg1[1][:])
-        da0.append(finish_part(nc.vector, n0, 0, slice(256, 384), "dy_grouped10"))
-        for part in da0[:2]:
-            quantize_da(part, first[0])
-        da0.append(finish_part(nc.gpsimd, n0, 0, slice(384, SLOTS), "dy_grouped11"))
-        m1 = times_dh(sl1, dyq1, w2, 1)
-        factors.append(sbuf([PACK, SLOTS], F32, "factors1", "z10"))
-        for cols in parts:
-            for t in range(PACK):
-                nc.scalar.activation(factors[1][:, t, cols], ts_all[:, cols], ACT.Copy, scale=wu[:, 1, t : t + 1])
-        window0 = sbuf([UNITS], F32, "window0", "dy10_codes")
-        nc.gpsimd.memset(window0[:], 0.0)
-        n1 = times_sigmoid(th1, m1, 1)
-        for part in da0[2:]:
-            quantize_da(part, first[0])
-        for h, grouped in enumerate((xg0, xg1)):
-            xr[h, 1] = turn_x(grouped, 1, 4 + h, f"x_by_row{h}1")
-        da1 = [finish_part(nc.vector, n1, 1, parts[0])]
-        xrq[1, 0] = quantize(xr[1, 0], E4M3, "xr10", "dy_grouped11")
-        quantize_da(da1[0], first[1])
-
-        def output_sums(j, n, starts, cols, name):
+        def output_sums(j, n, cols, copy, name, tag=None):
+            width = cols.stop - cols.start
             dw = bank(n, name)
             for h in range(HALVES):
-                product(dw, xrq[h, j // 2], E4M3, j % 2, da_operand(starts[h]), E5M2, h == 0, h == HALVES - 1)
-            sums = sbuf([cols.stop - cols.start], F32, name + "_sb")
-            nc.scalar.copy(sums[:], dw[:, cols])
+                product(dw[:, 0:width], columns(xrq[h], block(j)), E4M3, columns(daq[h], cols), E5M2, h == 0, h == HALVES - 1)
+            sums = sbuf([width], F32, name + "_sb", tag)
+            copy(sums[:], dw[:, 0:width])
             return sums
 
-        def scatter(window, sums, cols):
-            nc.vector.tensor_copy(window[:].indirect(offsets[:, cols.start // 16 : cols.stop // 16]), sums[:])
+        def scalar_scatter(window, sums, cols):
+            nc.scalar.activation(listed(window[:], cols), sums, ACT.Copy)
 
-        early = output_sums(0, 0, (first[0] - 256, first[1] - 256), parts[1], "dw0_early")
-        da1.append(finish_part(nc.vector, n1, 1, parts[1]))
-        xrq[1, 1] = quantize(xr[1, 1], E4M3, "xr11")
-        quantize_da(da1[1], first[1])
-        xrq[0, 1] = quantize(xr[0, 1], E4M3, "xr01", "n1")
-        every = slice(0, SLOTS)
-        sums1 = output_sums(1, 1, first, every, "dw1")
-        late = output_sums(0, 2, first, parts[1], "dw0_late")
         out_rows = out.rearrange("(p j) n -> p j n", j=PACK)
-        scatter(window1, early, parts[0])
-        scatter(window2, sums1, every)
-        nc.sync.dma_start(out_rows[:, 1, :], window2[:])
-        scatter(window1, late, parts[1])
-        nc.sync.dma_start(out_rows[:, 0, :], window1[:])
-        for j, n, window in ((2, 3, window0), (3, 6, window2)):
-            scatter(window, output_sums(j, n, first, every, f"dw{j}"), every)
-            nc.sync.dma_start(out_rows[:, j, :], window[:])
+        for j in range(2):
+            scalar_scatter(windows[j], output_sums(j, (3, 0)[j], parts[0], nc.scalar.copy, f"dw{j}_early")[:], parts[0])
+        finish(da1[1][:, K_PASS:], dh1[3], factor1, 3)
+        quantize(columns(xrq[1], parts[1]), E4M3, xr1[1][:])
+        quantize(columns(daq[1], parts[1]), E5M2, da1[1][:])
+        quantize(columns(xrq[0], parts[1]), E4M3, xr0[1][:])
+        late0 = output_sums(0, 4, parts[1], nc.vector.tensor_copy, "dw0_late")
+        late1 = output_sums(1, 5, parts[1], nc.scalar.copy, "dw1_late")
+        nc.vector.tensor_copy(listed(windows[0][:], parts[1]), late0[:])
+        nc.sync.dma_start(out_rows[:, 0, :], windows[0][:])
+        scalar_scatter(windows[1], late1[:], parts[1])
+        nc.scalar.dma_start(out_rows[:, 1, :], windows[1][:])
+        sums2 = output_sums(2, 6, every, nc.vector.tensor_copy, "dw2", "dw0_late_sb")
+        nc.vector.tensor_copy(listed(windows[2][:], every), sums2[:])
+        nc.sync.dma_start(out_rows[:, 2, :], windows[2][:])
+        sums3 = output_sums(3, 1, every, nc.scalar.copy, "dw3", "dw1_late_sb")
+        for cols in parts:
+            scalar_scatter(windows[3], sums3[:, cols], cols)
+        nc.scalar.dma_start(out_rows[:, 3, :], windows[3][:])

@@ -29,10 +29,14 @@ def tile_attend_gffn_sil_kernel(
     with ExitStack() as ctx:
         lists = ctx.enter_context(tc.tile_pool(name="lists", bufs=1))
         keep = ctx.enter_context(tc.tile_pool(name="keep", bufs=1))
+        shared = ctx.enter_context(tc.tile_pool(name="shared", bufs=1))
         psum = ctx.enter_context(tc.psum_pool(name="psum", bufs=1))
 
         def sbuf(shape, dtype, name, tag=None):
             return keep.tile([P, *shape], dtype, name=name, tag=tag or name, align_bytes=64)
+
+        def placed(shape, dtype, name, offset):
+            return shared.tile([P, *shape], dtype, name=name, offset=offset, align_bytes=64)
 
         def bank(n, name):
             return psum.tile([P, SLOTS], F32, name=name, tag=f"bank{n}")
@@ -48,8 +52,7 @@ def tile_attend_gffn_sil_kernel(
             nc.sync.dma_start(raw[:], rows[:, :, h * K_PASS : (h + 1) * K_PASS])
             return raw
 
-        def load_words(words, name):
-            table = sbuf([UNITS], I32, name)
+        def load_words(words, table):
             nc.sync.dma_start(table[:], words[0].rearrange("p n t -> p (n t)").bitcast(I32))
             return table
 
@@ -67,25 +70,23 @@ def tile_attend_gffn_sil_kernel(
             return column
 
         ts_table = sbuf([UNITS], F32, "ts_table")
-        nc.vector.memset(ts_table[:], 0.0)
-        nc.scalar.dma_start(ts_table[0:1, :], ts[0:1, :])
+        nc.scalar.dma_start(ts_table[P - 1 : P, :], ts[0:1, :])
         x_raw = [load_half(x_rows, 0, "x_raw0")]
         s1_table = load_scales(w1_scales, "s1_table")
-        w1_table = load_words(w1_words, "w1_table")
+        w1_table = load_words(w1_words, sbuf([UNITS], I32, "w1_table"))
         us_col = load_column(us, "us_col")
         wt_col = load_column(wt, "wt_col")
         s2_table = load_scales(w2_scales, "s2_table")
+        nc.vector.memset(ts_table[0 : P - 1, :], 0.0)
         x_raw.append(load_half(x_rows, 1, "x_raw1"))
         dy_raw = [load_half(dy_rows, 0, "dy_raw0")]
-        w2_table = load_words(w2_words, "w2_table")
+        w2_table = load_words(w2_words, placed([UNITS], I32, "w2_table", 2 * UNITS))
         dy_raw.append(load_half(dy_rows, 1, "dy_raw1"))
         warm = sbuf([2], F32, "warm")
         nc.vector.memset(warm[:, 0:1], 0.0)
         nc.scalar.activation(warm[:, 1:2], warm[:, 0:1], ACT.Silu)
         ident = sbuf([P], F32, "ident")
         make_identity(nc, ident[:])
-        windows = [sbuf([UNITS], F32, "window0")]
-        nc.vector.memset(windows[0][:], 0.0)
 
         def listed(table, cols):
             return table.indirect(offsets[:, cols.start // 16 : cols.stop // 16])
@@ -202,7 +203,7 @@ def tile_attend_gffn_sil_kernel(
         for b in range(4):
             nc.tensor.transpose(turned[:, block(b)], ts_row[:, block(b)], ident[:])
         ts_col = sbuf([4], F32, "ts_col")
-        nc.scalar.copy(ts_col[:], turned[:, 0::P])
+        nc.scalar.copy(ts_col[:], turned[:, P - 1 :: P])
         spread = bank(1, "spread")
         for b in range(4):
             nc.tensor.transpose(spread[:, block(b)], ts_col[:, b : b + 1].to_broadcast([P, P]), ident[:])
@@ -234,7 +235,9 @@ def tile_attend_gffn_sil_kernel(
         a1 = first_product(xq1, 1)
         dyq0 = quantize_pairs(dyg0, E5M2, "dy0")
         w2 = (gather(w2_table, U32, "w2", [every]), s2)
-        slope0 = sbuf([PACK, SLOTS], F32, "slope0", "w2_table")
+        slope0 = placed([PACK, SLOTS], F32, "slope0", 0)
+        windows = [placed([UNITS], F32, "window0", 4 * UNITS)]
+        nc.gpsimd.memset(windows[0][:], 0.0)
         times(slope0, th0, ALU.add, factor0)
         windows.append(cleared("window1", "factor0"))
         times(slope0, sl0, ALU.subtract, slope0)

@@ -19,6 +19,7 @@ PACK = 4
 K_PASS = P * PACK
 D, E, R, SLOTS, UNITS = 512, 512, 1024, 512, 2048
 HALVES = R // K_PASS
+KIB = 1024
 FLOPS = 2 * R * SLOTS * (D + E + D)
 
 
@@ -47,8 +48,7 @@ def tile_attend_gffn_sil_kernel(
         x_rows = xT.rearrange("(p j) r -> p j r", j=PACK)
         dy_rows = dyT.rearrange("(p j) r -> p j r", j=PACK)
 
-        def load_half(rows, h, name):
-            raw = sbuf([PACK, K_PASS], F32, name)
+        def load_half(rows, h, raw):
             nc.sync.dma_start(raw[:], rows[:, :, h * K_PASS : (h + 1) * K_PASS])
             return raw
 
@@ -56,9 +56,9 @@ def tile_attend_gffn_sil_kernel(
             nc.sync.dma_start(table[:], words[0].rearrange("p n t -> p (n t)").bitcast(I32))
             return table
 
-        def load_scales(scales, name):
+        def load_plane(scales, name):
             table = sbuf([UNITS // 4], I32, name)
-            nc.vector.memset(table[:], 0)
+            nc.gpsimd.memset(table[:], 0)
             for r in range(4):
                 nc.sync.dma_start(table[r:P:32, :], scales[0, r:16:4, :].bitcast(I32))
             return table
@@ -71,22 +71,26 @@ def tile_attend_gffn_sil_kernel(
 
         ts_table = sbuf([UNITS], F32, "ts_table")
         nc.scalar.dma_start(ts_table[P - 1 : P, :], ts[0:1, :])
-        x_raw = [load_half(x_rows, 0, "x_raw0")]
-        s1_table = load_scales(w1_scales, "s1_table")
+        s2_table = sbuf([UNITS // 4], I32, "s2_table")
+        nc.sync.dma_start(s2_table[P - 16 : P, :], w2_scales[0].bitcast(I32))
+        x_raw = [load_half(x_rows, 0, sbuf([PACK, K_PASS], F32, "x_raw0"))]
+        s1_table = load_plane(w1_scales, "s1_table")
+        ident = sbuf([P], F32, "ident")
+        make_identity(nc, ident[:])
+        nc.gpsimd.memset(s2_table[0 : P - 16, :], 0)
+        windows = [sbuf([UNITS], F32, "window0")]
+        nc.gpsimd.memset(windows[0][:], 0.0)
+        nc.vector.memset(ts_table[0 : P - 1, :], 0.0)
         w1_table = load_words(w1_words, sbuf([UNITS], I32, "w1_table"))
         us_col = load_column(us, "us_col")
         wt_col = load_column(wt, "wt_col")
-        s2_table = load_scales(w2_scales, "s2_table")
-        nc.vector.memset(ts_table[0 : P - 1, :], 0.0)
-        x_raw.append(load_half(x_rows, 1, "x_raw1"))
-        dy_raw = [load_half(dy_rows, 0, "dy_raw0")]
-        w2_table = load_words(w2_words, placed([UNITS], I32, "w2_table", 2 * UNITS))
-        dy_raw.append(load_half(dy_rows, 1, "dy_raw1"))
+        x_raw.append(load_half(x_rows, 1, sbuf([PACK, K_PASS], F32, "x_raw1")))
+        dy_raw = [load_half(dy_rows, 0, sbuf([PACK, K_PASS], F32, "dy_raw0"))]
+        w2_table = load_words(w2_words, placed([UNITS], I32, "w2_table", 7 * KIB))
+        dy_raw.append(load_half(dy_rows, 1, sbuf([PACK, K_PASS], F32, "dy_raw1")))
         warm = sbuf([2], F32, "warm")
         nc.vector.memset(warm[:, 0:1], 0.0)
         nc.scalar.activation(warm[:, 1:2], warm[:, 0:1], ACT.Silu)
-        ident = sbuf([P], F32, "ident")
-        make_identity(nc, ident[:])
 
         def listed(table, cols):
             return table.indirect(offsets[:, cols.start // 16 : cols.stop // 16])
@@ -100,12 +104,23 @@ def tile_attend_gffn_sil_kernel(
                 nc.vector.tensor_copy(picked[:, cols], listed(table[:].bitcast(dtype), cols))
             return picked
 
-        def group(raw, pair, name, copy):
-            grouped = sbuf([2 * K_PASS], BF16, name)
+        def place_scales(picked, name, tag):
+            plane = sbuf([SLOTS], U8, name, tag)
+            for q in range(4):
+                rows = picked[P - 16 + 4 * q : P - 12 + 4 * q, :]
+                nc.sync.dma_start(plane[32 * q : 32 * q + 4, :].bitcast(I32), rows.bitcast(I32))
+            return plane
+
+        def group_pair(grouped, raw, pair, copy):
             copy(
-                grouped[:].rearrange("p (t s j) -> p s j t", t=2, j=PACK),
+                grouped.rearrange("p (t s j) -> p s j t", t=2, j=PACK),
                 raw[:].rearrange("p j (s t) -> p s j t", t=PACK)[:, :, :, 2 * pair : 2 * pair + 2],
             )
+
+        def group(raw, name, copy):
+            grouped = sbuf([2, 2 * K_PASS], BF16, name)
+            for pair in range(2):
+                group_pair(grouped[:, pair, :], raw, pair, copy)
             return grouped
 
         def operand(width, name, tag=None):
@@ -134,13 +149,18 @@ def tile_attend_gffn_sil_kernel(
         def quantize_pairs(grouped, fmt, name, tag=None):
             target = operand(K_PASS, name, tag)
             for pair in range(2):
-                quantize(columns(target, parts[pair]), fmt, grouped[pair][:])
+                quantize(columns(target, parts[pair]), fmt, grouped[pair])
+            return target
+
+        def quantize_whole(grouped, fmt, name):
+            target = operand(K_PASS, name)
+            quantize(columns(target, every), fmt, grouped[:].rearrange("p u c -> p (u c)"))
             return target
 
         def turn_x(grouped, u, n, name):
             turned_words = bank(n, name + "_words")
             for t in range(PACK):
-                words = grouped[t // 2][:].bitcast(F32)[:, 256 * (t % 2) + u : 256 * (t % 2 + 1) : 2]
+                words = grouped[t // 2].bitcast(F32)[:, 256 * (t % 2) + u : 256 * (t % 2 + 1) : 2]
                 nc.tensor.transpose(turned_words[:, block(t)], words, ident[:])
             by_row = sbuf([2 * K_PASS], BF16, name)
             nc.scalar.copy(
@@ -149,16 +169,19 @@ def tile_attend_gffn_sil_kernel(
             )
             return by_row
 
-        def first_product(xq, h):
+        def first_product(xq, scaled):
             sums = [bank(4 + g, "a_by_slot") for g in range(4)]
             for g in range(4):
                 product(sums[g][:], columns(w1, block(g)), E4M3, columns(xq, every), E4M3)
+            for g in range(4):
+                nc.scalar.activation(scaled[g][:], sums[g][:], ACT.Copy, scale=ts_col[:, g : g + 1])
+            return scaled
+
+        def turn(scaled):
             by_row = [bank(t, "a_by_row") for t in range(PACK)]
             for g in range(4):
-                scaled = sbuf([K_PASS], F32, f"a_scaled{h}{g}", f"a_scaled{g}")
-                nc.scalar.activation(scaled[:], sums[g][:], ACT.Copy, scale=ts_col[:, g : g + 1])
                 for t in range(PACK):
-                    nc.tensor.transpose(by_row[t][:, block(g)], scaled[:, block(t)], ident[:])
+                    nc.tensor.transpose(by_row[t][:, block(g)], scaled[g][:, block(t)], ident[:])
             return by_row
 
         def activation(by_row, func, scale, name, tag):
@@ -167,10 +190,10 @@ def tile_attend_gffn_sil_kernel(
                 nc.scalar.activation(values[:, t, :], by_row[t][:], func, scale=scale[:, t : t + 1])
             return values
 
-        def outer(engine, h, tag=None):
+        def outer(engines, h, tag=None):
             factor = sbuf([PACK, SLOTS], F32, f"factor{h}", tag)
             for t in range(PACK):
-                engine.tensor_scalar(factor[:, t, :], ts_all[:], wu[:, h, t : t + 1], 0.0, ALU.mult, ALU.add)
+                engines[t].tensor_scalar(factor[:, t, :], ts_all[:], wu[:, h, t : t + 1], 0.0, ALU.mult, ALU.add)
             return factor
 
         def times(result, values, op, factor):
@@ -203,75 +226,80 @@ def tile_attend_gffn_sil_kernel(
         for b in range(4):
             nc.tensor.transpose(turned[:, block(b)], ts_row[:, block(b)], ident[:])
         ts_col = sbuf([4], F32, "ts_col")
-        nc.scalar.copy(ts_col[:], turned[:, P - 1 :: P])
+        nc.scalar.activation(ts_col[:], turned[:, P - 1 :: P], ACT.Copy, scale=0.5)
         spread = bank(1, "spread")
         for b in range(4):
             nc.tensor.transpose(spread[:, block(b)], ts_col[:, b : b + 1].to_broadcast([P, P]), ident[:])
         ts_all = sbuf([SLOTS], F32, "ts_all")
         nc.scalar.copy(ts_all[:], spread[:])
 
+        s2_rows = gather(s2_table, U8, "s2_rows", [every])
+        xg0 = [sbuf([2 * K_PASS], BF16, f"x_grouped0{pair}")[:] for pair in range(2)]
+        group_pair(xg0[0], x_raw[0], 0, nc.vector.tensor_copy)
+        group_pair(xg0[1], x_raw[0], 1, nc.scalar.copy)
         s1 = gather(s1_table, U8, "s1", [every])
-        xg0 = [group(x_raw[0], 0, "x_grouped00", nc.vector.tensor_copy), group(x_raw[0], 1, "x_grouped01", nc.scalar.copy)]
         xq0 = quantize_pairs(xg0, E4M3, "x0")
         xr0 = [turn_x(xg0, 0, 2, "x_by_row00")]
         w1 = (gather(w1_table, U32, "w1", parts), s1)
         wu = sbuf([HALVES, PACK], F32, "wu")
-        minus_us = sbuf([HALVES, PACK], F32, "minus_us")
-        half_us = [sbuf([PACK], F32, f"half_us{h}") for h in range(HALVES)]
-        nc.vector.scalar_tensor_tensor(wu[:], us_col, -0.5, wt_col, ALU.mult, ALU.mult)
-        nc.vector.tensor_scalar(minus_us[:], us_col, -1.0, 0.0, ALU.mult, ALU.add)
-        for h in range(HALVES):
-            nc.vector.tensor_scalar(half_us[h][:], us_col[:, h, :], 0.5, 0.0, ALU.mult, ALU.add)
-        a0 = first_product(xq0, 0)
-        factor0 = outer(nc.vector, 0)
-        xrq = [operand(K_PASS, "xr0", "w1_table")]
+        silu_scale = sbuf([HALVES, PACK], F32, "silu_scale")
+        nc.vector.scalar_tensor_tensor(wu[:], us_col, -1.0, wt_col, ALU.mult, ALU.mult)
+        nc.vector.tensor_scalar(silu_scale[:], us_col, -2.0, 0.0, ALU.mult, ALU.add)
+        a0 = turn(first_product(xq0, [sbuf([K_PASS], F32, f"a_scaled0{g}") for g in range(4)]))
+        xr0.append(turn_x(xg0, 1, 4, "x_by_row01"))
+        factor0 = outer([nc.vector] * PACK, 0)
+        xrq = [operand(2 * P, "xr00", "w1_table")]
         quantize(columns(xrq[0], parts[0]), E4M3, xr0[0][:])
-        s2 = gather(s2_table, U8, "s2", [every])
-        xg1 = [group(x_raw[1], 0, "x_grouped10", nc.scalar.copy), group(x_raw[1], 1, "x_grouped11", nc.vector.tensor_copy)]
-        th0 = activation(a0, ACT.Tanh, half_us[0], "tanh0", "x_raw1")
-        sl0 = activation(a0, ACT.Silu, minus_us[:, 0, :], "silu0", "half_us0")
-        dyg0 = [group(dy_raw[0], pair, f"dy_grouped0{pair}", nc.vector.tensor_copy) for pair in range(2)]
-        xq1 = quantize_pairs(xg1, E4M3, "x1", "dy_raw0")
-        a1 = first_product(xq1, 1)
-        dyq0 = quantize_pairs(dyg0, E5M2, "dy0")
+        th0 = activation(a0, ACT.Tanh, us_col[:, 0, :], "tanh0", None)
+        sl0 = activation(a0, ACT.Silu, silu_scale[:, 0, :], "silu0", None)
+        grouped = group(x_raw[1], "x_grouped1", nc.vector.tensor_copy)
+        xg1 = [grouped[:, pair, :] for pair in range(2)]
+        xq1 = quantize_whole(grouped, E4M3, "x1")
+        dyq0 = quantize_whole(group(dy_raw[0], "dy_grouped0", nc.vector.tensor_copy), E5M2, "dy0")
+        s2 = place_scales(s2_rows, "s2", "dy_raw0")
         w2 = (gather(w2_table, U32, "w2", [every]), s2)
+        scaled1 = [placed([K_PASS], F32, f"a_scaled1{g}", (8 + 2 * g) * KIB) for g in range(3)]
+        scaled1 = first_product(xq1, scaled1 + [sbuf([K_PASS], F32, "a_scaled13", "a_scaled03")])
         slope0 = placed([PACK, SLOTS], F32, "slope0", 0)
-        windows = [placed([UNITS], F32, "window0", 4 * UNITS)]
-        nc.gpsimd.memset(windows[0][:], 0.0)
+        windows.append(placed([UNITS], F32, "window1", 14 * KIB))
+        nc.gpsimd.memset(windows[1][:], 0.0)
         times(slope0, th0, ALU.add, factor0)
-        windows.append(cleared("window1", "factor0"))
+        dh0 = [second_product(dyq0, q, 4 + q) for q in range(4)]
+        a1 = turn(scaled1)
         times(slope0, sl0, ALU.subtract, slope0)
-        factor1 = outer(nc.gpsimd, 1, "half_us0")
+        factor1 = outer([nc.gpsimd] * 3 + [nc.vector], 1, "silu0")
         da0 = sbuf([PACK * SLOTS], BF16, "da0")
         for q in range(4):
-            finish(da0[:, q * K_PASS : (q + 1) * K_PASS], second_product(dyq0, q, 4 + q), slope0, q)
+            finish(da0[:, q * K_PASS : (q + 1) * K_PASS], dh0[q], slope0, q)
         daq = [operand(SLOTS, f"daq{h}") for h in range(HALVES)]
         quantize(columns(daq[0], every), E5M2, da0[:])
 
-        dyg1 = [group(dy_raw[1], pair, f"dy_grouped1{pair}", nc.scalar.copy) for pair in range(2)]
-        th1 = activation(a1, ACT.Tanh, half_us[1], "tanh1", "dy_raw1")
-        sl1 = activation(a1, ACT.Silu, minus_us[:, 1, :], "silu1", "half_us1")
-        dyq1 = quantize_pairs(dyg1, E5M2, "dy1")
-        windows.append(cleared("window2", "dy_grouped11"))
+        dyg1 = group(dy_raw[1], "dy_grouped1", nc.scalar.copy)
+        th1 = activation(a1, ACT.Tanh, us_col[:, 1, :], "tanh1", "dy_raw1")
+        sl1 = activation(a1, ACT.Silu, silu_scale[:, 1, :], "silu1", "us_col")
+        dyq1 = quantize_whole(dyg1, E5M2, "dy1")
+        windows.append(cleared("window2", "dy_grouped1"))
         times(factor1, th1, ALU.add, factor1)
         windows.append(cleared("window3", "dy_raw1"))
         times(factor1, sl1, ALU.subtract, factor1)
         xr1 = [turn_x(xg1, u, u, f"x_by_row1{u}") for u in range(2)]
-        xr0.append(turn_x(xg0, 1, 2, "x_by_row01"))
         da1 = [sbuf([PACK * SLOTS // 2], BF16, f"da1{part}") for part in range(2)]
         dh1 = [second_product(dyq1, q, 4 + q) for q in range(4)]
         xrq.append(operand(K_PASS, "xr1"))
         for q in range(3):
             finish(da1[q // 2][:, q % 2 * K_PASS : (q % 2 + 1) * K_PASS], dh1[q], factor1, q)
-            if q == 0:
+            if q == 1:
                 quantize(columns(xrq[1], parts[0]), E4M3, xr1[0][:])
         quantize(columns(daq[1], parts[0]), E5M2, da1[0][:])
+
+        def turned_x(h, j):
+            return columns(late_codes, block(j - 2)) if h == 0 and j >= 2 else columns(xrq[h], block(j))
 
         def output_sums(j, n, cols, copy, name, tag=None):
             width = cols.stop - cols.start
             dw = bank(n, name)
             for h in range(HALVES):
-                product(dw[:, 0:width], columns(xrq[h], block(j)), E4M3, columns(daq[h], cols), E5M2, h == 0, h == HALVES - 1)
+                product(dw[:, 0:width], turned_x(h, j), E4M3, columns(daq[h], cols), E5M2, h == 0, h == HALVES - 1)
             sums = sbuf([width], F32, name + "_sb", tag)
             copy(sums[:], dw[:, 0:width])
             return sums
@@ -285,7 +313,8 @@ def tile_attend_gffn_sil_kernel(
         finish(da1[1][:, K_PASS:], dh1[3], factor1, 3)
         quantize(columns(xrq[1], parts[1]), E4M3, xr1[1][:])
         quantize(columns(daq[1], parts[1]), E5M2, da1[1][:])
-        quantize(columns(xrq[0], parts[1]), E4M3, xr0[1][:])
+        late_codes = operand(2 * P, "xr01", "da10")
+        quantize(columns(late_codes, parts[0]), E4M3, xr0[1][:])
         late0 = output_sums(0, 4, parts[1], nc.vector.tensor_copy, "dw0_late")
         late1 = output_sums(1, 5, parts[1], nc.scalar.copy, "dw1_late")
         nc.vector.tensor_copy(listed(windows[0][:], parts[1]), late0[:])

@@ -58,7 +58,7 @@ def tile_attend_gffn_sil_kernel(
 
         def load_plane(scales, name):
             table = sbuf([UNITS // 4], I32, name)
-            nc.gpsimd.memset(table[:], 0)
+            nc.vector.memset(table[:], 0)
             for r in range(4):
                 nc.sync.dma_start(table[r:P:32, :], scales[0, r:16:4, :].bitcast(I32))
             return table
@@ -71,20 +71,16 @@ def tile_attend_gffn_sil_kernel(
 
         ts_table = sbuf([UNITS], F32, "ts_table")
         nc.scalar.dma_start(ts_table[P - 1 : P, :], ts[0:1, :])
-        s2_table = sbuf([UNITS // 4], I32, "s2_table")
-        nc.sync.dma_start(s2_table[P - 16 : P, :], w2_scales[0].bitcast(I32))
         x_raw = [load_half(x_rows, 0, sbuf([PACK, K_PASS], F32, "x_raw0"))]
         s1_table = load_plane(w1_scales, "s1_table")
         ident = sbuf([P], F32, "ident")
         make_identity(nc, ident[:])
-        nc.gpsimd.memset(s2_table[0 : P - 16, :], 0)
-        windows = [sbuf([UNITS], F32, "window0")]
-        nc.gpsimd.memset(windows[0][:], 0.0)
-        nc.vector.memset(ts_table[0 : P - 1, :], 0.0)
         w1_table = load_words(w1_words, sbuf([UNITS], I32, "w1_table"))
         us_col = load_column(us, "us_col")
         wt_col = load_column(wt, "wt_col")
-        x_raw.append(load_half(x_rows, 1, sbuf([PACK, K_PASS], F32, "x_raw1")))
+        s2_table = load_plane(w2_scales, "s2_table")
+        nc.vector.memset(ts_table[0 : P - 1, :].bitcast(I32), 0)
+        x_raw.append(load_half(x_rows, 1, placed([PACK, K_PASS], F32, "x_raw1", 26 * KIB)))
         dy_raw = [load_half(dy_rows, 0, sbuf([PACK, K_PASS], F32, "dy_raw0"))]
         w2_table = load_words(w2_words, placed([UNITS], I32, "w2_table", 7 * KIB))
         dy_raw.append(load_half(dy_rows, 1, sbuf([PACK, K_PASS], F32, "dy_raw1")))
@@ -103,13 +99,6 @@ def tile_attend_gffn_sil_kernel(
             for cols in pieces:
                 nc.vector.tensor_copy(picked[:, cols], listed(table[:].bitcast(dtype), cols))
             return picked
-
-        def place_scales(picked, name, tag):
-            plane = sbuf([SLOTS], U8, name, tag)
-            for q in range(4):
-                rows = picked[P - 16 + 4 * q : P - 12 + 4 * q, :]
-                nc.sync.dma_start(plane[32 * q : 32 * q + 4, :].bitcast(I32), rows.bitcast(I32))
-            return plane
 
         def group_pair(grouped, raw, pair, copy):
             copy(
@@ -184,16 +173,14 @@ def tile_attend_gffn_sil_kernel(
                     nc.tensor.transpose(by_row[t][:, block(g)], scaled[g][:, block(t)], ident[:])
             return by_row
 
-        def activation(by_row, func, scale, name, tag):
-            values = sbuf([PACK, SLOTS], F32, name, tag)
+        def activation(by_row, func, scale, values):
             for t in range(PACK):
                 nc.scalar.activation(values[:, t, :], by_row[t][:], func, scale=scale[:, t : t + 1])
             return values
 
-        def outer(engines, h, tag=None):
-            factor = sbuf([PACK, SLOTS], F32, f"factor{h}", tag)
-            for t in range(PACK):
-                engines[t].tensor_scalar(factor[:, t, :], ts_all[:], wu[:, h, t : t + 1], 0.0, ALU.mult, ALU.add)
+        def outer(engine, h, tiles, factor):
+            for n, t in enumerate(tiles):
+                engine.tensor_scalar(factor[:, n, :], ts_all[:], wu[:, h, t : t + 1], 0.0, ALU.mult, ALU.add)
             return factor
 
         def times(result, values, op, factor):
@@ -233,7 +220,6 @@ def tile_attend_gffn_sil_kernel(
         ts_all = sbuf([SLOTS], F32, "ts_all")
         nc.scalar.copy(ts_all[:], spread[:])
 
-        s2_rows = gather(s2_table, U8, "s2_rows", [every])
         xg0 = [sbuf([2 * K_PASS], BF16, f"x_grouped0{pair}")[:] for pair in range(2)]
         group_pair(xg0[0], x_raw[0], 0, nc.vector.tensor_copy)
         group_pair(xg0[1], x_raw[0], 1, nc.scalar.copy)
@@ -246,48 +232,55 @@ def tile_attend_gffn_sil_kernel(
         nc.vector.scalar_tensor_tensor(wu[:], us_col, -1.0, wt_col, ALU.mult, ALU.mult)
         nc.vector.tensor_scalar(silu_scale[:], us_col, -2.0, 0.0, ALU.mult, ALU.add)
         a0 = turn(first_product(xq0, [sbuf([K_PASS], F32, f"a_scaled0{g}") for g in range(4)]))
-        xr0.append(turn_x(xg0, 1, 4, "x_by_row01"))
-        factor0 = outer([nc.vector] * PACK, 0)
+        factor0 = outer(nc.vector, 0, range(PACK), sbuf([PACK, SLOTS], F32, "factor0"))
         xrq = [operand(2 * P, "xr00", "w1_table")]
         quantize(columns(xrq[0], parts[0]), E4M3, xr0[0][:])
-        th0 = activation(a0, ACT.Tanh, us_col[:, 0, :], "tanh0", None)
-        sl0 = activation(a0, ACT.Silu, silu_scale[:, 0, :], "silu0", None)
-        grouped = group(x_raw[1], "x_grouped1", nc.vector.tensor_copy)
-        xg1 = [grouped[:, pair, :] for pair in range(2)]
-        xq1 = quantize_whole(grouped, E4M3, "x1")
-        dyq0 = quantize_whole(group(dy_raw[0], "dy_grouped0", nc.vector.tensor_copy), E5M2, "dy0")
-        s2 = place_scales(s2_rows, "s2", "dy_raw0")
+        s2 = gather(s2_table, U8, "s2", [every])
+        xg1 = [sbuf([2 * K_PASS], BF16, f"x_grouped1{pair}")[:] for pair in range(2)]
+        group_pair(xg1[0], x_raw[1], 0, nc.scalar.copy)
+        group_pair(xg1[1], x_raw[1], 1, nc.vector.tensor_copy)
+        th0 = activation(a0, ACT.Tanh, us_col[:, 0, :], placed([PACK, SLOTS], F32, "tanh0", 22 * KIB))
+        sl0 = activation(a0, ACT.Silu, silu_scale[:, 0, :], placed([PACK, SLOTS], F32, "silu0", 30 * KIB))
+        dyg0 = group(dy_raw[0], "dy_grouped0", nc.vector.tensor_copy)
+        xq1 = quantize_pairs(xg1, E4M3, "x1", "dy_raw0")
+        dyq0 = quantize_whole(dyg0, E5M2, "dy0")
         w2 = (gather(w2_table, U32, "w2", [every]), s2)
         scaled1 = [placed([K_PASS], F32, f"a_scaled1{g}", (8 + 2 * g) * KIB) for g in range(3)]
         scaled1 = first_product(xq1, scaled1 + [sbuf([K_PASS], F32, "a_scaled13", "a_scaled03")])
         slope0 = placed([PACK, SLOTS], F32, "slope0", 0)
-        windows.append(placed([UNITS], F32, "window1", 14 * KIB))
-        nc.gpsimd.memset(windows[1][:], 0.0)
+        windows = [placed([UNITS], F32, "window0", 14 * KIB)]
+        nc.gpsimd.memset(windows[0][:], 0.0)
         times(slope0, th0, ALU.add, factor0)
         dh0 = [second_product(dyq0, q, 4 + q) for q in range(4)]
         a1 = turn(scaled1)
+        windows.append(placed([UNITS], F32, "window1", 22 * KIB))
+        nc.gpsimd.memset(windows[1][:], 0.0)
         times(slope0, sl0, ALU.subtract, slope0)
-        factor1 = outer([nc.gpsimd] * 3 + [nc.vector], 1, "silu0")
+        factor1 = outer(nc.gpsimd, 1, range(3), placed([3, SLOTS], F32, "factor1", 30 * KIB))
         da0 = sbuf([PACK * SLOTS], BF16, "da0")
         for q in range(4):
             finish(da0[:, q * K_PASS : (q + 1) * K_PASS], dh0[q], slope0, q)
+        last_factor = outer(nc.vector, 1, [3], placed([1, SLOTS], F32, "last_factor", 0))
         daq = [operand(SLOTS, f"daq{h}") for h in range(HALVES)]
         quantize(columns(daq[0], every), E5M2, da0[:])
 
         dyg1 = group(dy_raw[1], "dy_grouped1", nc.scalar.copy)
-        th1 = activation(a1, ACT.Tanh, us_col[:, 1, :], "tanh1", "dy_raw1")
-        sl1 = activation(a1, ACT.Silu, silu_scale[:, 1, :], "silu1", "us_col")
+        th1 = activation(a1, ACT.Tanh, us_col[:, 1, :], sbuf([PACK, SLOTS], F32, "tanh1", "dy_raw1"))
+        sl1 = activation(a1, ACT.Silu, silu_scale[:, 1, :], sbuf([PACK, SLOTS], F32, "silu1", "us_col"))
         dyq1 = quantize_whole(dyg1, E5M2, "dy1")
         windows.append(cleared("window2", "dy_grouped1"))
-        times(factor1, th1, ALU.add, factor1)
+        slope1 = sbuf([PACK, SLOTS], F32, "slope1", "factor0")
+        for rows, factor in ((slice(0, 2), factor1[:, 0:2, :]), (slice(2, 3), factor1[:, 2:3, :]), (slice(3, 4), last_factor[:])):
+            nc.vector.scalar_tensor_tensor(slope1[:, rows, :], th1[:, rows, :], 1.0, factor, ALU.add, ALU.mult)
         windows.append(cleared("window3", "dy_raw1"))
-        times(factor1, sl1, ALU.subtract, factor1)
+        times(slope1, sl1, ALU.subtract, slope1)
         xr1 = [turn_x(xg1, u, u, f"x_by_row1{u}") for u in range(2)]
+        xr0.append(turn_x(xg0, 1, 2, "x_by_row01"))
         da1 = [sbuf([PACK * SLOTS // 2], BF16, f"da1{part}") for part in range(2)]
         dh1 = [second_product(dyq1, q, 4 + q) for q in range(4)]
         xrq.append(operand(K_PASS, "xr1"))
         for q in range(3):
-            finish(da1[q // 2][:, q % 2 * K_PASS : (q % 2 + 1) * K_PASS], dh1[q], factor1, q)
+            finish(da1[q // 2][:, q % 2 * K_PASS : (q % 2 + 1) * K_PASS], dh1[q], slope1, q)
             if q == 1:
                 quantize(columns(xrq[1], parts[0]), E4M3, xr1[0][:])
         quantize(columns(daq[1], parts[0]), E5M2, da1[0][:])
@@ -310,7 +303,7 @@ def tile_attend_gffn_sil_kernel(
         out_rows = out.rearrange("(p j) n -> p j n", j=PACK)
         for j in range(2):
             scalar_scatter(windows[j], output_sums(j, (3, 0)[j], parts[0], nc.scalar.copy, f"dw{j}_early")[:], parts[0])
-        finish(da1[1][:, K_PASS:], dh1[3], factor1, 3)
+        finish(da1[1][:, K_PASS:], dh1[3], slope1, 3)
         quantize(columns(xrq[1], parts[1]), E4M3, xr1[1][:])
         quantize(columns(daq[1], parts[1]), E5M2, da1[1][:])
         late_codes = operand(2 * P, "xr01", "da10")

@@ -56,9 +56,9 @@ def tile_attend_gffn_sil_kernel(
             nc.sync.dma_start(table[:], words[0].rearrange("p n t -> p (n t)").bitcast(I32))
             return table
 
-        def load_plane(scales, name):
+        def load_plane(scales, name, engine):
             table = sbuf([UNITS // 4], I32, name)
-            nc.vector.memset(table[:], 0)
+            engine.memset(table[:], 0)
             for r in range(4):
                 nc.sync.dma_start(table[r:P:32, :], scales[0, r:16:4, :].bitcast(I32))
             return table
@@ -71,19 +71,19 @@ def tile_attend_gffn_sil_kernel(
 
         ts_table = sbuf([UNITS], F32, "ts_table")
         nc.scalar.dma_start(ts_table[P - 1 : P, :], ts[0:1, :])
+        nc.vector.memset(ts_table[0 : P - 1, :].bitcast(I32), 0)
         x_raw = [load_half(x_rows, 0, sbuf([PACK, K_PASS], F32, "x_raw0"))]
-        s1_table = load_plane(w1_scales, "s1_table")
+        s1_table = load_plane(w1_scales, "s1_table", nc.gpsimd)
         ident = sbuf([P], F32, "ident")
         make_identity(nc, ident[:])
         w1_table = load_words(w1_words, sbuf([UNITS], I32, "w1_table"))
         us_col = load_column(us, "us_col")
         wt_col = load_column(wt, "wt_col")
-        s2_table = load_plane(w2_scales, "s2_table")
-        nc.vector.memset(ts_table[0 : P - 1, :].bitcast(I32), 0)
+        s2_table = load_plane(w2_scales, "s2_table", nc.vector)
         x_raw.append(load_half(x_rows, 1, placed([PACK, K_PASS], F32, "x_raw1", 26 * KIB)))
         dy_raw = [load_half(dy_rows, 0, sbuf([PACK, K_PASS], F32, "dy_raw0"))]
         w2_table = load_words(w2_words, placed([UNITS], I32, "w2_table", 7 * KIB))
-        dy_raw.append(load_half(dy_rows, 1, sbuf([PACK, K_PASS], F32, "dy_raw1")))
+        dy_raw.append(load_half(dy_rows, 1, placed([PACK, K_PASS], F32, "dy_raw1", 38 * KIB)))
         warm = sbuf([2], F32, "warm")
         nc.vector.memset(warm[:, 0:1], 0.0)
         nc.scalar.activation(warm[:, 1:2], warm[:, 0:1], ACT.Silu)
@@ -260,19 +260,21 @@ def tile_attend_gffn_sil_kernel(
         da0 = sbuf([PACK * SLOTS], BF16, "da0")
         for q in range(4):
             finish(da0[:, q * K_PASS : (q + 1) * K_PASS], dh0[q], slope0, q)
-        last_factor = outer(nc.vector, 1, [3], placed([1, SLOTS], F32, "last_factor", 0))
         daq = [operand(SLOTS, f"daq{h}") for h in range(HALVES)]
         quantize(columns(daq[0], every), E5M2, da0[:])
 
         dyg1 = group(dy_raw[1], "dy_grouped1", nc.scalar.copy)
-        th1 = activation(a1, ACT.Tanh, us_col[:, 1, :], sbuf([PACK, SLOTS], F32, "tanh1", "dy_raw1"))
+        last_factor = placed([1, SLOTS], F32, "last_factor", 38 * KIB)
+        nc.scalar.activation(last_factor[:, 0, :], ts_all[:], ACT.Copy, scale=wu[:, 1, 3:4])
+        th1 = activation(a1, ACT.Tanh, us_col[:, 1, :], placed([PACK, SLOTS], F32, "tanh1", 40 * KIB))
         sl1 = activation(a1, ACT.Silu, silu_scale[:, 1, :], sbuf([PACK, SLOTS], F32, "silu1", "us_col"))
         dyq1 = quantize_whole(dyg1, E5M2, "dy1")
         windows.append(cleared("window2", "dy_grouped1"))
         slope1 = sbuf([PACK, SLOTS], F32, "slope1", "factor0")
         for rows, factor in ((slice(0, 2), factor1[:, 0:2, :]), (slice(2, 3), factor1[:, 2:3, :]), (slice(3, 4), last_factor[:])):
             nc.vector.scalar_tensor_tensor(slope1[:, rows, :], th1[:, rows, :], 1.0, factor, ALU.add, ALU.mult)
-        windows.append(cleared("window3", "dy_raw1"))
+        windows.append(placed([UNITS], F32, "window3", 40 * KIB))
+        nc.gpsimd.memset(windows[3][:], 0.0)
         times(slope1, sl1, ALU.subtract, slope1)
         xr1 = [turn_x(xg1, u, u, f"x_by_row1{u}") for u in range(2)]
         xr0.append(turn_x(xg0, 1, 2, "x_by_row01"))

@@ -80,13 +80,15 @@ def tile_attend_gffn_sil_kernel(
         us_col = load_column(us, "us_col")
         wt_col = load_column(wt, "wt_col")
         s2_table = load_plane(w2_scales, "s2_table", nc.vector)
+        warm = sbuf([2], F32, "warm")
+        nc.vector.memset(warm[:, 0:1], 0.0)
+        nc.scalar.activation(warm[:, 1:2], warm[:, 0:1], ACT.Silu)
+        windows = [sbuf([UNITS], F32, "window0")]
+        nc.vector.memset(windows[0][:].bitcast(I32), 0)
         x_raw.append(load_half(x_rows, 1, placed([PACK, K_PASS], F32, "x_raw1", 26 * KIB)))
         dy_raw = [load_half(dy_rows, 0, sbuf([PACK, K_PASS], F32, "dy_raw0"))]
         w2_table = load_words(w2_words, placed([UNITS], I32, "w2_table", 7 * KIB))
         dy_raw.append(load_half(dy_rows, 1, placed([PACK, K_PASS], F32, "dy_raw1", 38 * KIB)))
-        warm = sbuf([2], F32, "warm")
-        nc.vector.memset(warm[:, 0:1], 0.0)
-        nc.scalar.activation(warm[:, 1:2], warm[:, 0:1], ACT.Silu)
 
         def listed(table, cols):
             return table.indirect(offsets[:, cols.start // 16 : cols.stop // 16])
@@ -248,13 +250,11 @@ def tile_attend_gffn_sil_kernel(
         scaled1 = [placed([K_PASS], F32, f"a_scaled1{g}", (8 + 2 * g) * KIB) for g in range(3)]
         scaled1 = first_product(xq1, scaled1 + [sbuf([K_PASS], F32, "a_scaled13", "a_scaled03")])
         slope0 = placed([PACK, SLOTS], F32, "slope0", 0)
-        windows = [placed([UNITS], F32, "window0", 14 * KIB)]
-        nc.gpsimd.memset(windows[0][:], 0.0)
+        windows.append(placed([UNITS], F32, "window1", 14 * KIB))
+        nc.gpsimd.memset(windows[1][:], 0.0)
         times(slope0, th0, ALU.add, factor0)
         dh0 = [second_product(dyq0, q, 4 + q) for q in range(4)]
         a1 = turn(scaled1)
-        windows.append(placed([UNITS], F32, "window1", 22 * KIB))
-        nc.gpsimd.memset(windows[1][:], 0.0)
         times(slope0, sl0, ALU.subtract, slope0)
         factor1 = outer(nc.gpsimd, 1, range(3), placed([3, SLOTS], F32, "factor1", 30 * KIB))
         da0 = sbuf([PACK * SLOTS], BF16, "da0")

@@ -160,16 +160,16 @@ def tile_attend_gffn_sil_kernel(
             )
             return by_row
 
-        def first_product(xq, scaled):
-            sums = [bank(4 + g, "a_by_slot") for g in range(4)]
+        def first_product(xq, first_bank, scaled):
+            sums = [bank(first_bank + g, "a_by_slot") for g in range(4)]
             for g in range(4):
                 product(sums[g][:], columns(w1, block(g)), E4M3, columns(xq, every), E4M3)
             for g in range(4):
                 nc.scalar.activation(scaled[g][:], sums[g][:], ACT.Copy, scale=ts_col[:, g : g + 1])
             return scaled
 
-        def turn(scaled):
-            by_row = [bank(t, "a_by_row") for t in range(PACK)]
+        def turn(scaled, first_bank):
+            by_row = [bank(first_bank + t, "a_by_row") for t in range(PACK)]
             for g in range(4):
                 for t in range(PACK):
                     nc.tensor.transpose(by_row[t][:, block(g)], scaled[g][:, block(t)], ident[:])
@@ -233,7 +233,7 @@ def tile_attend_gffn_sil_kernel(
         silu_scale = sbuf([HALVES, PACK], F32, "silu_scale")
         nc.vector.scalar_tensor_tensor(wu[:], us_col, -1.0, wt_col, ALU.mult, ALU.mult)
         nc.vector.tensor_scalar(silu_scale[:], us_col, -2.0, 0.0, ALU.mult, ALU.add)
-        a0 = turn(first_product(xq0, [sbuf([K_PASS], F32, f"a_scaled0{g}") for g in range(4)]))
+        a0 = turn(first_product(xq0, 4, [sbuf([K_PASS], F32, f"a_scaled0{g}") for g in range(4)]), 0)
         factor0 = outer(nc.vector, 0, range(PACK), sbuf([PACK, SLOTS], F32, "factor0"))
         xrq = [operand(2 * P, "xr00", "w1_table")]
         quantize(columns(xrq[0], parts[0]), E4M3, xr0[0][:])
@@ -248,13 +248,13 @@ def tile_attend_gffn_sil_kernel(
         dyq0 = quantize_whole(dyg0, E5M2, "dy0")
         w2 = (gather(w2_table, U32, "w2", [every]), s2)
         scaled1 = [placed([K_PASS], F32, f"a_scaled1{g}", (8 + 2 * g) * KIB) for g in range(3)]
-        scaled1 = first_product(xq1, scaled1 + [sbuf([K_PASS], F32, "a_scaled13", "a_scaled03")])
+        scaled1 = first_product(xq1, 0, scaled1 + [sbuf([K_PASS], F32, "a_scaled13", "a_scaled03")])
         slope0 = placed([PACK, SLOTS], F32, "slope0", 0)
         windows.append(placed([UNITS], F32, "window1", 14 * KIB))
         nc.gpsimd.memset(windows[1][:], 0.0)
         times(slope0, th0, ALU.add, factor0)
-        dh0 = [second_product(dyq0, q, 4 + q) for q in range(4)]
-        a1 = turn(scaled1)
+        dh0 = [second_product(dyq0, q, q) for q in range(4)]
+        a1 = turn(scaled1, 4)
         times(slope0, sl0, ALU.subtract, slope0)
         factor1 = outer(nc.gpsimd, 1, range(3), placed([3, SLOTS], F32, "factor1", 30 * KIB))
         da0 = sbuf([PACK * SLOTS], BF16, "da0")
@@ -276,10 +276,10 @@ def tile_attend_gffn_sil_kernel(
         windows.append(placed([UNITS], F32, "window3", 40 * KIB))
         nc.gpsimd.memset(windows[3][:], 0.0)
         times(slope1, sl1, ALU.subtract, slope1)
-        xr1 = [turn_x(xg1, u, u, f"x_by_row1{u}") for u in range(2)]
-        xr0.append(turn_x(xg0, 1, 2, "x_by_row01"))
+        xr1 = [turn_x(xg1, u, 4 + u, f"x_by_row1{u}") for u in range(2)]
+        xr0.append(turn_x(xg0, 1, 6, "x_by_row01"))
         da1 = [sbuf([PACK * SLOTS // 2], BF16, f"da1{part}") for part in range(2)]
-        dh1 = [second_product(dyq1, q, 4 + q) for q in range(4)]
+        dh1 = [second_product(dyq1, q, q) for q in range(4)]
         xrq.append(operand(K_PASS, "xr1"))
         for q in range(3):
             finish(da1[q // 2][:, q % 2 * K_PASS : (q % 2 + 1) * K_PASS], dh1[q], slope1, q)
@@ -304,22 +304,22 @@ def tile_attend_gffn_sil_kernel(
 
         out_rows = out.rearrange("(p j) n -> p j n", j=PACK)
         for j in range(2):
-            scalar_scatter(windows[j], output_sums(j, (3, 0)[j], parts[0], nc.scalar.copy, f"dw{j}_early")[:], parts[0])
+            scalar_scatter(windows[j], output_sums(j, (7, 4)[j], parts[0], nc.scalar.copy, f"dw{j}_early")[:], parts[0])
         finish(da1[1][:, K_PASS:], dh1[3], slope1, 3)
         quantize(columns(xrq[1], parts[1]), E4M3, xr1[1][:])
         quantize(columns(daq[1], parts[1]), E5M2, da1[1][:])
         late_codes = operand(2 * P, "xr01", "da10")
         quantize(columns(late_codes, parts[0]), E4M3, xr0[1][:])
-        late0 = output_sums(0, 4, parts[1], nc.vector.tensor_copy, "dw0_late")
-        late1 = output_sums(1, 5, parts[1], nc.scalar.copy, "dw1_late")
+        late0 = output_sums(0, 0, parts[1], nc.vector.tensor_copy, "dw0_late")
+        late1 = output_sums(1, 1, parts[1], nc.scalar.copy, "dw1_late")
         nc.vector.tensor_copy(listed(windows[0][:], parts[1]), late0[:])
         nc.sync.dma_start(out_rows[:, 0, :], windows[0][:])
         scalar_scatter(windows[1], late1[:], parts[1])
         nc.scalar.dma_start(out_rows[:, 1, :], windows[1][:])
-        sums2 = output_sums(2, 6, every, nc.vector.tensor_copy, "dw2", "dw0_late_sb")
+        sums2 = output_sums(2, 2, every, nc.vector.tensor_copy, "dw2", "dw0_late_sb")
         nc.vector.tensor_copy(listed(windows[2][:], every), sums2[:])
         nc.sync.dma_start(out_rows[:, 2, :], windows[2][:])
-        sums3 = output_sums(3, 1, every, nc.scalar.copy, "dw3", "dw1_late_sb")
+        sums3 = output_sums(3, 5, every, nc.scalar.copy, "dw3", "dw1_late_sb")
         for cols in parts:
             scalar_scatter(windows[3], sums3[:, cols], cols)
         nc.scalar.dma_start(out_rows[:, 3, :], windows[3][:])

@@ -85,10 +85,10 @@ def tile_attend_gffn_sil_kernel(
         nc.scalar.activation(warm[:, 1:2], warm[:, 0:1], ACT.Silu)
         windows = [sbuf([UNITS], F32, "window0")]
         nc.vector.memset(windows[0][:].bitcast(I32), 0)
-        x_raw.append(load_half(x_rows, 1, placed([PACK, K_PASS], F32, "x_raw1", 26 * KIB)))
-        dy_raw = [load_half(dy_rows, 0, sbuf([PACK, K_PASS], F32, "dy_raw0"))]
-        w2_table = load_words(w2_words, placed([UNITS], I32, "w2_table", 7 * KIB))
-        dy_raw.append(load_half(dy_rows, 1, placed([PACK, K_PASS], F32, "dy_raw1", 38 * KIB)))
+        x_raw.append(load_half(x_rows, 1, sbuf([PACK, K_PASS], F32, "x_raw1")))
+        dy_raw = [load_half(dy_rows, 0, placed([PACK, K_PASS], F32, "dy_raw0", 33 * KIB))]
+        w2_table = load_words(w2_words, placed([UNITS], I32, "w2_table", 20 * KIB))
+        dy_raw.append(load_half(dy_rows, 1, placed([PACK, K_PASS], F32, "dy_raw1", 48 * KIB)))
 
         def listed(table, cols):
             return table.indirect(offsets[:, cols.start // 16 : cols.stop // 16])
@@ -165,7 +165,7 @@ def tile_attend_gffn_sil_kernel(
             for g in range(4):
                 product(sums[g][:], columns(w1, block(g)), E4M3, columns(xq, every), E4M3)
             for g in range(4):
-                nc.scalar.activation(scaled[g][:], sums[g][:], ACT.Copy, scale=ts_col[:, g : g + 1])
+                nc.scalar.activation(scaled[g], sums[g][:], ACT.Copy, scale=ts_col[:, g : g + 1])
             return scaled
 
         def turn(scaled, first_bank):
@@ -233,30 +233,34 @@ def tile_attend_gffn_sil_kernel(
         silu_scale = sbuf([HALVES, PACK], F32, "silu_scale")
         nc.vector.scalar_tensor_tensor(wu[:], us_col, -1.0, wt_col, ALU.mult, ALU.mult)
         nc.vector.tensor_scalar(silu_scale[:], us_col, -2.0, 0.0, ALU.mult, ALU.add)
-        a0 = turn(first_product(xq0, 4, [sbuf([K_PASS], F32, f"a_scaled0{g}") for g in range(4)]), 0)
+        a0 = turn(first_product(xq0, 4, [sbuf([K_PASS], F32, f"a_scaled0{g}")[:] for g in range(4)]), 0)
         factor0 = outer(nc.vector, 0, range(PACK), sbuf([PACK, SLOTS], F32, "factor0"))
         xrq = [operand(2 * P, "xr00", "w1_table")]
         quantize(columns(xrq[0], parts[0]), E4M3, xr0[0][:])
         s2 = gather(s2_table, U8, "s2", [every])
-        xg1 = [sbuf([2 * K_PASS], BF16, f"x_grouped1{pair}")[:] for pair in range(2)]
-        group_pair(xg1[0], x_raw[1], 0, nc.scalar.copy)
-        group_pair(xg1[1], x_raw[1], 1, nc.vector.tensor_copy)
-        th0 = activation(a0, ACT.Tanh, us_col[:, 0, :], placed([PACK, SLOTS], F32, "tanh0", 22 * KIB))
-        sl0 = activation(a0, ACT.Silu, silu_scale[:, 0, :], placed([PACK, SLOTS], F32, "silu0", 30 * KIB))
-        dyg0 = group(dy_raw[0], "dy_grouped0", nc.vector.tensor_copy)
-        xq1 = quantize_pairs(xg1, E4M3, "x1", "dy_raw0")
-        dyq0 = quantize_whole(dyg0, E5M2, "dy0")
+        th0 = activation(a0, ACT.Tanh, us_col[:, 0, :], sbuf([PACK, SLOTS], F32, "tanh0"))
+        grouped = group(x_raw[1], "x_grouped1", nc.vector.tensor_copy)
+        xg1 = [grouped[:, pair, :] for pair in range(2)]
+        xq1 = quantize_whole(grouped, E4M3, "x1")
+        dyg0 = [placed([2 * K_PASS], BF16, "dy_grouped00", 7 * KIB)[:], sbuf([2 * K_PASS], BF16, "dy_grouped01")[:]]
+        group_pair(dyg0[0], dy_raw[0], 0, nc.vector.tensor_copy)
+        group_pair(dyg0[1], dy_raw[0], 1, nc.scalar.copy)
+        sl0 = activation(a0, ACT.Silu, silu_scale[:, 0, :], placed([PACK, SLOTS], F32, "silu0", 32 * KIB))
+        scaled_sums = placed([PACK, K_PASS], F32, "a_scaled1", 40 * KIB)
+        scaled1 = first_product(xq1, 0, [scaled_sums[:, g, :] for g in range(4)])
+        dyq0 = operand(K_PASS, "dy0")
+        quantize(columns(dyq0, parts[0]), E5M2, dyg0[0])
+        sigmoid0 = placed([PACK, SLOTS], F32, "sigmoid0", 0)
+        times(sigmoid0, th0, ALU.add, factor0)
+        quantize(columns(dyq0, parts[1]), E5M2, dyg0[1])
         w2 = (gather(w2_table, U32, "w2", [every]), s2)
-        scaled1 = [placed([K_PASS], F32, f"a_scaled1{g}", (8 + 2 * g) * KIB) for g in range(3)]
-        scaled1 = first_product(xq1, 0, scaled1 + [sbuf([K_PASS], F32, "a_scaled13", "a_scaled03")])
-        slope0 = placed([PACK, SLOTS], F32, "slope0", 0)
-        windows.append(placed([UNITS], F32, "window1", 14 * KIB))
-        nc.gpsimd.memset(windows[1][:], 0.0)
-        times(slope0, th0, ALU.add, factor0)
         dh0 = [second_product(dyq0, q, q) for q in range(4)]
         a1 = turn(scaled1, 4)
-        times(slope0, sl0, ALU.subtract, slope0)
-        factor1 = outer(nc.gpsimd, 1, range(3), placed([3, SLOTS], F32, "factor1", 30 * KIB))
+        slope0 = placed([PACK, SLOTS], F32, "slope0", 16 * KIB)
+        windows.append(placed([UNITS], F32, "window1", 24 * KIB))
+        nc.gpsimd.memset(windows[1][:], 0.0)
+        times(slope0, sl0, ALU.subtract, sigmoid0)
+        factor1 = outer(nc.gpsimd, 1, range(3), placed([3, SLOTS], F32, "factor1", 32 * KIB))
         da0 = sbuf([PACK * SLOTS], BF16, "da0")
         for q in range(4):
             finish(da0[:, q * K_PASS : (q + 1) * K_PASS], dh0[q], slope0, q)
@@ -264,16 +268,16 @@ def tile_attend_gffn_sil_kernel(
         quantize(columns(daq[0], every), E5M2, da0[:])
 
         dyg1 = group(dy_raw[1], "dy_grouped1", nc.scalar.copy)
-        last_factor = placed([1, SLOTS], F32, "last_factor", 38 * KIB)
+        last_factor = placed([1, SLOTS], F32, "last_factor", 48 * KIB)
         nc.scalar.activation(last_factor[:, 0, :], ts_all[:], ACT.Copy, scale=wu[:, 1, 3:4])
-        th1 = activation(a1, ACT.Tanh, us_col[:, 1, :], placed([PACK, SLOTS], F32, "tanh1", 40 * KIB))
+        th1 = activation(a1, ACT.Tanh, us_col[:, 1, :], placed([PACK, SLOTS], F32, "tanh1", 50 * KIB))
         sl1 = activation(a1, ACT.Silu, silu_scale[:, 1, :], sbuf([PACK, SLOTS], F32, "silu1", "us_col"))
         dyq1 = quantize_whole(dyg1, E5M2, "dy1")
         windows.append(cleared("window2", "dy_grouped1"))
         slope1 = sbuf([PACK, SLOTS], F32, "slope1", "factor0")
         for rows, factor in ((slice(0, 2), factor1[:, 0:2, :]), (slice(2, 3), factor1[:, 2:3, :]), (slice(3, 4), last_factor[:])):
             nc.vector.scalar_tensor_tensor(slope1[:, rows, :], th1[:, rows, :], 1.0, factor, ALU.add, ALU.mult)
-        windows.append(placed([UNITS], F32, "window3", 40 * KIB))
+        windows.append(placed([UNITS], F32, "window3", 50 * KIB))
         nc.gpsimd.memset(windows[3][:], 0.0)
         times(slope1, sl1, ALU.subtract, slope1)
         xr1 = [turn_x(xg1, u, 4 + u, f"x_by_row1{u}") for u in range(2)]

@@ -56,39 +56,38 @@ def tile_attend_gffn_sil_kernel(
             nc.sync.dma_start(table[:], words[0].rearrange("p n t -> p (n t)").bitcast(I32))
             return table
 
-        def load_plane(scales, name, engine):
+        def load_scales(scales, name, engine):
             table = sbuf([UNITS // 4], I32, name)
-            engine.memset(table[:], 0)
-            for r in range(4):
-                nc.sync.dma_start(table[r:P:32, :], scales[0, r:16:4, :].bitcast(I32))
+            nc.sync.dma_start(table[P - 16 : P, :], scales[0].bitcast(I32))
+            engine.memset(table[0 : P - 16, :], 0)
             return table
+
+        def place_scales(rows, plane):
+            for q in range(4):
+                source = rows[P - 16 + 4 * q : P - 12 + 4 * q, :]
+                nc.sync.dma_start(plane[32 * q : 32 * q + 4, :].bitcast(I32), source.bitcast(I32))
+            return plane
 
         def load_column(vector, name):
             padded = sbuf([HALVES, 2 * PACK], F32, name)
             column = padded[:, :, 0:PACK]
-            nc.sync.dma_start(column, vector.rearrange("(h p t) o -> p h (t o)", h=HALVES, t=PACK))
+            nc.scalar.dma_start(column, vector.rearrange("(h p t) o -> p h (t o)", h=HALVES, t=PACK))
             return column
 
+        us_col = load_column(us, "us_col")
+        wt_col = load_column(wt, "wt_col")
         ts_table = sbuf([UNITS], F32, "ts_table")
         nc.scalar.dma_start(ts_table[P - 1 : P, :], ts[0:1, :])
         nc.vector.memset(ts_table[0 : P - 1, :].bitcast(I32), 0)
-        x_raw = [load_half(x_rows, 0, sbuf([PACK, K_PASS], F32, "x_raw0"))]
-        s1_table = load_plane(w1_scales, "s1_table", nc.gpsimd)
+        s1_table = load_scales(w1_scales, "s1_table", nc.gpsimd)
         ident = sbuf([P], F32, "ident")
         make_identity(nc, ident[:])
+        s2_table = load_scales(w2_scales, "s2_table", nc.vector)
+        x_raw = [load_half(x_rows, 0, sbuf([PACK, K_PASS], F32, "x_raw0"))]
         w1_table = load_words(w1_words, sbuf([UNITS], I32, "w1_table"))
-        us_col = load_column(us, "us_col")
-        wt_col = load_column(wt, "wt_col")
-        s2_table = load_plane(w2_scales, "s2_table", nc.vector)
         warm = sbuf([2], F32, "warm")
         nc.vector.memset(warm[:, 0:1], 0.0)
         nc.scalar.activation(warm[:, 1:2], warm[:, 0:1], ACT.Silu)
-        windows = [sbuf([UNITS], F32, "window0")]
-        nc.vector.memset(windows[0][:].bitcast(I32), 0)
-        x_raw.append(load_half(x_rows, 1, sbuf([PACK, K_PASS], F32, "x_raw1")))
-        dy_raw = [load_half(dy_rows, 0, placed([PACK, K_PASS], F32, "dy_raw0", 33 * KIB))]
-        w2_table = load_words(w2_words, placed([UNITS], I32, "w2_table", 20 * KIB))
-        dy_raw.append(load_half(dy_rows, 1, placed([PACK, K_PASS], F32, "dy_raw1", 48 * KIB)))
 
         def listed(table, cols):
             return table.indirect(offsets[:, cols.start // 16 : cols.stop // 16])
@@ -108,8 +107,7 @@ def tile_attend_gffn_sil_kernel(
                 raw[:].rearrange("p j (s t) -> p s j t", t=PACK)[:, :, :, 2 * pair : 2 * pair + 2],
             )
 
-        def group(raw, name, copy):
-            grouped = sbuf([2, 2 * K_PASS], BF16, name)
+        def group(raw, grouped, copy):
             for pair in range(2):
                 group_pair(grouped[:, pair, :], raw, pair, copy)
             return grouped
@@ -222,37 +220,40 @@ def tile_attend_gffn_sil_kernel(
         ts_all = sbuf([SLOTS], F32, "ts_all")
         nc.scalar.copy(ts_all[:], spread[:])
 
-        xg0 = [sbuf([2 * K_PASS], BF16, f"x_grouped0{pair}")[:] for pair in range(2)]
-        group_pair(xg0[0], x_raw[0], 0, nc.vector.tensor_copy)
-        group_pair(xg0[1], x_raw[0], 1, nc.scalar.copy)
-        s1 = gather(s1_table, U8, "s1", [every])
-        xq0 = quantize_pairs(xg0, E4M3, "x0")
-        xr0 = [turn_x(xg0, 0, 2, "x_by_row00")]
-        w1 = (gather(w1_table, U32, "w1", parts), s1)
+        s1 = place_scales(gather(s1_table, U8, "s1_rows", [every]), sbuf([SLOTS], U8, "s1"))
+        s2_rows = gather(s2_table, U8, "s2_rows", [every])
+        x_raw.append(load_half(x_rows, 1, sbuf([PACK, K_PASS], F32, "x_raw1")))
+        dy_raw = [load_half(dy_rows, 0, sbuf([PACK, K_PASS], F32, "dy_raw0"))]
+        s2 = place_scales(s2_rows, sbuf([SLOTS], U8, "s2", "x_raw1"))
+        w2_table = load_words(w2_words, placed([UNITS], I32, "w2_table", 20 * KIB))
+        dy_raw.append(load_half(dy_rows, 1, placed([PACK, K_PASS], F32, "dy_raw1", 48 * KIB)))
         wu = sbuf([HALVES, PACK], F32, "wu")
         silu_scale = sbuf([HALVES, PACK], F32, "silu_scale")
         nc.vector.scalar_tensor_tensor(wu[:], us_col, -1.0, wt_col, ALU.mult, ALU.mult)
         nc.vector.tensor_scalar(silu_scale[:], us_col, -2.0, 0.0, ALU.mult, ALU.add)
-        a0 = turn(first_product(xq0, 4, [sbuf([K_PASS], F32, f"a_scaled0{g}")[:] for g in range(4)]), 0)
+        xg0 = [sbuf([2 * K_PASS], BF16, f"x_grouped0{pair}")[:] for pair in range(2)]
+        group_pair(xg0[0], x_raw[0], 0, nc.vector.tensor_copy)
+        group_pair(xg0[1], x_raw[0], 1, nc.scalar.copy)
+        xq0 = quantize_pairs(xg0, E4M3, "x0")
+        xr0 = [turn_x(xg0, 0, 2, "x_by_row00")]
         factor0 = outer(nc.vector, 0, range(PACK), sbuf([PACK, SLOTS], F32, "factor0"))
+        w1 = (gather(w1_table, U32, "w1", parts), s1)
+        a0 = turn(first_product(xq0, 4, [sbuf([K_PASS], F32, f"a_scaled0{g}")[:] for g in range(4)]), 0)
         xrq = [operand(2 * P, "xr00", "w1_table")]
         quantize(columns(xrq[0], parts[0]), E4M3, xr0[0][:])
-        s2 = gather(s2_table, U8, "s2", [every])
         th0 = activation(a0, ACT.Tanh, us_col[:, 0, :], sbuf([PACK, SLOTS], F32, "tanh0"))
-        grouped = group(x_raw[1], "x_grouped1", nc.vector.tensor_copy)
+        grouped = group(x_raw[1], sbuf([2, 2 * K_PASS], BF16, "x_grouped1"), nc.vector.tensor_copy)
         xg1 = [grouped[:, pair, :] for pair in range(2)]
         xq1 = quantize_whole(grouped, E4M3, "x1")
-        dyg0 = [placed([2 * K_PASS], BF16, "dy_grouped00", 7 * KIB)[:], sbuf([2 * K_PASS], BF16, "dy_grouped01")[:]]
-        group_pair(dyg0[0], dy_raw[0], 0, nc.vector.tensor_copy)
-        group_pair(dyg0[1], dy_raw[0], 1, nc.scalar.copy)
         sl0 = activation(a0, ACT.Silu, silu_scale[:, 0, :], placed([PACK, SLOTS], F32, "silu0", 32 * KIB))
         scaled_sums = placed([PACK, K_PASS], F32, "a_scaled1", 40 * KIB)
         scaled1 = first_product(xq1, 0, [scaled_sums[:, g, :] for g in range(4)])
-        dyq0 = operand(K_PASS, "dy0")
-        quantize(columns(dyq0, parts[0]), E5M2, dyg0[0])
+        dyg0 = group(dy_raw[0], placed([2, 2 * K_PASS], BF16, "dy_grouped0", 6 * KIB), nc.vector.tensor_copy)
+        dyq0 = quantize_whole(dyg0, E5M2, "dy0")
         sigmoid0 = placed([PACK, SLOTS], F32, "sigmoid0", 0)
+        windows = [placed([UNITS], F32, "window0", 8 * KIB)]
+        nc.gpsimd.memset(windows[0][:], 0.0)
         times(sigmoid0, th0, ALU.add, factor0)
-        quantize(columns(dyq0, parts[1]), E5M2, dyg0[1])
         w2 = (gather(w2_table, U32, "w2", [every]), s2)
         dh0 = [second_product(dyq0, q, q) for q in range(4)]
         a1 = turn(scaled1, 4)
@@ -267,7 +268,7 @@ def tile_attend_gffn_sil_kernel(
         daq = [operand(SLOTS, f"daq{h}") for h in range(HALVES)]
         quantize(columns(daq[0], every), E5M2, da0[:])
 
-        dyg1 = group(dy_raw[1], "dy_grouped1", nc.scalar.copy)
+        dyg1 = group(dy_raw[1], sbuf([2, 2 * K_PASS], BF16, "dy_grouped1"), nc.scalar.copy)
         last_factor = placed([1, SLOTS], F32, "last_factor", 48 * KIB)
         nc.scalar.activation(last_factor[:, 0, :], ts_all[:], ACT.Copy, scale=wu[:, 1, 3:4])
         th1 = activation(a1, ACT.Tanh, us_col[:, 1, :], placed([PACK, SLOTS], F32, "tanh1", 50 * KIB))

@@ -184,9 +184,15 @@ def tile_attend_gffn_sil_kernel(
             return factor
 
         def times(result, values, op, factor):
-            for pair in range(2):
-                rows = slice(2 * pair, 2 * pair + 2)
-                nc.vector.scalar_tensor_tensor(result[:, rows, :], values[:, rows, :], 1.0, factor[:, rows, :], op, ALU.mult)
+            nc.vector.scalar_tensor_tensor(result, values, 1.0, factor, op, ALU.mult)
+
+        def times_by_slots(result, values, op, factor):
+            for cols in parts:
+                times(result[:, :, cols], values[:, :, cols], op, factor[:, :, cols])
+
+        def times_silu(result, values, factor):
+            times(result[:, 0:2, :], values[:, 0:2, :], ALU.subtract, factor[:, 0:2, :])
+            times_by_slots(result[:, 2:4, :], values[:, 2:4, :], ALU.subtract, factor[:, 2:4, :])
 
         def second_product(dyq, q, n):
             dh = bank(n, "dh")
@@ -244,29 +250,28 @@ def tile_attend_gffn_sil_kernel(
         th0 = activation(a0, ACT.Tanh, us_col[:, 0, :], sbuf([PACK, SLOTS], F32, "tanh0"))
         grouped = group(x_raw[1], sbuf([2, 2 * K_PASS], BF16, "x_grouped1"), nc.vector.tensor_copy)
         xg1 = [grouped[:, pair, :] for pair in range(2)]
-        xq1 = quantize_whole(grouped, E4M3, "x1")
+        xq1 = quantize_pairs(xg1, E4M3, "x1")
         sl0 = activation(a0, ACT.Silu, silu_scale[:, 0, :], placed([PACK, SLOTS], F32, "silu0", 32 * KIB))
         scaled_sums = placed([PACK, K_PASS], F32, "a_scaled1", 40 * KIB)
         scaled1 = first_product(xq1, 0, [scaled_sums[:, g, :] for g in range(4)])
         dyg0 = group(dy_raw[0], placed([2, 2 * K_PASS], BF16, "dy_grouped0", 6 * KIB), nc.vector.tensor_copy)
-        dyq0 = quantize_whole(dyg0, E5M2, "dy0")
+        dyq0 = quantize_pairs([dyg0[:, pair, :] for pair in range(2)], E5M2, "dy0")
         sigmoid0 = placed([PACK, SLOTS], F32, "sigmoid0", 0)
         windows = [placed([UNITS], F32, "window0", 8 * KIB)]
         nc.gpsimd.memset(windows[0][:], 0.0)
-        times(sigmoid0, th0, ALU.add, factor0)
+        for rows in (slice(0, 2), slice(2, 4)):
+            times(sigmoid0[:, rows, :], th0[:, rows, :], ALU.add, factor0[:, rows, :])
         w2 = (gather(w2_table, U32, "w2", [every]), s2)
         dh0 = [second_product(dyq0, q, q) for q in range(4)]
         a1 = turn(scaled1, 4)
         slope0 = placed([PACK, SLOTS], F32, "slope0", 16 * KIB)
         windows.append(placed([UNITS], F32, "window1", 24 * KIB))
         nc.gpsimd.memset(windows[1][:], 0.0)
-        times(slope0, sl0, ALU.subtract, sigmoid0)
+        times_silu(slope0, sl0, sigmoid0)
         factor1 = outer(nc.gpsimd, 1, range(3), placed([3, SLOTS], F32, "factor1", 32 * KIB))
         da0 = sbuf([PACK * SLOTS], BF16, "da0")
         for q in range(4):
             finish(da0[:, q * K_PASS : (q + 1) * K_PASS], dh0[q], slope0, q)
-        daq = [operand(SLOTS, f"daq{h}") for h in range(HALVES)]
-        quantize(columns(daq[0], every), E5M2, da0[:])
 
         dyg1 = group(dy_raw[1], sbuf([2, 2 * K_PASS], BF16, "dy_grouped1"), nc.scalar.copy)
         last_factor = placed([1, SLOTS], F32, "last_factor", 48 * KIB)
@@ -274,26 +279,27 @@ def tile_attend_gffn_sil_kernel(
         th1 = activation(a1, ACT.Tanh, us_col[:, 1, :], placed([PACK, SLOTS], F32, "tanh1", 50 * KIB))
         sl1 = activation(a1, ACT.Silu, silu_scale[:, 1, :], sbuf([PACK, SLOTS], F32, "silu1", "us_col"))
         dyq1 = quantize_whole(dyg1, E5M2, "dy1")
-        windows.append(cleared("window2", "dy_grouped1"))
+        daq = [operand(SLOTS, "daq0", "dy_grouped1"), operand(SLOTS, "daq1")]
+        quantize(columns(daq[0], every), E5M2, da0[:])
+        windows.append(cleared("window2", "da0"))
         slope1 = sbuf([PACK, SLOTS], F32, "slope1", "factor0")
         for rows, factor in ((slice(0, 2), factor1[:, 0:2, :]), (slice(2, 3), factor1[:, 2:3, :]), (slice(3, 4), last_factor[:])):
-            nc.vector.scalar_tensor_tensor(slope1[:, rows, :], th1[:, rows, :], 1.0, factor, ALU.add, ALU.mult)
+            times(slope1[:, rows, :], th1[:, rows, :], ALU.add, factor)
         windows.append(placed([UNITS], F32, "window3", 50 * KIB))
         nc.gpsimd.memset(windows[3][:], 0.0)
-        times(slope1, sl1, ALU.subtract, slope1)
+        times_silu(slope1, sl1, slope1)
         xr1 = [turn_x(xg1, u, 4 + u, f"x_by_row1{u}") for u in range(2)]
         xr0.append(turn_x(xg0, 1, 6, "x_by_row01"))
         da1 = [sbuf([PACK * SLOTS // 2], BF16, f"da1{part}") for part in range(2)]
         dh1 = [second_product(dyq1, q, q) for q in range(4)]
-        xrq.append(operand(K_PASS, "xr1"))
-        for q in range(3):
-            finish(da1[q // 2][:, q % 2 * K_PASS : (q % 2 + 1) * K_PASS], dh1[q], slope1, q)
-            if q == 1:
-                quantize(columns(xrq[1], parts[0]), E4M3, xr1[0][:])
+        xrq.append(operand(2 * P, "xr10"))
+        for q in range(2):
+            finish(da1[0][:, q * K_PASS : (q + 1) * K_PASS], dh1[q], slope1, q)
+        quantize(columns(xrq[1], parts[0]), E4M3, xr1[0][:])
         quantize(columns(daq[1], parts[0]), E5M2, da1[0][:])
 
         def turned_x(h, j):
-            return columns(late_codes, block(j - 2)) if h == 0 and j >= 2 else columns(xrq[h], block(j))
+            return columns(late_codes[h], block(j - 2)) if j >= 2 else columns(xrq[h], block(j))
 
         def output_sums(j, n, cols, copy, name, tag=None):
             width = cols.stop - cols.start
@@ -310,11 +316,13 @@ def tile_attend_gffn_sil_kernel(
         out_rows = out.rearrange("(p j) n -> p j n", j=PACK)
         for j in range(2):
             scalar_scatter(windows[j], output_sums(j, (7, 4)[j], parts[0], nc.scalar.copy, f"dw{j}_early")[:], parts[0])
-        finish(da1[1][:, K_PASS:], dh1[3], slope1, 3)
-        quantize(columns(xrq[1], parts[1]), E4M3, xr1[1][:])
-        quantize(columns(daq[1], parts[1]), E5M2, da1[1][:])
-        late_codes = operand(2 * P, "xr01", "da10")
-        quantize(columns(late_codes, parts[0]), E4M3, xr0[1][:])
+        for q in range(2, 4):
+            finish(da1[1][:, q % 2 * K_PASS : (q % 2 + 1) * K_PASS], dh1[q], slope1, q)
+        for q in range(2, 4):
+            quantize(columns(daq[1], block(q)), E5M2, da1[1][:, q % 2 * K_PASS : (q % 2 + 1) * K_PASS])
+        late_codes = [operand(2 * P, f"xr{h}1", "da11" if h == 0 else None) for h in range(HALVES)]
+        for h, by_row in enumerate((xr0, xr1)):
+            quantize(columns(late_codes[h], parts[0]), E4M3, by_row[1][:])
         late0 = output_sums(0, 0, parts[1], nc.vector.tensor_copy, "dw0_late")
         late1 = output_sums(1, 1, parts[1], nc.scalar.copy, "dw1_late")
         nc.vector.tensor_copy(listed(windows[0][:], parts[1]), late0[:])

@@ -74,17 +74,17 @@ def tile_attend_gffn_sil_kernel(
             nc.scalar.dma_start(column, vector.rearrange("(h p t) o -> p h (t o)", h=HALVES, t=PACK))
             return column
 
-        us_col = load_column(us, "us_col")
-        wt_col = load_column(wt, "wt_col")
         ts_table = sbuf([UNITS], F32, "ts_table")
         nc.scalar.dma_start(ts_table[P - 1 : P, :], ts[0:1, :])
+        us_col = load_column(us, "us_col")
+        wt_col = load_column(wt, "wt_col")
         nc.vector.memset(ts_table[0 : P - 1, :].bitcast(I32), 0)
         s1_table = load_scales(w1_scales, "s1_table", nc.gpsimd)
         ident = sbuf([P], F32, "ident")
         make_identity(nc, ident[:])
         s2_table = load_scales(w2_scales, "s2_table", nc.vector)
         x_raw = [load_half(x_rows, 0, sbuf([PACK, K_PASS], F32, "x_raw0"))]
-        w1_table = load_words(w1_words, sbuf([UNITS], I32, "w1_table"))
+        w1_table = load_words(w1_words, placed([UNITS], I32, "w1_table", 58 * KIB))
         warm = sbuf([2], F32, "warm")
         nc.vector.memset(warm[:, 0:1], 0.0)
         nc.scalar.activation(warm[:, 1:2], warm[:, 0:1], ACT.Silu)
@@ -242,11 +242,14 @@ def tile_attend_gffn_sil_kernel(
         group_pair(xg0[1], x_raw[0], 1, nc.scalar.copy)
         xq0 = quantize_pairs(xg0, E4M3, "x0")
         xr0 = [turn_x(xg0, 0, 2, "x_by_row00")]
-        factor0 = outer(nc.vector, 0, range(PACK), sbuf([PACK, SLOTS], F32, "factor0"))
+        factor0 = [outer(nc.vector, 0, range(2), sbuf([2, SLOTS], F32, "factor00"))]
         w1 = (gather(w1_table, U32, "w1", parts), s1)
         a0 = turn(first_product(xq0, 4, [sbuf([K_PASS], F32, f"a_scaled0{g}")[:] for g in range(4)]), 0)
-        xrq = [operand(2 * P, "xr00", "w1_table")]
+        factor0.append(outer(nc.vector, 0, range(2, 4), placed([2, SLOTS], F32, "factor01", 58 * KIB)))
+        xrq = [(placed([2 * P], U32, "xr00_codes", 62 * KIB), sbuf([2 * P], U8, "xr00_scales"))]
         quantize(columns(xrq[0], parts[0]), E4M3, xr0[0][:])
+        last_factor = sbuf([1, SLOTS], F32, "last_factor", "a_scaled00")
+        nc.scalar.activation(last_factor[:, 0, :], ts_all[:], ACT.Copy, scale=wu[:, 1, 3:4])
         th0 = activation(a0, ACT.Tanh, us_col[:, 0, :], sbuf([PACK, SLOTS], F32, "tanh0"))
         grouped = group(x_raw[1], sbuf([2, 2 * K_PASS], BF16, "x_grouped1"), nc.vector.tensor_copy)
         xg1 = [grouped[:, pair, :] for pair in range(2)]
@@ -259,8 +262,9 @@ def tile_attend_gffn_sil_kernel(
         sigmoid0 = placed([PACK, SLOTS], F32, "sigmoid0", 0)
         windows = [placed([UNITS], F32, "window0", 8 * KIB)]
         nc.gpsimd.memset(windows[0][:], 0.0)
-        for rows in (slice(0, 2), slice(2, 4)):
-            times(sigmoid0[:, rows, :], th0[:, rows, :], ALU.add, factor0[:, rows, :])
+        for pair in range(2):
+            rows = slice(2 * pair, 2 * pair + 2)
+            times(sigmoid0[:, rows, :], th0[:, rows, :], ALU.add, factor0[pair][:])
         w2 = (gather(w2_table, U32, "w2", [every]), s2)
         dh0 = [second_product(dyq0, q, q) for q in range(4)]
         a1 = turn(scaled1, 4)
@@ -274,15 +278,13 @@ def tile_attend_gffn_sil_kernel(
             finish(da0[:, q * K_PASS : (q + 1) * K_PASS], dh0[q], slope0, q)
 
         dyg1 = group(dy_raw[1], sbuf([2, 2 * K_PASS], BF16, "dy_grouped1"), nc.scalar.copy)
-        last_factor = placed([1, SLOTS], F32, "last_factor", 48 * KIB)
-        nc.scalar.activation(last_factor[:, 0, :], ts_all[:], ACT.Copy, scale=wu[:, 1, 3:4])
         th1 = activation(a1, ACT.Tanh, us_col[:, 1, :], placed([PACK, SLOTS], F32, "tanh1", 50 * KIB))
         sl1 = activation(a1, ACT.Silu, silu_scale[:, 1, :], sbuf([PACK, SLOTS], F32, "silu1", "us_col"))
         dyq1 = quantize_whole(dyg1, E5M2, "dy1")
         daq = [operand(SLOTS, "daq0", "dy_grouped1"), operand(SLOTS, "daq1")]
         quantize(columns(daq[0], every), E5M2, da0[:])
         windows.append(cleared("window2", "da0"))
-        slope1 = sbuf([PACK, SLOTS], F32, "slope1", "factor0")
+        slope1 = sbuf([PACK, SLOTS], F32, "slope1", "x_raw0")
         for rows, factor in ((slice(0, 2), factor1[:, 0:2, :]), (slice(2, 3), factor1[:, 2:3, :]), (slice(3, 4), last_factor[:])):
             times(slope1[:, rows, :], th1[:, rows, :], ALU.add, factor)
         windows.append(placed([UNITS], F32, "window3", 50 * KIB))

@@ -78,16 +78,16 @@ def tile_attend_gffn_sil_kernel(
         nc.scalar.dma_start(ts_table[P - 1 : P, :], ts[0:1, :])
         us_col = load_column(us, "us_col")
         wt_col = load_column(wt, "wt_col")
-        nc.vector.memset(ts_table[0 : P - 1, :].bitcast(I32), 0)
-        s1_table = load_scales(w1_scales, "s1_table", nc.gpsimd)
         ident = sbuf([P], F32, "ident")
         make_identity(nc, ident[:])
-        s2_table = load_scales(w2_scales, "s2_table", nc.vector)
-        x_raw = [load_half(x_rows, 0, sbuf([PACK, K_PASS], F32, "x_raw0"))]
-        w1_table = load_words(w1_words, placed([UNITS], I32, "w1_table", 58 * KIB))
         warm = sbuf([2], F32, "warm")
         nc.vector.memset(warm[:, 0:1], 0.0)
         nc.scalar.activation(warm[:, 1:2], warm[:, 0:1], ACT.Silu)
+        nc.vector.memset(ts_table[0 : P - 1, :].bitcast(I32), 0)
+        s1_table = load_scales(w1_scales, "s1_table", nc.gpsimd)
+        s2_table = load_scales(w2_scales, "s2_table", nc.vector)
+        x_raw = [load_half(x_rows, 0, sbuf([PACK, K_PASS], F32, "x_raw0"))]
+        w1_table = load_words(w1_words, placed([UNITS], I32, "w1_table", 58 * KIB))
 
         def listed(table, cols):
             return table.indirect(offsets[:, cols.start // 16 : cols.stop // 16])
@@ -146,13 +146,14 @@ def tile_attend_gffn_sil_kernel(
             quantize(columns(target, every), fmt, grouped[:].rearrange("p u c -> p (u c)"))
             return target
 
-        def turn_x(grouped, u, n, name):
+        def turn_x(grouped, u, n, name, copy=nc.scalar.copy, by_row=None):
             turned_words = bank(n, name + "_words")
             for t in range(PACK):
                 words = grouped[t // 2].bitcast(F32)[:, 256 * (t % 2) + u : 256 * (t % 2 + 1) : 2]
                 nc.tensor.transpose(turned_words[:, block(t)], words, ident[:])
-            by_row = sbuf([2 * K_PASS], BF16, name)
-            nc.scalar.copy(
+            if by_row is None:
+                by_row = sbuf([2 * K_PASS], BF16, name)
+            copy(
                 by_row[:].rearrange("s (e p t) -> s e p t", e=2, t=PACK),
                 turned_words[:].bitcast(BF16).rearrange("s (t p e) -> s e p t", t=PACK, e=2),
             )
@@ -197,7 +198,7 @@ def tile_attend_gffn_sil_kernel(
         def second_product(dyq, q, n):
             dh = bank(n, "dh")
             for t in range(PACK):
-                product(dh[:, block(t)], columns(dyq, block(t)), E5M2, columns(w2, block(q)), E4M3)
+                product(dh[:, block(t)], dyq[t], E5M2, columns(w2, block(q)), E4M3)
             return dh
 
         def finish(grouped, dh, factor, q):
@@ -214,13 +215,15 @@ def tile_attend_gffn_sil_kernel(
             return window
 
         ts_row = sbuf([SLOTS], F32, "ts_row")
-        nc.scalar.activation(ts_row[:], listed(ts_table[:], every), ACT.Copy)
-        turned = bank(0, "turned")
-        for b in range(4):
-            nc.tensor.transpose(turned[:, block(b)], ts_row[:, block(b)], ident[:])
         ts_col = sbuf([4], F32, "ts_col")
-        nc.scalar.activation(ts_col[:], turned[:, P - 1 :: P], ACT.Copy, scale=0.5)
         spread = bank(1, "spread")
+        for cols in parts:
+            nc.scalar.activation(ts_row[:, cols], listed(ts_table[:], cols), ACT.Copy)
+        for c in range(2):
+            turned = bank(2 * c, "turned")
+            for b in range(2):
+                nc.tensor.transpose(turned[:, block(b)], ts_row[:, block(2 * c + b)], ident[:])
+            nc.scalar.activation(ts_col[:, 2 * c : 2 * c + 2], turned[:, P - 1 : 2 * P : P], ACT.Copy, scale=0.5)
         for b in range(4):
             nc.tensor.transpose(spread[:, block(b)], ts_col[:, b : b + 1].to_broadcast([P, P]), ident[:])
         ts_all = sbuf([SLOTS], F32, "ts_all")
@@ -230,75 +233,98 @@ def tile_attend_gffn_sil_kernel(
         s2_rows = gather(s2_table, U8, "s2_rows", [every])
         x_raw.append(load_half(x_rows, 1, sbuf([PACK, K_PASS], F32, "x_raw1")))
         dy_raw = [load_half(dy_rows, 0, sbuf([PACK, K_PASS], F32, "dy_raw0"))]
+        w2_table = load_words(w2_words, placed([UNITS], I32, "w2_table", 24 * KIB))
         s2 = place_scales(s2_rows, sbuf([SLOTS], U8, "s2", "x_raw1"))
-        w2_table = load_words(w2_words, placed([UNITS], I32, "w2_table", 20 * KIB))
-        dy_raw.append(load_half(dy_rows, 1, placed([PACK, K_PASS], F32, "dy_raw1", 48 * KIB)))
+        dy_raw.append(load_half(dy_rows, 1, placed([PACK, K_PASS], F32, "dy_raw1", 78 * KIB)))
         wu = sbuf([HALVES, PACK], F32, "wu")
         silu_scale = sbuf([HALVES, PACK], F32, "silu_scale")
         nc.vector.scalar_tensor_tensor(wu[:], us_col, -1.0, wt_col, ALU.mult, ALU.mult)
         nc.vector.tensor_scalar(silu_scale[:], us_col, -2.0, 0.0, ALU.mult, ALU.add)
         xg0 = [sbuf([2 * K_PASS], BF16, f"x_grouped0{pair}")[:] for pair in range(2)]
         group_pair(xg0[0], x_raw[0], 0, nc.vector.tensor_copy)
-        group_pair(xg0[1], x_raw[0], 1, nc.scalar.copy)
+        group_pair(xg0[1], x_raw[0], 1, nc.vector.tensor_copy)
         xq0 = quantize_pairs(xg0, E4M3, "x0")
-        xr0 = [turn_x(xg0, 0, 2, "x_by_row00")]
-        factor0 = [outer(nc.vector, 0, range(2), sbuf([2, SLOTS], F32, "factor00"))]
+        factors = [sbuf([2, SLOTS], F32, f"factor{h}0") for h in range(HALVES)]
+        for h in range(HALVES):
+            for t in range(2):
+                nc.scalar.activation(factors[h][:, t, :], spread[:], ACT.Copy, scale=wu[:, h, t : t + 1])
+        factor02 = outer(nc.vector, 0, [2], sbuf([1, SLOTS], F32, "factor02", "x_raw0"))
         w1 = (gather(w1_table, U32, "w1", parts), s1)
+        xr0 = [turn_x(xg0, 0, 3, "x_by_row00", nc.vector.tensor_copy, placed([2 * K_PASS], BF16, "x_by_row00", 58 * KIB))]
         a0 = turn(first_product(xq0, 4, [sbuf([K_PASS], F32, f"a_scaled0{g}")[:] for g in range(4)]), 0)
-        factor0.append(outer(nc.vector, 0, range(2, 4), placed([2, SLOTS], F32, "factor01", 58 * KIB)))
+        factor03 = outer(nc.vector, 0, [3], placed([1, SLOTS], F32, "factor03", 60 * KIB))
         xrq = [(placed([2 * P], U32, "xr00_codes", 62 * KIB), sbuf([2 * P], U8, "xr00_scales"))]
         quantize(columns(xrq[0], parts[0]), E4M3, xr0[0][:])
-        last_factor = sbuf([1, SLOTS], F32, "last_factor", "a_scaled00")
-        nc.scalar.activation(last_factor[:, 0, :], ts_all[:], ACT.Copy, scale=wu[:, 1, 3:4])
+        factor12 = sbuf([1, SLOTS], F32, "factor12", "a_scaled00")
+        nc.scalar.activation(factor12[:, 0, :], ts_all[:], ACT.Copy, scale=wu[:, 1, 2:3])
         th0 = activation(a0, ACT.Tanh, us_col[:, 0, :], sbuf([PACK, SLOTS], F32, "tanh0"))
         grouped = group(x_raw[1], sbuf([2, 2 * K_PASS], BF16, "x_grouped1"), nc.vector.tensor_copy)
         xg1 = [grouped[:, pair, :] for pair in range(2)]
         xq1 = quantize_pairs(xg1, E4M3, "x1")
-        sl0 = activation(a0, ACT.Silu, silu_scale[:, 0, :], placed([PACK, SLOTS], F32, "silu0", 32 * KIB))
-        scaled_sums = placed([PACK, K_PASS], F32, "a_scaled1", 40 * KIB)
-        scaled1 = first_product(xq1, 0, [scaled_sums[:, g, :] for g in range(4)])
-        dyg0 = group(dy_raw[0], placed([2, 2 * K_PASS], BF16, "dy_grouped0", 6 * KIB), nc.vector.tensor_copy)
-        dyq0 = quantize_pairs([dyg0[:, pair, :] for pair in range(2)], E5M2, "dy0")
+        dyg0 = [placed([2 * K_PASS], BF16, "dy_grouped00", 7 * KIB)[:], sbuf([2 * K_PASS], BF16, "dy_grouped01")[:]]
+        sl0 = [placed([2, SLOTS], F32, f"silu0{pair}", (35 + 4 * pair) * KIB) for pair in range(2)]
+        for t in range(PACK):
+            nc.scalar.activation(sl0[t // 2][:, t % 2, :], a0[t][:], ACT.Silu, scale=silu_scale[:, 0, t : t + 1])
+        scaled_sums = sbuf([3, K_PASS], F32, "a_scaled1")
+        last_sums = placed([K_PASS], F32, "a_scaled13", 25 * KIB)
+        scaled1 = first_product(xq1, 0, [scaled_sums[:, g, :] for g in range(3)] + [last_sums[:]])
+        for pair in range(2):
+            group_pair(dyg0[pair], dy_raw[0], pair, nc.vector.tensor_copy)
+        dyq0 = [operand(2 * P, f"dy0{pair}") for pair in range(2)]
+        for pair in range(2):
+            quantize(columns(dyq0[pair], parts[0]), E5M2, dyg0[pair])
         sigmoid0 = placed([PACK, SLOTS], F32, "sigmoid0", 0)
         windows = [placed([UNITS], F32, "window0", 8 * KIB)]
         nc.gpsimd.memset(windows[0][:], 0.0)
-        for pair in range(2):
-            rows = slice(2 * pair, 2 * pair + 2)
-            times(sigmoid0[:, rows, :], th0[:, rows, :], ALU.add, factor0[pair][:])
+        for rows, factor in ((slice(0, 2), factors[0]), (slice(2, 3), factor02), (slice(3, 4), factor03)):
+            times(sigmoid0[:, rows, :], th0[:, rows, :], ALU.add, factor[:])
         w2 = (gather(w2_table, U32, "w2", [every]), s2)
-        dh0 = [second_product(dyq0, q, q) for q in range(4)]
-        a1 = turn(scaled1, 4)
-        slope0 = placed([PACK, SLOTS], F32, "slope0", 16 * KIB)
-        windows.append(placed([UNITS], F32, "window1", 24 * KIB))
+        dh0 = [second_product([columns(dyq0[t // 2], block(t % 2)) for t in range(PACK)], q, 4 + q) for q in range(4)]
+        a1 = turn(scaled1, 0)
+        slope0 = placed([PACK, SLOTS], F32, "slope0", 17 * KIB)
+        windows.append(placed([UNITS], F32, "window1", 27 * KIB))
         nc.gpsimd.memset(windows[1][:], 0.0)
-        times_silu(slope0, sl0, sigmoid0)
-        factor1 = outer(nc.gpsimd, 1, range(3), placed([3, SLOTS], F32, "factor1", 32 * KIB))
-        da0 = sbuf([PACK * SLOTS], BF16, "da0")
+        times(slope0[:, 0:2, :], sl0[0][:], ALU.subtract, sigmoid0[:, 0:2, :])
+        times_by_slots(slope0[:, 2:4, :], sl0[1][:], ALU.subtract, sigmoid0[:, 2:4, :])
+        dyg1 = group(dy_raw[1], placed([2, 2 * K_PASS], BF16, "dy_grouped1", 44 * KIB), nc.scalar.copy)
+        factor13 = outer(nc.gpsimd, 1, [3], placed([1, SLOTS], F32, "factor13", 38 * KIB))
+        da0 = placed([PACK * SLOTS], BF16, "da0", 40 * KIB)
         for q in range(4):
             finish(da0[:, q * K_PASS : (q + 1) * K_PASS], dh0[q], slope0, q)
 
-        dyg1 = group(dy_raw[1], sbuf([2, 2 * K_PASS], BF16, "dy_grouped1"), nc.scalar.copy)
-        th1 = activation(a1, ACT.Tanh, us_col[:, 1, :], placed([PACK, SLOTS], F32, "tanh1", 50 * KIB))
-        sl1 = activation(a1, ACT.Silu, silu_scale[:, 1, :], sbuf([PACK, SLOTS], F32, "silu1", "us_col"))
-        dyq1 = quantize_whole(dyg1, E5M2, "dy1")
-        daq = [operand(SLOTS, "daq0", "dy_grouped1"), operand(SLOTS, "daq1")]
+        th1 = activation(a1, ACT.Tanh, us_col[:, 1, :], placed([PACK, SLOTS], F32, "tanh1", 82 * KIB))
+        sl1 = activation(a1, ACT.Silu, silu_scale[:, 1, :], placed([PACK, SLOTS], F32, "silu1", 72 * KIB))
+        dyq1 = (placed([K_PASS], U32, "dy1_codes", 0), sbuf([K_PASS], U8, "dy1_scales"))
+        quantize(columns(dyq1, every), E5M2, dyg1[:].rearrange("p u c -> p (u c)"))
+        daq = [operand(SLOTS, "daq0"), operand(SLOTS, "daq1")]
         quantize(columns(daq[0], every), E5M2, da0[:])
-        windows.append(cleared("window2", "da0"))
-        slope1 = sbuf([PACK, SLOTS], F32, "slope1", "x_raw0")
-        for rows, factor in ((slice(0, 2), factor1[:, 0:2, :]), (slice(2, 3), factor1[:, 2:3, :]), (slice(3, 4), last_factor[:])):
+        windows.append(placed([UNITS], F32, "window2", 40 * KIB))
+        nc.gpsimd.memset(windows[2][:], 0.0)
+        slope1 = placed([PACK, SLOTS], F32, "slope1", 16 * KIB)
+        for rows, factor in ((slice(0, 2), factors[1][:]), (slice(2, 3), factor12[:]), (slice(3, 4), factor13[:])):
             times(slope1[:, rows, :], th1[:, rows, :], ALU.add, factor)
-        windows.append(placed([UNITS], F32, "window3", 50 * KIB))
+        windows.append(placed([UNITS], F32, "window3", 82 * KIB))
         nc.gpsimd.memset(windows[3][:], 0.0)
-        times_silu(slope1, sl1, slope1)
-        xr1 = [turn_x(xg1, u, 4 + u, f"x_by_row1{u}") for u in range(2)]
-        xr0.append(turn_x(xg0, 1, 6, "x_by_row01"))
+        def times_silu1(pair, cols):
+            rows = slice(2 * pair, 2 * pair + 2)
+            times(slope1[:, rows, cols], sl1[:, rows, cols], ALU.subtract, slope1[:, rows, cols])
+
+        xr1 = [turn_x(xg1, 0, 4, "x_by_row10", by_row=placed([2 * K_PASS], BF16, "x_by_row10", 80 * KIB))]
+        xr0.append(turn_x(xg0, 1, 1, "x_by_row01"))
+        xr1.append(turn_x(xg1, 1, 2, "x_by_row11"))
         da1 = [sbuf([PACK * SLOTS // 2], BF16, f"da1{part}") for part in range(2)]
-        dh1 = [second_product(dyq1, q, q) for q in range(4)]
+        dh1 = [second_product([columns(dyq1, block(t)) for t in range(PACK)], q, (5, 6, 7, 0)[q]) for q in range(4)]
         xrq.append(operand(2 * P, "xr10"))
+        late_codes = [operand(2 * P, f"xr{h}1", "da11" if h == 1 else None) for h in range(HALVES)]
+        times_silu1(0, parts[0])
+        times_silu1(1, parts[0])
+        times_silu1(0, parts[1])
         for q in range(2):
             finish(da1[0][:, q * K_PASS : (q + 1) * K_PASS], dh1[q], slope1, q)
         quantize(columns(xrq[1], parts[0]), E4M3, xr1[0][:])
         quantize(columns(daq[1], parts[0]), E5M2, da1[0][:])
+        times_silu1(1, parts[1])
+        quantize(columns(late_codes[0], parts[0]), E4M3, xr0[1][:])
 
         def turned_x(h, j):
             return columns(late_codes[h], block(j - 2)) if j >= 2 else columns(xrq[h], block(j))
@@ -317,24 +343,22 @@ def tile_attend_gffn_sil_kernel(
 
         out_rows = out.rearrange("(p j) n -> p j n", j=PACK)
         for j in range(2):
-            scalar_scatter(windows[j], output_sums(j, (7, 4)[j], parts[0], nc.scalar.copy, f"dw{j}_early")[:], parts[0])
+            scalar_scatter(windows[j], output_sums(j, (3, 4)[j], parts[0], nc.scalar.copy, f"dw{j}_early")[:], parts[0])
         for q in range(2, 4):
             finish(da1[1][:, q % 2 * K_PASS : (q % 2 + 1) * K_PASS], dh1[q], slope1, q)
         for q in range(2, 4):
             quantize(columns(daq[1], block(q)), E5M2, da1[1][:, q % 2 * K_PASS : (q % 2 + 1) * K_PASS])
-        late_codes = [operand(2 * P, f"xr{h}1", "da11" if h == 0 else None) for h in range(HALVES)]
-        for h, by_row in enumerate((xr0, xr1)):
-            quantize(columns(late_codes[h], parts[0]), E4M3, by_row[1][:])
-        late0 = output_sums(0, 0, parts[1], nc.vector.tensor_copy, "dw0_late")
-        late1 = output_sums(1, 1, parts[1], nc.scalar.copy, "dw1_late")
+        quantize(columns(late_codes[1], parts[0]), E4M3, xr1[1][:])
+        late0 = output_sums(0, 5, parts[1], nc.vector.tensor_copy, "dw0_late")
+        late1 = output_sums(1, 6, parts[1], nc.scalar.copy, "dw1_late")
+        sums2 = output_sums(2, 1, every, nc.scalar.copy, "dw2")
         nc.vector.tensor_copy(listed(windows[0][:], parts[1]), late0[:])
         nc.sync.dma_start(out_rows[:, 0, :], windows[0][:])
         scalar_scatter(windows[1], late1[:], parts[1])
         nc.scalar.dma_start(out_rows[:, 1, :], windows[1][:])
-        sums2 = output_sums(2, 2, every, nc.vector.tensor_copy, "dw2", "dw0_late_sb")
         nc.vector.tensor_copy(listed(windows[2][:], every), sums2[:])
         nc.sync.dma_start(out_rows[:, 2, :], windows[2][:])
-        sums3 = output_sums(3, 5, every, nc.scalar.copy, "dw3", "dw1_late_sb")
+        sums3 = output_sums(3, 2, every, nc.scalar.copy, "dw3", "dw1_late_sb")
         for cols in parts:
             scalar_scatter(windows[3], sums3[:, cols], cols)
         nc.scalar.dma_start(out_rows[:, 3, :], windows[3][:])

@@ -95,8 +95,8 @@ def tile_attend_gffn_sil_kernel(
         every = slice(0, SLOTS)
         parts = [slice(0, SLOTS // 2), slice(SLOTS // 2, SLOTS)]
 
-        def gather(table, dtype, name, pieces):
-            picked = sbuf([SLOTS], dtype, name)
+        def gather(table, dtype, name, pieces, offset=None):
+            picked = sbuf([SLOTS], dtype, name) if offset is None else placed([SLOTS], dtype, name, offset)
             for cols in pieces:
                 nc.vector.tensor_copy(picked[:, cols], listed(table[:].bitcast(dtype), cols))
             return picked
@@ -226,69 +226,78 @@ def tile_attend_gffn_sil_kernel(
             nc.scalar.activation(ts_col[:, 2 * c : 2 * c + 2], turned[:, P - 1 : 2 * P : P], ACT.Copy, scale=0.5)
         for b in range(4):
             nc.tensor.transpose(spread[:, block(b)], ts_col[:, b : b + 1].to_broadcast([P, P]), ident[:])
-        ts_all = sbuf([SLOTS], F32, "ts_all")
-        nc.scalar.copy(ts_all[:], spread[:])
 
         s1 = place_scales(gather(s1_table, U8, "s1_rows", [every]), sbuf([SLOTS], U8, "s1"))
-        s2_rows = gather(s2_table, U8, "s2_rows", [every])
+        s2_rows = gather(s2_table, U8, "s2_rows", [every], 24 * KIB)
         x_raw.append(load_half(x_rows, 1, sbuf([PACK, K_PASS], F32, "x_raw1")))
-        dy_raw = [load_half(dy_rows, 0, sbuf([PACK, K_PASS], F32, "dy_raw0"))]
-        w2_table = load_words(w2_words, placed([UNITS], I32, "w2_table", 24 * KIB))
+        dy_first = [sbuf([PACK, K_PASS // 2], F32, f"dy_raw0{c}") for c in range(2)]
+        for c in range(2):
+            nc.sync.dma_start(dy_first[c][:], dy_rows[:, :, c * K_PASS // 2 : (c + 1) * K_PASS // 2])
+        w2_table = load_words(w2_words, placed([UNITS], I32, "w2_table", 25 * KIB))
         s2 = place_scales(s2_rows, sbuf([SLOTS], U8, "s2", "x_raw1"))
-        dy_raw.append(load_half(dy_rows, 1, placed([PACK, K_PASS], F32, "dy_raw1", 78 * KIB)))
+        dy_last = [placed([PACK, K_PASS // 2], F32, "dy_raw10", 79 * KIB), sbuf([PACK, K_PASS // 2], F32, "dy_raw11")]
+        for c in range(2):
+            first = K_PASS + c * K_PASS // 2
+            nc.sync.dma_start(dy_last[c][:], dy_rows[:, :, first : first + K_PASS // 2])
         wu = sbuf([HALVES, PACK], F32, "wu")
         silu_scale = sbuf([HALVES, PACK], F32, "silu_scale")
         nc.vector.scalar_tensor_tensor(wu[:], us_col, -1.0, wt_col, ALU.mult, ALU.mult)
-        nc.vector.tensor_scalar(silu_scale[:], us_col, -2.0, 0.0, ALU.mult, ALU.add)
+        nc.scalar.activation(silu_scale[:], us_col, ACT.Copy, scale=-2.0)
         xg0 = [sbuf([2 * K_PASS], BF16, f"x_grouped0{pair}")[:] for pair in range(2)]
-        group_pair(xg0[0], x_raw[0], 0, nc.vector.tensor_copy)
+        group_pair(xg0[0], x_raw[0], 0, nc.scalar.copy)
         group_pair(xg0[1], x_raw[0], 1, nc.vector.tensor_copy)
+        ts_all = sbuf([SLOTS], F32, "ts_all", "x_raw0")
+        nc.scalar.copy(ts_all[:], spread[:])
         xq0 = quantize_pairs(xg0, E4M3, "x0")
-        factors = [sbuf([2, SLOTS], F32, f"factor{h}0") for h in range(HALVES)]
-        for h in range(HALVES):
-            for t in range(2):
-                nc.scalar.activation(factors[h][:, t, :], spread[:], ACT.Copy, scale=wu[:, h, t : t + 1])
-        factor02 = outer(nc.vector, 0, [2], sbuf([1, SLOTS], F32, "factor02", "x_raw0"))
+        xr0 = [turn_x(xg0, 0, 3, "x_by_row00")]
+        factor0 = [outer(nc.vector, 0, range(2), sbuf([2, SLOTS], F32, "factor00"))]
         w1 = (gather(w1_table, U32, "w1", parts), s1)
-        xr0 = [turn_x(xg0, 0, 3, "x_by_row00", nc.vector.tensor_copy, placed([2 * K_PASS], BF16, "x_by_row00", 58 * KIB))]
         a0 = turn(first_product(xq0, 4, [sbuf([K_PASS], F32, f"a_scaled0{g}")[:] for g in range(4)]), 0)
-        factor03 = outer(nc.vector, 0, [3], placed([1, SLOTS], F32, "factor03", 60 * KIB))
+        factor0.append(outer(nc.vector, 0, range(2, 4), placed([2, SLOTS], F32, "factor01", 58 * KIB)))
         xrq = [(placed([2 * P], U32, "xr00_codes", 62 * KIB), sbuf([2 * P], U8, "xr00_scales"))]
         quantize(columns(xrq[0], parts[0]), E4M3, xr0[0][:])
-        factor12 = sbuf([1, SLOTS], F32, "factor12", "a_scaled00")
-        nc.scalar.activation(factor12[:, 0, :], ts_all[:], ACT.Copy, scale=wu[:, 1, 2:3])
+        last_factor = sbuf([1, SLOTS], F32, "last_factor", "a_scaled00")
+        nc.scalar.activation(last_factor[:, 0, :], ts_all[:], ACT.Copy, scale=wu[:, 1, 3:4])
         th0 = activation(a0, ACT.Tanh, us_col[:, 0, :], sbuf([PACK, SLOTS], F32, "tanh0"))
         grouped = group(x_raw[1], sbuf([2, 2 * K_PASS], BF16, "x_grouped1"), nc.vector.tensor_copy)
         xg1 = [grouped[:, pair, :] for pair in range(2)]
         xq1 = quantize_pairs(xg1, E4M3, "x1")
         dyg0 = [placed([2 * K_PASS], BF16, "dy_grouped00", 7 * KIB)[:], sbuf([2 * K_PASS], BF16, "dy_grouped01")[:]]
-        sl0 = [placed([2, SLOTS], F32, f"silu0{pair}", (35 + 4 * pair) * KIB) for pair in range(2)]
+        sl0 = [placed([2, SLOTS], F32, "silu00", 38 * KIB), sbuf([2, SLOTS], F32, "silu01")]
         for t in range(PACK):
             nc.scalar.activation(sl0[t // 2][:, t % 2, :], a0[t][:], ACT.Silu, scale=silu_scale[:, 0, t : t + 1])
-        scaled_sums = sbuf([3, K_PASS], F32, "a_scaled1")
-        last_sums = placed([K_PASS], F32, "a_scaled13", 25 * KIB)
-        scaled1 = first_product(xq1, 0, [scaled_sums[:, g, :] for g in range(3)] + [last_sums[:]])
-        for pair in range(2):
-            group_pair(dyg0[pair], dy_raw[0], pair, nc.vector.tensor_copy)
+        first_sums = sbuf([3, K_PASS], F32, "a_scaled1")
+        last_sums = placed([K_PASS], F32, "a_scaled13", 24 * KIB)
+        scaled1 = first_product(xq1, 0, [first_sums[:, g, :] for g in range(3)] + [last_sums[:]])
+        for c in range(2):
+            for pair in range(2):
+                nc.vector.tensor_copy(
+                    dyg0[pair].rearrange("p (t s j) -> p s j t", t=2, j=PACK)[:, c * P // 2 : (c + 1) * P // 2],
+                    dy_first[c][:].rearrange("p j (s t) -> p s j t", t=PACK)[:, :, :, 2 * pair : 2 * pair + 2],
+                )
         dyq0 = [operand(2 * P, f"dy0{pair}") for pair in range(2)]
         for pair in range(2):
             quantize(columns(dyq0[pair], parts[0]), E5M2, dyg0[pair])
         sigmoid0 = placed([PACK, SLOTS], F32, "sigmoid0", 0)
         windows = [placed([UNITS], F32, "window0", 8 * KIB)]
         nc.gpsimd.memset(windows[0][:], 0.0)
-        for rows, factor in ((slice(0, 2), factors[0]), (slice(2, 3), factor02), (slice(3, 4), factor03)):
-            times(sigmoid0[:, rows, :], th0[:, rows, :], ALU.add, factor[:])
+        for pair in range(2):
+            rows = slice(2 * pair, 2 * pair + 2)
+            times(sigmoid0[:, rows, :], th0[:, rows, :], ALU.add, factor0[pair][:])
         w2 = (gather(w2_table, U32, "w2", [every]), s2)
         dh0 = [second_product([columns(dyq0[t // 2], block(t % 2)) for t in range(PACK)], q, 4 + q) for q in range(4)]
         a1 = turn(scaled1, 0)
-        slope0 = placed([PACK, SLOTS], F32, "slope0", 17 * KIB)
-        windows.append(placed([UNITS], F32, "window1", 27 * KIB))
+        slope0 = placed([PACK, SLOTS], F32, "slope0", 16 * KIB)
+        windows.append(placed([UNITS], F32, "window1", 30 * KIB))
         nc.gpsimd.memset(windows[1][:], 0.0)
         times(slope0[:, 0:2, :], sl0[0][:], ALU.subtract, sigmoid0[:, 0:2, :])
         times_by_slots(slope0[:, 2:4, :], sl0[1][:], ALU.subtract, sigmoid0[:, 2:4, :])
-        dyg1 = group(dy_raw[1], placed([2, 2 * K_PASS], BF16, "dy_grouped1", 44 * KIB), nc.scalar.copy)
-        factor13 = outer(nc.gpsimd, 1, [3], placed([1, SLOTS], F32, "factor13", 38 * KIB))
-        da0 = placed([PACK * SLOTS], BF16, "da0", 40 * KIB)
+        dyg1 = placed([2, 2 * K_PASS], BF16, "dy_grouped1", 48 * KIB)
+        dyg1_rows = dyg1[:].rearrange("p u (t s j) -> p s j (u t)", t=2, j=PACK)
+        for c in range(2):
+            nc.scalar.copy(dyg1_rows[:, c * P // 2 : (c + 1) * P // 2], dy_last[c][:].rearrange("p j (s t) -> p s j t", t=PACK))
+        factor1 = outer(nc.gpsimd, 1, range(3), placed([3, SLOTS], F32, "factor1", 38 * KIB))
+        da0 = placed([PACK * SLOTS], BF16, "da0", 44 * KIB)
         for q in range(4):
             finish(da0[:, q * K_PASS : (q + 1) * K_PASS], dh0[q], slope0, q)
 
@@ -298,10 +307,10 @@ def tile_attend_gffn_sil_kernel(
         quantize(columns(dyq1, every), E5M2, dyg1[:].rearrange("p u c -> p (u c)"))
         daq = [operand(SLOTS, "daq0"), operand(SLOTS, "daq1")]
         quantize(columns(daq[0], every), E5M2, da0[:])
-        windows.append(placed([UNITS], F32, "window2", 40 * KIB))
+        windows.append(placed([UNITS], F32, "window2", 44 * KIB))
         nc.gpsimd.memset(windows[2][:], 0.0)
         slope1 = placed([PACK, SLOTS], F32, "slope1", 16 * KIB)
-        for rows, factor in ((slice(0, 2), factors[1][:]), (slice(2, 3), factor12[:]), (slice(3, 4), factor13[:])):
+        for rows, factor in ((slice(0, 2), factor1[:, 0:2, :]), (slice(2, 3), factor1[:, 2:3, :]), (slice(3, 4), last_factor[:])):
             times(slope1[:, rows, :], th1[:, rows, :], ALU.add, factor)
         windows.append(placed([UNITS], F32, "window3", 82 * KIB))
         nc.gpsimd.memset(windows[3][:], 0.0)
@@ -351,14 +360,17 @@ def tile_attend_gffn_sil_kernel(
         quantize(columns(late_codes[1], parts[0]), E4M3, xr1[1][:])
         late0 = output_sums(0, 5, parts[1], nc.vector.tensor_copy, "dw0_late")
         late1 = output_sums(1, 6, parts[1], nc.scalar.copy, "dw1_late")
-        sums2 = output_sums(2, 1, every, nc.scalar.copy, "dw2")
         nc.vector.tensor_copy(listed(windows[0][:], parts[1]), late0[:])
         nc.sync.dma_start(out_rows[:, 0, :], windows[0][:])
         scalar_scatter(windows[1], late1[:], parts[1])
         nc.scalar.dma_start(out_rows[:, 1, :], windows[1][:])
+        sums2 = output_sums(2, 5, every, nc.vector.tensor_copy, "dw2")
         nc.vector.tensor_copy(listed(windows[2][:], every), sums2[:])
         nc.sync.dma_start(out_rows[:, 2, :], windows[2][:])
-        sums3 = output_sums(3, 2, every, nc.scalar.copy, "dw3", "dw1_late_sb")
-        for cols in parts:
-            scalar_scatter(windows[3], sums3[:, cols], cols)
+        sums3 = [
+            output_sums(3, 1, parts[0], nc.scalar.copy, "dw3_first", "dw1_late_sb"),
+            output_sums(3, 2, parts[1], nc.scalar.copy, "dw3_second"),
+        ]
+        for cols, sums in zip(parts, sums3):
+            scalar_scatter(windows[3], sums[:], cols)
         nc.scalar.dma_start(out_rows[:, 3, :], windows[3][:])

@@ -56,11 +56,14 @@ def tile_attend_gffn_sil_kernel(
             nc.sync.dma_start(table[:], words[0].rearrange("p n t -> p (n t)").bitcast(I32))
             return table
 
-        def load_scales(scales, name, engine):
+        def load_scales(scales, name):
             table = sbuf([UNITS // 4], I32, name)
             nc.sync.dma_start(table[P - 16 : P, :], scales[0].bitcast(I32))
-            engine.memset(table[0 : P - 16, :], 0)
             return table
+
+        def gather_scales(table, name, offset=None):
+            nc.vector.memset(table[0 : P - 16, :], 0)
+            return gather(table, U8, name, [every], offset)
 
         def place_scales(rows, plane):
             for q in range(4):
@@ -68,24 +71,23 @@ def tile_attend_gffn_sil_kernel(
                 nc.sync.dma_start(plane[32 * q : 32 * q + 4, :].bitcast(I32), source.bitcast(I32))
             return plane
 
-        def load_column(vector, name):
-            padded = sbuf([HALVES, 2 * PACK], F32, name)
+        def load_column(vector, padded):
             column = padded[:, :, 0:PACK]
             nc.scalar.dma_start(column, vector.rearrange("(h p t) o -> p h (t o)", h=HALVES, t=PACK))
             return column
 
         ts_table = sbuf([UNITS], F32, "ts_table")
         nc.scalar.dma_start(ts_table[P - 1 : P, :], ts[0:1, :])
-        us_col = load_column(us, "us_col")
-        wt_col = load_column(wt, "wt_col")
+        us_col = load_column(us, sbuf([HALVES, 2 * PACK], F32, "us_col"))
+        wt_col = load_column(wt, placed([HALVES, 2 * PACK], F32, "wt_col", 24 * KIB))
         ident = sbuf([P], F32, "ident")
         make_identity(nc, ident[:])
         warm = sbuf([2], F32, "warm")
         nc.vector.memset(warm[:, 0:1], 0.0)
         nc.scalar.activation(warm[:, 1:2], warm[:, 0:1], ACT.Silu)
         nc.vector.memset(ts_table[0 : P - 1, :].bitcast(I32), 0)
-        s1_table = load_scales(w1_scales, "s1_table", nc.gpsimd)
-        s2_table = load_scales(w2_scales, "s2_table", nc.vector)
+        s1_table = load_scales(w1_scales, "s1_table")
+        s2_table = load_scales(w2_scales, "s2_table")
         x_raw = [load_half(x_rows, 0, sbuf([PACK, K_PASS], F32, "x_raw0"))]
         w1_table = load_words(w1_words, placed([UNITS], I32, "w1_table", 58 * KIB))
 
@@ -164,7 +166,7 @@ def tile_attend_gffn_sil_kernel(
             for g in range(4):
                 product(sums[g][:], columns(w1, block(g)), E4M3, columns(xq, every), E4M3)
             for g in range(4):
-                nc.scalar.activation(scaled[g], sums[g][:], ACT.Copy, scale=ts_col[:, g : g + 1])
+                nc.scalar.activation(scaled[g], sums[g][:], ACT.Copy, scale=sum_scale[:, g : g + 1])
             return scaled
 
         def turn(scaled, first_bank):
@@ -226,9 +228,11 @@ def tile_attend_gffn_sil_kernel(
             nc.scalar.activation(ts_col[:, 2 * c : 2 * c + 2], turned[:, P - 1 : 2 * P : P], ACT.Copy, scale=0.5)
         for b in range(4):
             nc.tensor.transpose(spread[:, block(b)], ts_col[:, b : b + 1].to_broadcast([P, P]), ident[:])
+        sum_scale = sbuf([4], F32, "sum_scale")
+        nc.scalar.copy(sum_scale[:], ts_col[:])
 
-        s1 = place_scales(gather(s1_table, U8, "s1_rows", [every]), sbuf([SLOTS], U8, "s1"))
-        s2_rows = gather(s2_table, U8, "s2_rows", [every], 24 * KIB)
+        s1 = place_scales(gather_scales(s1_table, "s1_rows"), sbuf([SLOTS], U8, "s1"))
+        s2_rows = gather_scales(s2_table, "s2_rows", 24 * KIB)
         x_raw.append(load_half(x_rows, 1, sbuf([PACK, K_PASS], F32, "x_raw1")))
         dy_first = [sbuf([PACK, K_PASS // 2], F32, f"dy_raw0{c}") for c in range(2)]
         for c in range(2):
@@ -244,16 +248,18 @@ def tile_attend_gffn_sil_kernel(
         nc.vector.scalar_tensor_tensor(wu[:], us_col, -1.0, wt_col, ALU.mult, ALU.mult)
         nc.scalar.activation(silu_scale[:], us_col, ACT.Copy, scale=-2.0)
         xg0 = [sbuf([2 * K_PASS], BF16, f"x_grouped0{pair}")[:] for pair in range(2)]
-        group_pair(xg0[0], x_raw[0], 0, nc.scalar.copy)
+        group_pair(xg0[0], x_raw[0], 0, nc.vector.tensor_copy)
         group_pair(xg0[1], x_raw[0], 1, nc.vector.tensor_copy)
-        ts_all = sbuf([SLOTS], F32, "ts_all", "x_raw0")
+        ts_all = sbuf([SLOTS], F32, "ts_all")
         nc.scalar.copy(ts_all[:], spread[:])
         xq0 = quantize_pairs(xg0, E4M3, "x0")
-        xr0 = [turn_x(xg0, 0, 3, "x_by_row00")]
-        factor0 = [outer(nc.vector, 0, range(2), sbuf([2, SLOTS], F32, "factor00"))]
+        factor00 = sbuf([3, SLOTS], F32, "factor00")
+        for t in range(3):
+            nc.scalar.activation(factor00[:, t, :], spread[:], ACT.Copy, scale=wu[:, 0, t : t + 1])
+        xr0 = [turn_x(xg0, 0, 2, "x_by_row00", by_row=sbuf([2 * K_PASS], BF16, "x_by_row00", "ts_col"))]
         w1 = (gather(w1_table, U32, "w1", parts), s1)
         a0 = turn(first_product(xq0, 4, [sbuf([K_PASS], F32, f"a_scaled0{g}")[:] for g in range(4)]), 0)
-        factor0.append(outer(nc.vector, 0, range(2, 4), placed([2, SLOTS], F32, "factor01", 58 * KIB)))
+        factor03 = outer(nc.vector, 0, [3], placed([1, SLOTS], F32, "factor03", 58 * KIB))
         xrq = [(placed([2 * P], U32, "xr00_codes", 62 * KIB), sbuf([2 * P], U8, "xr00_scales"))]
         quantize(columns(xrq[0], parts[0]), E4M3, xr0[0][:])
         last_factor = sbuf([1, SLOTS], F32, "last_factor", "a_scaled00")
@@ -281,9 +287,8 @@ def tile_attend_gffn_sil_kernel(
         sigmoid0 = placed([PACK, SLOTS], F32, "sigmoid0", 0)
         windows = [placed([UNITS], F32, "window0", 8 * KIB)]
         nc.gpsimd.memset(windows[0][:], 0.0)
-        for pair in range(2):
-            rows = slice(2 * pair, 2 * pair + 2)
-            times(sigmoid0[:, rows, :], th0[:, rows, :], ALU.add, factor0[pair][:])
+        for rows, factor in ((slice(0, 2), factor00[:, 0:2, :]), (slice(2, 3), factor00[:, 2:3, :]), (slice(3, 4), factor03[:])):
+            times(sigmoid0[:, rows, :], th0[:, rows, :], ALU.add, factor)
         w2 = (gather(w2_table, U32, "w2", [every]), s2)
         dh0 = [second_product([columns(dyq0[t // 2], block(t % 2)) for t in range(PACK)], q, 4 + q) for q in range(4)]
         a1 = turn(scaled1, 0)

from contextlib import ExitStack

import concourse.mybir as mybir
from concourse.masks import make_identity

F32 = mybir.dt.float32
BF16 = mybir.dt.bfloat16
I32 = mybir.dt.int32
U32 = mybir.dt.uint32
U16 = mybir.dt.uint16
U8 = mybir.dt.uint8
E4M3 = mybir.dt.float8_e4m3fn_x4
E5M2 = mybir.dt.float8_e5m2_x4
ACT = mybir.ActivationFunctionType
ALU = mybir.AluOpType

P = 128
PACK = 4
K_PASS = P * PACK
D, E, R, SLOTS, UNITS = 512, 512, 1024, 512, 2048
HALVES = R // K_PASS
KIB = 1024
FLOPS = 2 * R * SLOTS * (D + E + D)


def tile_attend_gffn_sil_kernel(
    tc, xT, w1_words, w1_scales, dyT, w2_words, w2_scales, us, ts, wt, offs, out
):
    nc = tc.nc
    with ExitStack() as ctx:
        lists = ctx.enter_context(tc.tile_pool(name="lists", bufs=1))
        keep = ctx.enter_context(tc.tile_pool(name="keep", bufs=1))
        shared = ctx.enter_context(tc.tile_pool(name="shared", bufs=1))
        psum = ctx.enter_context(tc.psum_pool(name="psum", bufs=1))

        def sbuf(shape, dtype, name, tag=None):
            return keep.tile([P, *shape], dtype, name=name, tag=tag or name, align_bytes=64)

        def placed(shape, dtype, name, offset):
            return shared.tile([P, *shape], dtype, name=name, offset=offset, align_bytes=64)

        def bank(n, name):
            return psum.tile([P, SLOTS], F32, name=name, tag=f"bank{n}")

        offsets = lists.tile([P, SLOTS // 16], U16, name="offsets")
        nc.sync.dma_start(offsets[:], offs)

        x_rows = xT.rearrange("(p j) r -> p j r", j=PACK)
        dy_rows = dyT.rearrange("(p j) r -> p j r", j=PACK)

        def load_half(rows, h, raw):
            nc.sync.dma_start(raw[:], rows[:, :, h * K_PASS : (h + 1) * K_PASS])
            return raw

        def load_words(words, table):
            nc.sync.dma_start(table[:], words[0].rearrange("p n t -> p (n t)").bitcast(I32))
            return table

        def load_scales(scales, name):
            table = sbuf([UNITS // 4], I32, name)
            nc.sync.dma_start(table[P - 16 : P, :], scales[0].bitcast(I32))
            return table

        def gather_scales(table, name, offset=None):
            nc.vector.memset(table[0 : P - 16, :], 0)
            return gather(table, U8, name, [every], offset)

        def place_scales(rows, plane):
            for q in range(4):
                source = rows[P - 16 + 4 * q : P - 12 + 4 * q, :]
                nc.sync.dma_start(plane[32 * q : 32 * q + 4, :].bitcast(I32), source.bitcast(I32))
            return plane

        def load_column(vector, padded):
            column = padded[:, :, 0:PACK]
            nc.scalar.dma_start(column, vector.rearrange("(h p t) o -> p h (t o)", h=HALVES, t=PACK))
            return column

        ts_table = sbuf([UNITS], F32, "ts_table")
        nc.scalar.dma_start(ts_table[P - 1 : P, :], ts[0:1, :])
        us_col = load_column(us, sbuf([HALVES, 2 * PACK], F32, "us_col"))
        wt_col = load_column(wt, placed([HALVES, 2 * PACK], F32, "wt_col", 24 * KIB))
        ident = sbuf([P], F32, "ident")
        make_identity(nc, ident[:])
        warm = sbuf([2], F32, "warm")
        nc.vector.memset(warm[:, 0:1], 0.0)
        nc.scalar.activation(warm[:, 1:2], warm[:, 0:1], ACT.Silu)
        nc.vector.memset(ts_table[0 : P - 1, :].bitcast(I32), 0)
        s1_table = load_scales(w1_scales, "s1_table")
        s2_table = load_scales(w2_scales, "s2_table")
        x_raw = [load_half(x_rows, 0, sbuf([PACK, K_PASS], F32, "x_raw0"))]
        w1_table = load_words(w1_words, placed([UNITS], I32, "w1_table", 58 * KIB))

        def listed(table, cols):
            return table.indirect(offsets[:, cols.start // 16 : cols.stop // 16])

        every = slice(0, SLOTS)
        parts = [slice(0, SLOTS // 2), slice(SLOTS // 2, SLOTS)]

        def gather(table, dtype, name, pieces, offset=None):
            picked = sbuf([SLOTS], dtype, name) if offset is None else placed([SLOTS], dtype, name, offset)
            for cols in pieces:
                nc.vector.tensor_copy(picked[:, cols], listed(table[:].bitcast(dtype), cols))
            return picked

        def group_pair(grouped, raw, pair, copy):
            copy(
                grouped.rearrange("p (t s j) -> p s j t", t=2, j=PACK),
                raw[:].rearrange("p j (s t) -> p s j t", t=PACK)[:, :, :, 2 * pair : 2 * pair + 2],
            )

        def group(raw, grouped, copy):
            for pair in range(2):
                group_pair(grouped[:, pair, :], raw, pair, copy)
            return grouped

        def operand(width, name, tag=None):
            return sbuf([width], U32, name + "_codes", tag), sbuf([width], U8, name + "_scales")

        def columns(pair, cols):
            return pair[0][:, cols], pair[1][:, cols]

        def quantize(target, fmt, grouped):
            nc.vector.quantize_mx(out=target[0].bitcast(fmt), scales=target[1], in_=grouped)

        def product(acc, lhs, fmt_l, rhs, fmt_r, start=True, stop=True):
            nc.tensor.matmul_mx(
                out=acc,
                lhsT=lhs[0].bitcast(fmt_l),
                lhsT_scale=lhs[1],
                rhs=rhs[0].bitcast(fmt_r),
                rhs_scale=rhs[1],
                start=start,
                stop=stop,
            )

        def block(k):
            return slice(k * P, (k + 1) * P)

        def quantize_pairs(grouped, fmt, name, tag=None):
            target = operand(K_PASS, name, tag)
            for pair in range(2):
                quantize(columns(target, parts[pair]), fmt, grouped[pair])
            return target

        def quantize_whole(grouped, fmt, name):
            target = operand(K_PASS, name)
            quantize(columns(target, every), fmt, grouped[:].rearrange("p u c -> p (u c)"))
            return target

        def turn_x(grouped, u, n, name, copy=nc.scalar.copy, by_row=None):
            turned_words = bank(n, name + "_words")
            for t in range(PACK):
                words = grouped[t // 2].bitcast(F32)[:, 256 * (t % 2) + u : 256 * (t % 2 + 1) : 2]
                nc.tensor.transpose(turned_words[:, block(t)], words, ident[:])
            if by_row is None:
                by_row = sbuf([2 * K_PASS], BF16, name)
            copy(
                by_row[:].rearrange("s (e p t) -> s e p t", e=2, t=PACK),
                turned_words[:].bitcast(BF16).rearrange("s (t p e) -> s e p t", t=PACK, e=2),
            )
            return by_row

        def first_product(xq, first_bank, scaled):
            sums = [bank(first_bank + g, "a_by_slot") for g in range(4)]
            for g in range(4):
                product(sums[g][:], columns(w1, block(g)), E4M3, columns(xq, every), E4M3)
            for g in range(4):
                nc.scalar.activation(scaled[g], sums[g][:], ACT.Copy, scale=sum_scale[:, g : g + 1])
            return scaled

        def turn(scaled, first_bank):
            by_row = [bank(first_bank + t, "a_by_row") for t in range(PACK)]
            for g in range(4):
                for t in range(PACK):
                    nc.tensor.transpose(by_row[t][:, block(g)], scaled[g][:, block(t)], ident[:])
            return by_row

        def activation(by_row, func, scale, values):
            for t in range(PACK):
                nc.scalar.activation(values[:, t, :], by_row[t][:], func, scale=scale[:, t : t + 1])
            return values

        def outer(engine, h, tiles, factor):
            for n, t in enumerate(tiles):
                engine.tensor_scalar(factor[:, n, :], ts_all[:], wu[:, h, t : t + 1], 0.0, ALU.mult, ALU.add)
            return factor

        def times(result, values, op, factor):
            nc.vector.scalar_tensor_tensor(result, values, 1.0, factor, op, ALU.mult)

        def times_by_slots(result, values, op, factor):
            for cols in parts:
                times(result[:, :, cols], values[:, :, cols], op, factor[:, :, cols])

        def times_silu(result, values, factor):
            times(result[:, 0:2, :], values[:, 0:2, :], ALU.subtract, factor[:, 0:2, :])
            times_by_slots(result[:, 2:4, :], values[:, 2:4, :], ALU.subtract, factor[:, 2:4, :])

        def second_product(dyq, q, n):
            dh = bank(n, "dh")
            for t in range(PACK):
                product(dh[:, block(t)], dyq[t], E5M2, columns(w2, block(q)), E4M3)
            return dh

        def finish(grouped, dh, factor, q):
            nc.vector.tensor_tensor(
                grouped.rearrange("p (c i t) -> p c t i", i=4, t=PACK),
                dh[:].rearrange("p (t c i) -> p c t i", i=4, t=PACK),
                factor[:, :, block(q)].rearrange("p t (c i) -> p c t i", i=4),
                ALU.mult,
            )

        def cleared(name, tag):
            window = sbuf([UNITS], F32, name, tag)
            nc.gpsimd.memset(window[:], 0.0)
            return window

        ts_row = sbuf([SLOTS], F32, "ts_row")
        ts_col = sbuf([4], F32, "ts_col")
        spread = bank(1, "spread")
        for cols in parts:
            nc.scalar.activation(ts_row[:, cols], listed(ts_table[:], cols), ACT.Copy)
        for c in range(2):
            turned = bank(2 * c, "turned")
            for b in range(2):
                nc.tensor.transpose(turned[:, block(b)], ts_row[:, block(2 * c + b)], ident[:])
            nc.scalar.activation(ts_col[:, 2 * c : 2 * c + 2], turned[:, P - 1 : 2 * P : P], ACT.Copy, scale=0.5)
        for b in range(4):
            nc.tensor.transpose(spread[:, block(b)], ts_col[:, b : b + 1].to_broadcast([P, P]), ident[:])
        sum_scale = sbuf([4], F32, "sum_scale")
        nc.scalar.copy(sum_scale[:], ts_col[:])

        s1 = place_scales(gather_scales(s1_table, "s1_rows"), sbuf([SLOTS], U8, "s1"))
        s2_rows = gather_scales(s2_table, "s2_rows", 24 * KIB)
        x_raw.append(load_half(x_rows, 1, sbuf([PACK, K_PASS], F32, "x_raw1")))
        dy_first = [sbuf([PACK, K_PASS // 2], F32, f"dy_raw0{c}") for c in range(2)]
        for c in range(2):
            nc.sync.dma_start(dy_first[c][:], dy_rows[:, :, c * K_PASS // 2 : (c + 1) * K_PASS // 2])
        w2_table = load_words(w2_words, placed([UNITS], I32, "w2_table", 25 * KIB))
        s2 = place_scales(s2_rows, sbuf([SLOTS], U8, "s2", "x_raw1"))
        dy_last = [placed([PACK, K_PASS // 2], F32, "dy_raw10", 79 * KIB), sbuf([PACK, K_PASS // 2], F32, "dy_raw11")]
        for c in range(2):
            first = K_PASS + c * K_PASS // 2
            nc.sync.dma_start(dy_last[c][:], dy_rows[:, :, first : first + K_PASS // 2])
        wu = sbuf([HALVES, PACK], F32, "wu")
        silu_scale = sbuf([HALVES, PACK], F32, "silu_scale")
        nc.vector.scalar_tensor_tensor(wu[:], us_col, -1.0, wt_col, ALU.mult, ALU.mult)
        nc.scalar.activation(silu_scale[:], us_col, ACT.Copy, scale=-2.0)
        xg0 = [sbuf([2 * K_PASS], BF16, f"x_grouped0{pair}")[:] for pair in range(2)]
        group_pair(xg0[0], x_raw[0], 0, nc.vector.tensor_copy)
        group_pair(xg0[1], x_raw[0], 1, nc.vector.tensor_copy)
        ts_all = sbuf([SLOTS], F32, "ts_all")
        nc.scalar.copy(ts_all[:], spread[:])
        xq0 = quantize_pairs(xg0, E4M3, "x0")
        factor00 = sbuf([3, SLOTS], F32, "factor00")
        for t in range(3):
            nc.scalar.activation(factor00[:, t, :], spread[:], ACT.Copy, scale=wu[:, 0, t : t + 1])
        xr0 = [turn_x(xg0, 0, 2, "x_by_row00", by_row=sbuf([2 * K_PASS], BF16, "x_by_row00", "ts_col"))]
        w1 = (gather(w1_table, U32, "w1", parts), s1)
        a0 = turn(first_product(xq0, 4, [sbuf([K_PASS], F32, f"a_scaled0{g}")[:] for g in range(4)]), 0)
        factor03 = outer(nc.vector, 0, [3], placed([1, SLOTS], F32, "factor03", 58 * KIB))
        xrq = [(placed([2 * P], U32, "xr00_codes", 62 * KIB), sbuf([2 * P], U8, "xr00_scales"))]
        quantize(columns(xrq[0], parts[0]), E4M3, xr0[0][:])
        last_factor = sbuf([1, SLOTS], F32, "last_factor", "a_scaled00")
        nc.scalar.activation(last_factor[:, 0, :], ts_all[:], ACT.Copy, scale=wu[:, 1, 3:4])
        th0 = activation(a0, ACT.Tanh, us_col[:, 0, :], sbuf([PACK, SLOTS], F32, "tanh0"))
        grouped = group(x_raw[1], sbuf([2, 2 * K_PASS], BF16, "x_grouped1"), nc.vector.tensor_copy)
        xg1 = [grouped[:, pair, :] for pair in range(2)]
        xq1 = quantize_pairs(xg1, E4M3, "x1")
        dyg0 = [placed([2 * K_PASS], BF16, "dy_grouped00", 7 * KIB)[:], sbuf([2 * K_PASS], BF16, "dy_grouped01")[:]]
        sl0 = [placed([2, SLOTS], F32, "silu00", 38 * KIB), sbuf([2, SLOTS], F32, "silu01")]
        for t in range(PACK):
            nc.scalar.activation(sl0[t // 2][:, t % 2, :], a0[t][:], ACT.Silu, scale=silu_scale[:, 0, t : t + 1])
        first_sums = sbuf([3, K_PASS], F32, "a_scaled1")
        last_sums = placed([K_PASS], F32, "a_scaled13", 24 * KIB)
        scaled1 = first_product(xq1, 0, [first_sums[:, g, :] for g in range(3)] + [last_sums[:]])
        for c in range(2):
            for pair in range(2):
                nc.vector.tensor_copy(
                    dyg0[pair].rearrange("p (t s j) -> p s j t", t=2, j=PACK)[:, c * P // 2 : (c + 1) * P // 2],
                    dy_first[c][:].rearrange("p j (s t) -> p s j t", t=PACK)[:, :, :, 2 * pair : 2 * pair + 2],
                )
        dyq0 = [operand(2 * P, f"dy0{pair}") for pair in range(2)]
        for pair in range(2):
            quantize(columns(dyq0[pair], parts[0]), E5M2, dyg0[pair])
        sigmoid0 = placed([PACK, SLOTS], F32, "sigmoid0", 0)
        windows = [placed([UNITS], F32, "window0", 8 * KIB)]
        nc.gpsimd.memset(windows[0][:], 0.0)
        for rows, factor in ((slice(0, 2), factor00[:, 0:2, :]), (slice(2, 3), factor00[:, 2:3, :]), (slice(3, 4), factor03[:])):
            times(sigmoid0[:, rows, :], th0[:, rows, :], ALU.add, factor)
        w2 = (gather(w2_table, U32, "w2", [every]), s2)
        dh0 = [second_product([columns(dyq0[t // 2], block(t % 2)) for t in range(PACK)], q, 4 + q) for q in range(4)]
        a1 = turn(scaled1, 0)
        slope0 = placed([PACK, SLOTS], F32, "slope0", 16 * KIB)
        windows.append(placed([UNITS], F32, "window1", 30 * KIB))
        nc.gpsimd.memset(windows[1][:], 0.0)
        times(slope0[:, 0:2, :], sl0[0][:], ALU.subtract, sigmoid0[:, 0:2, :])
        times_by_slots(slope0[:, 2:4, :], sl0[1][:], ALU.subtract, sigmoid0[:, 2:4, :])
        dyg1 = placed([2, 2 * K_PASS], BF16, "dy_grouped1", 48 * KIB)
        dyg1_rows = dyg1[:].rearrange("p u (t s j) -> p s j (u t)", t=2, j=PACK)
        for c in range(2):
            nc.scalar.copy(dyg1_rows[:, c * P // 2 : (c + 1) * P // 2], dy_last[c][:].rearrange("p j (s t) -> p s j t", t=PACK))
        factor1 = outer(nc.gpsimd, 1, range(3), placed([3, SLOTS], F32, "factor1", 38 * KIB))
        da0 = placed([PACK * SLOTS], BF16, "da0", 44 * KIB)
        for q in range(4):
            finish(da0[:, q * K_PASS : (q + 1) * K_PASS], dh0[q], slope0, q)

        th1 = activation(a1, ACT.Tanh, us_col[:, 1, :], placed([PACK, SLOTS], F32, "tanh1", 82 * KIB))
        sl1 = activation(a1, ACT.Silu, silu_scale[:, 1, :], placed([PACK, SLOTS], F32, "silu1", 72 * KIB))
        dyq1 = (placed([K_PASS], U32, "dy1_codes", 0), sbuf([K_PASS], U8, "dy1_scales"))
        quantize(columns(dyq1, every), E5M2, dyg1[:].rearrange("p u c -> p (u c)"))
        daq = [operand(SLOTS, "daq0"), operand(SLOTS, "daq1")]
        quantize(columns(daq[0], every), E5M2, da0[:])
        windows.append(placed([UNITS], F32, "window2", 44 * KIB))
        nc.gpsimd.memset(windows[2][:], 0.0)
        slope1 = placed([PACK, SLOTS], F32, "slope1", 16 * KIB)
        for rows, factor in ((slice(0, 2), factor1[:, 0:2, :]), (slice(2, 3), factor1[:, 2:3, :]), (slice(3, 4), last_factor[:])):
            times(slope1[:, rows, :], th1[:, rows, :], ALU.add, factor)
        windows.append(placed([UNITS], F32, "window3", 82 * KIB))
        nc.gpsimd.memset(windows[3][:], 0.0)
        def times_silu1(pair, cols):
            rows = slice(2 * pair, 2 * pair + 2)
            times(slope1[:, rows, cols], sl1[:, rows, cols], ALU.subtract, slope1[:, rows, cols])

        xr1 = [turn_x(xg1, 0, 4, "x_by_row10", by_row=placed([2 * K_PASS], BF16, "x_by_row10", 80 * KIB))]
        xr0.append(turn_x(xg0, 1, 1, "x_by_row01"))
        xr1.append(turn_x(xg1, 1, 2, "x_by_row11"))
        da1 = [sbuf([PACK * SLOTS // 2], BF16, f"da1{part}") for part in range(2)]
        dh1 = [second_product([columns(dyq1, block(t)) for t in range(PACK)], q, (5, 6, 7, 0)[q]) for q in range(4)]
        xrq.append(operand(2 * P, "xr10"))
        late_codes = [operand(2 * P, f"xr{h}1", "da11" if h == 1 else None) for h in range(HALVES)]
        times_silu1(0, parts[0])
        times_silu1(1, parts[0])
        times_silu1(0, parts[1])
        for q in range(2):
            finish(da1[0][:, q * K_PASS : (q + 1) * K_PASS], dh1[q], slope1, q)
        quantize(columns(xrq[1], parts[0]), E4M3, xr1[0][:])
        quantize(columns(daq[1], parts[0]), E5M2, da1[0][:])
        times_silu1(1, parts[1])
        quantize(columns(late_codes[0], parts[0]), E4M3, xr0[1][:])

        def turned_x(h, j):
            return columns(late_codes[h], block(j - 2)) if j >= 2 else columns(xrq[h], block(j))

        def output_sums(j, n, cols, copy, name, tag=None):
            width = cols.stop - cols.start
            dw = bank(n, name)
            for h in range(HALVES):
                product(dw[:, 0:width], turned_x(h, j), E4M3, columns(daq[h], cols), E5M2, h == 0, h == HALVES - 1)
            sums = sbuf([width], F32, name + "_sb", tag)
            copy(sums[:], dw[:, 0:width])
            return sums

        def scalar_scatter(window, sums, cols):
            nc.scalar.activation(listed(window[:], cols), sums, ACT.Copy)

        out_rows = out.rearrange("(p j) n -> p j n", j=PACK)
        for j in range(2):
            scalar_scatter(windows[j], output_sums(j, (3, 4)[j], parts[0], nc.scalar.copy, f"dw{j}_early")[:], parts[0])
        for q in range(2, 4):
            finish(da1[1][:, q % 2 * K_PASS : (q % 2 + 1) * K_PASS], dh1[q], slope1, q)
        for q in range(2, 4):
            quantize(columns(daq[1], block(q)), E5M2, da1[1][:, q % 2 * K_PASS : (q % 2 + 1) * K_PASS])
        quantize(columns(late_codes[1], parts[0]), E4M3, xr1[1][:])
        late0 = output_sums(0, 5, parts[1], nc.vector.tensor_copy, "dw0_late")
        late1 = output_sums(1, 6, parts[1], nc.scalar.copy, "dw1_late")
        nc.vector.tensor_copy(listed(windows[0][:], parts[1]), late0[:])
        nc.sync.dma_start(out_rows[:, 0, :], windows[0][:])
        scalar_scatter(windows[1], late1[:], parts[1])
        nc.scalar.dma_start(out_rows[:, 1, :], windows[1][:])
        sums2 = output_sums(2, 5, every, nc.vector.tensor_copy, "dw2")
        nc.vector.tensor_copy(listed(windows[2][:], every), sums2[:])
        nc.sync.dma_start(out_rows[:, 2, :], windows[2][:])
        sums3 = [
            output_sums(3, 1, parts[0], nc.scalar.copy, "dw3_first", "dw1_late_sb"),
            output_sums(3, 2, parts[1], nc.scalar.copy, "dw3_second"),
        ]
        for cols, sums in zip(parts, sums3):
            scalar_scatter(windows[3], sums[:], cols)
        nc.scalar.dma_start(out_rows[:, 3, :], windows[3][:])
